import numpy as np
import ml_dtypes


def mxq(x, axis, fmt="e4m3"):
    dtype, down = {"e4m3": (ml_dtypes.float8_e4m3fn, 7), "e5m2": (ml_dtypes.float8_e5m2, 14)}[fmt]
    v = np.moveaxis(np.asarray(x, np.float32).astype(ml_dtypes.bfloat16).astype(np.float64), axis, -1)
    blocks = v.reshape(v.shape[:-1] + (-1, 32))
    amax = np.abs(blocks).max(-1, keepdims=True)
    byte = np.maximum(np.where(amax > 0, np.frexp(amax)[1] - 1 + 127, 0) - down, 1)
    scale = np.exp2(byte - 127.0)
    codes = (blocks / scale).astype(np.float32).astype(dtype).astype(np.float64)
    return np.moveaxis((codes * scale).reshape(v.shape), -1, axis)


WIDE = False


def mx_kscale(k):
    if not WIDE:
        return np.ones(k)
    levels = np.array([10, -10, 5, -5, 0])
    if k % 512:
        return np.exp2(np.random.permutation(np.resize(levels, k // 32))).repeat(32)
    a = np.empty((k // 512, 16))
    for p in range(k // 512):
        a[p, :8] = np.random.permutation(np.resize(levels, 8))
        for g in range(8):
            far = levels[np.abs(levels - a[p, g]) >= 10]
            a[p, g + 8] = far[np.random.randint(len(far))]
    return np.exp2(a.ravel()).repeat(32)


def f64(x):
    return np.asarray(x).astype(np.float64)


def striped(idx):
    return np.tile(np.asarray(idx).reshape(-1, 16).T, (8, 1)).astype(np.uint16)


def unstriped(offs):
    return offs[:16].T.reshape(-1).astype(np.int64)


def bf(x):
    return np.asarray(x, np.float32).astype(ml_dtypes.bfloat16)


def planes(Y):
    r, m = Y.shape
    b = f64(bf(Y)).reshape(r // 32, 32, m)
    amax = np.abs(b).max(1)
    byte = np.clip(np.where(amax > 0, np.frexp(amax)[1] - 1 + 127 - 7, 1), 1, 254)
    codes = (b * np.exp2(127.0 - byte)[:, None, :]).reshape(r, m).astype(np.float32).astype(ml_dtypes.float8_e4m3fn).view(np.uint8)
    words = codes.reshape(r // 512, 128, 4, m).transpose(0, 1, 3, 2)
    return np.ascontiguousarray(words), np.ascontiguousarray(byte.astype(np.uint8).reshape(r // 512, 16, m))


E, T, J, G, F = 512, 1024, 512, 128, 512


def setup_inputs():
    n = np.random.standard_normal
    idx = np.random.permutation(T)[:J]
    idx2 = np.random.permutation(T)[:J]
    idx3 = np.random.permutation(T)[:J]
    idx4 = np.random.permutation(T)[:J]
    fe = mx_kscale(E)
    return {
        "vals": (n((E, T)) / fe[:, None]).astype(np.float32),
        "ca": (np.random.uniform(0.1, 0.4, (1, J))).astype(np.float32),
        "cb": (np.random.uniform(0.1, 0.4, (1, J))).astype(np.float32),
        "cc": (np.random.uniform(0.1, 0.4, (1, J))).astype(np.float32),
        "cd": (np.random.uniform(0.1, 0.4, (1, J))).astype(np.float32),
        "aw": (np.random.uniform(0.1, 0.9, (1, J))).astype(np.float32),
        "wo": (n((E, F)) * 2 / np.sqrt(E) * fe[:, None]).astype(np.float32),
        "offs": striped(idx),
        "offs2": striped(idx2),
        "offs3": striped(idx3),
        "offs4": striped(idx4),
    }


def reference(vals, ca, cb, cc, cd, aw, wo, offs, offs2, offs3, offs4):
    idx = unstriped(offs)
    idx2 = unstriped(offs2)
    idx3 = unstriped(offs3)
    idx4 = unstriped(offs4)
    v = f64(vals)[:, idx] * f64(ca) + f64(vals)[:, idx2] * f64(cb) + f64(vals)[:, idx3] * f64(cc) + f64(vals)[:, idx4] * f64(cd)
    b = (v * f64(aw)).reshape(E, G, J // G).sum(axis=2)
    woq = mxq(f64(wo), 0, "e4m3")
    bq = mxq(b, 0, "e4m3")
    y = woq.T @ bq
    words, scales = planes(y)
    return y, words, scales

@@ -1,0 +1,145 @@
+from contextlib import ExitStack
+
+import concourse.mybir as mybir
+from concourse.masks import make_identity
+
+E, T, J, G, F = 512, 1024, 512, 128, 512
+FLOPS = 2 * E * F * G
+
+F32 = mybir.dt.float32
+BF16 = mybir.dt.bfloat16
+I32 = mybir.dt.int32
+U32 = mybir.dt.uint32
+U16 = mybir.dt.uint16
+U8 = mybir.dt.uint8
+FP8X4 = mybir.dt.float8_e4m3fn_x4
+MULT = mybir.AluOpType.mult
+ADD = mybir.AluOpType.add
+
+P = 128
+PACK = 4
+POINTS = J // G
+CORNERS = 4
+
+
+def tile_attend_deformable_pl_kernel(tc, vals, ca, cb, cc, cd, aw, wo, offs, offs2, offs3, offs4, out_0, out_1, out_2):
+    nc = tc.nc
+    corner_rows = (ca, cb, cc, cd)
+    lists_hbm = (offs, offs2, offs3, offs4)
+
+    with ExitStack() as ctx:
+        keep = ctx.enter_context(tc.tile_pool(name="keep", bufs=1))
+        ring = ctx.enter_context(tc.tile_pool(name="ring", bufs=4))
+        psum = ctx.enter_context(tc.psum_pool(name="psum", bufs=2))
+
+        planes = [keep.tile([P, T], F32, name="plane%d" % t) for t in range(PACK)]
+        lists = [keep.tile([P, J // 16], U16, name="list%d" % c) for c in range(CORNERS)]
+        corner = [keep.tile([P, POINTS], F32, name="corner%d" % c) for c in range(CORNERS)]
+        attn = keep.tile([P, POINTS], F32)
+        wo_raw = keep.tile([P, PACK, F], F32)
+        vals_planes = vals.rearrange("(p t) c -> p t c", t=PACK)
+
+        def by_query(row):
+            return row.rearrange("o (g r) -> g (o r)", r=POINTS)
+
+        nc.scalar.dma_start(out=attn[:], in_=by_query(aw))
+        nc.scalar.dma_start(out=corner[0][:], in_=by_query(corner_rows[0]))
+        nc.sync.dma_start(out=planes[0][:], in_=vals_planes[:, 0, :])
+        nc.sync.dma_start(lists[0][:], lists_hbm[0])
+        for c in range(1, CORNERS):
+            nc.scalar.dma_start(out=corner[c][:], in_=by_query(corner_rows[c]))
+            nc.sync.dma_start(lists[c][:], lists_hbm[c])
+        nc.sync.dma_start(out=planes[1][:], in_=vals_planes[:, 1, :])
+        nc.sync.dma_start(out=wo_raw[:], in_=wo.rearrange("(p t) f -> p t f", t=PACK))
+        for t in range(2, PACK):
+            nc.sync.dma_start(out=planes[t][:], in_=vals_planes[:, t, :])
+
+        ident = keep.tile([P, P], F32)
+        make_identity(nc, ident[:])
+
+        spread = []
+        for c in range(CORNERS):
+            weight = keep.tile([P, POINTS], F32, name="weight%d" % c)
+            nc.vector.tensor_tensor(weight[:], corner[c][:], attn[:], MULT)
+            spread_bank = psum.tile([P, POINTS, G], F32, name="spread_bank")
+            for r in range(POINTS):
+                nc.tensor.transpose(spread_bank[:, r, :], weight[:, r : r + 1].to_broadcast([P, P]), ident[:])
+            row = keep.tile([P, J], F32, name="spread%d" % c)
+            nc.scalar.copy(out=row[:].rearrange("p (g r) -> p g r", r=POINTS), in_=spread_bank[:].rearrange("p r g -> p g r"))
+            spread.append(row)
+
+        wo_bf = keep.tile([P, PACK, P, PACK], BF16, align_bytes=64)
+        wo_dealt = wo_raw[:].rearrange("p k (m t) -> p t m k", t=PACK)
+        wo_codes = keep.tile([P, F], U32, align_bytes=64)
+        wo_scales = keep.tile([P, F], U8, align_bytes=64)
+
+        b_bf = keep.tile([P, G, PACK], BF16, align_bytes=64)
+        for t in range(PACK):
+            last = t == PACK - 1
+            turned = CORNERS - 1 if last else CORNERS
+            acc = psum.tile([P, P], F32, name="acc")
+            for c in range(CORNERS):
+                prod = ring.tile([P, J], F32, name="prod")
+                nc.vector.tensor_tensor(prod[:], planes[t][:].indirect(lists[c][:]), spread[c][:], MULT)
+                if c < turned:
+                    for r in range(POINTS):
+                        nc.tensor.matmul(
+                            acc[:], prod[:, r:J:POINTS], ident[:], is_transpose=True,
+                            start=(c == 0 and r == 0), stop=(c == turned - 1 and r == POINTS - 1),
+                        )
+                else:
+                    rest = keep.tile([P, G], F32, name="rest")
+                    nc.vector.tensor_reduce(
+                        rest[:], prod[:].rearrange("p (g r) -> p g r", r=POINTS), mybir.AxisListType.X, ADD
+                    )
+            acc_sb = ring.tile([P, P], F32, name="acc_sb")
+            nc.scalar.copy(out=acc_sb[:], in_=acc[:])
+            back = psum.tile([P, G], F32, name="back")
+            nc.tensor.transpose(back[:], acc_sb[:], ident[:])
+            if last:
+                nc.vector.quantize_mx(
+                    out=wo_codes[:].bitcast(FP8X4), scales=wo_scales[:], in_=wo_bf[:].rearrange("p t m k -> p (t m k)")
+                )
+                nc.vector.tensor_tensor(b_bf[:, :, t], back[:], rest[:], ADD)
+            else:
+                nc.scalar.copy(out=b_bf[:, :, t], in_=back[:])
+            if t == 0:
+                for u in range(PACK):
+                    nc.scalar.copy(out=wo_bf[:, u, :, :], in_=wo_dealt[:, u, :, :])
+
+        b_codes = keep.tile([P, G], U32, align_bytes=64)
+        b_scales = keep.tile([P, G], U8, align_bytes=64)
+        nc.vector.quantize_mx(out=b_codes[:].bitcast(FP8X4), scales=b_scales[:], in_=b_bf[:].rearrange("p g t -> p (g t)"))
+
+        y = keep.tile([P, PACK, G], F32)
+        half = PACK // 2
+        for h in range(2):
+            y_bank = psum.tile([P, half, G], F32, name="y_bank")
+            for u in range(half):
+                cols = slice((h * half + u) * P, (h * half + u + 1) * P)
+                nc.tensor.matmul_mx(
+                    out=y_bank[:, u, :],
+                    lhsT=wo_codes[:, cols].bitcast(FP8X4),
+                    lhsT_scale=wo_scales[:, cols],
+                    rhs=b_codes[:].bitcast(FP8X4),
+                    rhs_scale=b_scales[:],
+                    start=True,
+                    stop=True,
+                )
+            if h == 0:
+                nc.scalar.copy(out=y[:, 0:half, :], in_=y_bank[:])
+            else:
+                nc.vector.tensor_copy(out=y[:, half:PACK, :], in_=y_bank[:])
+        nc.scalar.dma_start(out=out_0.rearrange("(p t) g -> p t g", t=PACK), in_=y[:])
+
+        y_bf = keep.tile([P, G, PACK], BF16, align_bytes=64)
+        nc.vector.tensor_copy(out=y_bf[:], in_=y[:].rearrange("p t g -> p g t"))
+        y_codes = keep.tile([P, G], U32, align_bytes=64)
+        y_scales = keep.tile([P, G], U8, align_bytes=64)
+        nc.vector.quantize_mx(out=y_codes[:].bitcast(FP8X4), scales=y_scales[:], in_=y_bf[:].rearrange("p g t -> p (g t)"))
+        nc.sync.dma_start(out=out_1.rearrange("z p c r -> p (z c r)").bitcast(I32), in_=y_codes[:].bitcast(I32))
+        for q in range(4):
+            queue = nc.sync if q % 2 == 0 else nc.scalar
+            queue.dma_start(
+                out=out_2[0, 4 * q : 4 * q + 4, :].bitcast(I32), in_=y_scales[32 * q : 32 * q + 4, :].bitcast(I32)
+            )

@@ -15,11 +15,17 @@ U8 = mybir.dt.uint8
 FP8X4 = mybir.dt.float8_e4m3fn_x4
 MULT = mybir.AluOpType.mult
 ADD = mybir.AluOpType.add
+COPY = mybir.ActivationFunctionType.Copy
 
 P = 128
 PACK = 4
-POINTS = J // G
 CORNERS = 4
+PAIRS = J // 2
+BLOCKS = 4
+PLAIN = 2
+PICKS = 3
+WO_FIRST = 6
+WO_EVERY = 2
 
 
 def tile_attend_deformable_pl_kernel(tc, vals, ca, cb, cc, cd, aw, wo, offs, offs2, offs3, offs4, out_0, out_1, out_2):
@@ -29,94 +35,142 @@ def tile_attend_deformable_pl_kernel(tc, vals, ca, cb, cc, cd, aw, wo, offs, off
 
     with ExitStack() as ctx:
         keep = ctx.enter_context(tc.tile_pool(name="keep", bufs=1))
-        ring = ctx.enter_context(tc.tile_pool(name="ring", bufs=4))
-        psum = ctx.enter_context(tc.psum_pool(name="psum", bufs=2))
+        ring = ctx.enter_context(tc.tile_pool(name="ring", bufs=3))
+        turn = ctx.enter_context(tc.psum_pool(name="turn", bufs=5))
+        psum = ctx.enter_context(tc.psum_pool(name="psum", bufs=1))
 
         planes = [keep.tile([P, T], F32, name="plane%d" % t) for t in range(PACK)]
         lists = [keep.tile([P, J // 16], U16, name="list%d" % c) for c in range(CORNERS)]
-        corner = [keep.tile([P, POINTS], F32, name="corner%d" % c) for c in range(CORNERS)]
-        attn = keep.tile([P, POINTS], F32)
+        corner = [keep.tile([P, BLOCKS], F32, name="corner%d" % c) for c in range(CORNERS)]
+        attn = keep.tile([P, BLOCKS], F32)
         wo_raw = keep.tile([P, PACK, F], F32)
         vals_planes = vals.rearrange("(p t) c -> p t c", t=PACK)
 
-        def by_query(row):
-            return row.rearrange("o (g r) -> g (o r)", r=POINTS)
+        def load_row(dst, row):
+            nc.sync.dma_start(
+                out=dst.rearrange("p (h u) -> p h u", u=2), in_=row.rearrange("o (h p u) -> p (o h) u", h=2, u=2)
+            )
 
-        nc.scalar.dma_start(out=attn[:], in_=by_query(aw))
-        nc.scalar.dma_start(out=corner[0][:], in_=by_query(corner_rows[0]))
+        fused_first = list(range(PLAIN, CORNERS)) + list(range(PLAIN))
         nc.sync.dma_start(out=planes[0][:], in_=vals_planes[:, 0, :])
         nc.sync.dma_start(lists[0][:], lists_hbm[0])
-        for c in range(1, CORNERS):
-            nc.scalar.dma_start(out=corner[c][:], in_=by_query(corner_rows[c]))
-            nc.sync.dma_start(lists[c][:], lists_hbm[c])
+        load_row(attn[:], aw)
+        for c in fused_first:
+            load_row(corner[c][:], corner_rows[c])
+        nc.sync.dma_start(lists[1][:], lists_hbm[1])
         nc.sync.dma_start(out=planes[1][:], in_=vals_planes[:, 1, :])
-        nc.sync.dma_start(out=wo_raw[:], in_=wo.rearrange("(p t) f -> p t f", t=PACK))
+        for c in range(2, CORNERS):
+            nc.sync.dma_start(lists[c][:], lists_hbm[c])
         for t in range(2, PACK):
             nc.sync.dma_start(out=planes[t][:], in_=vals_planes[:, t, :])
+        nc.sync.dma_start(out=wo_raw[:], in_=wo.rearrange("(p t) f -> p t f", t=PACK))
 
         ident = keep.tile([P, P], F32)
         make_identity(nc, ident[:])
 
-        spread = []
-        for c in range(CORNERS):
-            weight = keep.tile([P, POINTS], F32, name="weight%d" % c)
-            nc.vector.tensor_tensor(weight[:], corner[c][:], attn[:], MULT)
-            spread_bank = psum.tile([P, POINTS, G], F32, name="spread_bank")
-            for r in range(POINTS):
-                nc.tensor.transpose(spread_bank[:, r, :], weight[:, r : r + 1].to_broadcast([P, P]), ident[:])
-            row = keep.tile([P, J], F32, name="spread%d" % c)
-            nc.scalar.copy(out=row[:].rearrange("p (g r) -> p g r", r=POINTS), in_=spread_bank[:].rearrange("p r g -> p g r"))
-            spread.append(row)
+        weight = {}
+        for c in fused_first:
+            weight[c] = keep.tile([P, BLOCKS], F32, name="weight%d" % c)
+            nc.gpsimd.tensor_tensor(weight[c][:], corner[c][:], attn[:], MULT)
+        spread = {}
+        for c in range(PLAIN, CORNERS):
+            spread_bank = turn.tile([P, BLOCKS, P], F32, name="spread_bank", tag="turn")
+            for s in range(BLOCKS):
+                nc.tensor.transpose(spread_bank[:, s, :], weight[c][:, s : s + 1].to_broadcast([P, P]), ident[:])
+            spread[c] = keep.tile([P, J], F32, name="spread%d" % c)
+            nc.scalar.copy(
+                out=spread[c][:].rearrange("p (h m u) -> p h m u", h=2, u=2),
+                in_=spread_bank[:].rearrange("p (h u) m -> p h m u", u=2),
+            )
 
         wo_bf = keep.tile([P, PACK, P, PACK], BF16, align_bytes=64)
-        wo_dealt = wo_raw[:].rearrange("p k (m t) -> p t m k", t=PACK)
-        wo_codes = keep.tile([P, F], U32, align_bytes=64)
-        wo_scales = keep.tile([P, F], U8, align_bytes=64)
+        wo_dealt = wo_raw[:].rearrange("p k (m t) -> p m t k", t=PACK)
+        wo_into = wo_bf[:].rearrange("p t m k -> p m t k")
+        piece = P // PACK
 
-        b_bf = keep.tile([P, G, PACK], BF16, align_bytes=64)
+        sums01 = psum.tile([P, 2, PAIRS], F32, name="sums01", tag="bank0")
+        sums2 = psum.tile([P, PAIRS], F32, name="sums2", tag="bank1")
+        sums3 = psum.tile([P, PAIRS], F32, name="sums3", tag="bank2")
+        sums = (sums01[:, 0, :], sums01[:, 1, :], sums2[:], sums3[:])
+
+        def block(tile, h, u):
+            return tile[:, h * PAIRS + u : (h + 1) * PAIRS : 2]
+
+        picks = [keep.tile([P, J], F32, name="pick%d" % i, tag="pick%d" % i, align_bytes=64) for i in range(PICKS)]
         for t in range(PACK):
-            last = t == PACK - 1
-            turned = CORNERS - 1 if last else CORNERS
-            acc = psum.tile([P, P], F32, name="acc")
             for c in range(CORNERS):
-                prod = ring.tile([P, J], F32, name="prod")
-                nc.vector.tensor_tensor(prod[:], planes[t][:].indirect(lists[c][:]), spread[c][:], MULT)
-                if c < turned:
-                    for r in range(POINTS):
-                        nc.tensor.matmul(
-                            acc[:], prod[:, r:J:POINTS], ident[:], is_transpose=True,
-                            start=(c == 0 and r == 0), stop=(c == turned - 1 and r == POINTS - 1),
-                        )
+                picked = picks[(t * CORNERS + c) % PICKS]
+                if c < PLAIN:
+                    nc.vector.tensor_copy(picked[:], planes[t][:].indirect(lists[c][:]))
+                    scaled = ring.tile([P, 2, 2, P], F32, name="scaled")
+                    for h in range(2):
+                        turned = turn.tile([P, 2, P], F32, name="turned", tag="turn")
+                        for u in range(2):
+                            nc.tensor.transpose(turned[:, u, :], block(picked, h, u), ident[:])
+                        for u in range(2):
+                            nc.scalar.activation(
+                                out=scaled[:, h, u, :], in_=turned[:, u, :], func=COPY, scale=weight[c][:, 2 * h + u : 2 * h + u + 1]
+                            )
+                    for h in range(2):
+                        for u in range(2):
+                            nc.tensor.matmul(
+                                sums[t][:, h * P : (h + 1) * P], scaled[:, h, u, :], ident[:], is_transpose=True,
+                                start=(c == 0 and h == 0 and u == 0), stop=False,
+                            )
                 else:
-                    rest = keep.tile([P, G], F32, name="rest")
-                    nc.vector.tensor_reduce(
-                        rest[:], prod[:].rearrange("p (g r) -> p g r", r=POINTS), mybir.AxisListType.X, ADD
-                    )
-            acc_sb = ring.tile([P, P], F32, name="acc_sb")
-            nc.scalar.copy(out=acc_sb[:], in_=acc[:])
-            back = psum.tile([P, G], F32, name="back")
-            nc.tensor.transpose(back[:], acc_sb[:], ident[:])
-            if last:
-                nc.vector.quantize_mx(
-                    out=wo_codes[:].bitcast(FP8X4), scales=wo_scales[:], in_=wo_bf[:].rearrange("p t m k -> p (t m k)")
+                    cuts = 2 if (t, c) == (PACK - 1, CORNERS - 1) else 1
+                    n = J // cuts
+                    for h in range(cuts):
+                        nc.vector.tensor_tensor(
+                            picked[:, h * n : (h + 1) * n],
+                            planes[t][:].indirect(lists[c][:, h * n // 16 : (h + 1) * n // 16]),
+                            spread[c][:, h * n : (h + 1) * n],
+                            MULT,
+                        )
+                    if c == PLAIN:
+                        added = [turn.tile([P, P], F32, name="added%d" % h, tag="turn") for h in range(2)]
+                    for h in range(2):
+                        for u in range(2):
+                            nc.tensor.matmul(
+                                added[h][:], block(picked, h, u), ident[:], is_transpose=True,
+                                start=(c == PLAIN and u == 0), stop=(c == CORNERS - 1 and u == 1),
+                            )
+                step = t * CORNERS + c - WO_FIRST
+                if step >= 0 and step % WO_EVERY == 0 and step // WO_EVERY < PACK:
+                    m = slice(step // WO_EVERY * piece, (step // WO_EVERY + 1) * piece)
+                    nc.scalar.copy(out=wo_into[:, m, :, :], in_=wo_dealt[:, m, :, :])
+            added_sb = ring.tile([P, 2, P], F32, name="added_sb")
+            for h in range(2):
+                nc.scalar.copy(out=added_sb[:, h, :], in_=added[h][:])
+                nc.tensor.matmul(
+                    sums[t][:, h * P : (h + 1) * P], added_sb[:, h, :], ident[:], is_transpose=True, start=False, stop=(h == 1)
                 )
-                nc.vector.tensor_tensor(b_bf[:, :, t], back[:], rest[:], ADD)
-            else:
-                nc.scalar.copy(out=b_bf[:, :, t], in_=back[:])
-            if t == 0:
-                for u in range(PACK):
-                    nc.scalar.copy(out=wo_bf[:, u, :, :], in_=wo_dealt[:, u, :, :])
+
+        b_bf = keep.tile([P, G, PACK], BF16, tag="pick1", align_bytes=64)
+        wo_codes = keep.tile([P, F], U32, tag="pick2", align_bytes=64)
+        wo_scales = keep.tile([P, F], U8, align_bytes=64)
+        with nc.allow_low_precision(reason="float32 sums, rounded once on the way to the quantiser"):
+            nc.vector.tensor_reduce(
+                b_bf[:, :, 0:2], sums01[:].rearrange("p t (g v) -> p g t v", v=2), mybir.AxisListType.X, ADD
+            )
+            nc.vector.tensor_reduce(b_bf[:, :, 2], sums2[:].rearrange("p (g v) -> p g v", v=2), mybir.AxisListType.X, ADD)
+            nc.vector.quantize_mx(
+                out=wo_codes[:].bitcast(FP8X4), scales=wo_scales[:], in_=wo_bf[:].rearrange("p t m k -> p (t m k)")
+            )
+            nc.vector.tensor_reduce(b_bf[:, :, 3], sums3[:].rearrange("p (g v) -> p g v", v=2), mybir.AxisListType.X, ADD)
 
         b_codes = keep.tile([P, G], U32, align_bytes=64)
         b_scales = keep.tile([P, G], U8, align_bytes=64)
         nc.vector.quantize_mx(out=b_codes[:].bitcast(FP8X4), scales=b_scales[:], in_=b_bf[:].rearrange("p g t -> p (g t)"))
 
         y = keep.tile([P, PACK, G], F32)
-        half = PACK // 2
+        y_bf = keep.tile([P, G, PACK], BF16, align_bytes=64)
+        out_planes = out_0.rearrange("(p t) g -> p t g", t=PACK)
         for h in range(2):
-            y_bank = psum.tile([P, half, G], F32, name="y_bank")
-            for u in range(half):
-                cols = slice((h * half + u) * P, (h * half + u + 1) * P)
+            two = slice(2 * h, 2 * h + 2)
+            y_bank = psum.tile([P, 2, G], F32, name="y_bank", tag="bank%d" % h)
+            for u in range(2):
+                cols = slice((2 * h + u) * P, (2 * h + u + 1) * P)
                 nc.tensor.matmul_mx(
                     out=y_bank[:, u, :],
                     lhsT=wo_codes[:, cols].bitcast(FP8X4),
@@ -126,14 +180,11 @@ def tile_attend_deformable_pl_kernel(tc, vals, ca, cb, cc, cd, aw, wo, offs, off
                     start=True,
                     stop=True,
                 )
-            if h == 0:
-                nc.scalar.copy(out=y[:, 0:half, :], in_=y_bank[:])
-            else:
-                nc.vector.tensor_copy(out=y[:, half:PACK, :], in_=y_bank[:])
-        nc.scalar.dma_start(out=out_0.rearrange("(p t) g -> p t g", t=PACK), in_=y[:])
+            nc.vector.tensor_copy(out=y_bf[:, :, two], in_=y_bank[:].rearrange("p t g -> p g t"))
+            nc.scalar.copy(out=y[:, two, :], in_=y_bank[:])
+            queue = nc.sync if h == 0 else nc.scalar
+            queue.dma_start(out=out_planes[:, two, :], in_=y[:, two, :])
 
-        y_bf = keep.tile([P, G, PACK], BF16, align_bytes=64)
-        nc.vector.tensor_copy(out=y_bf[:], in_=y[:].rearrange("p t g -> p g t"))
         y_codes = keep.tile([P, G], U32, align_bytes=64)
         y_scales = keep.tile([P, G], U8, align_bytes=64)
         nc.vector.quantize_mx(out=y_codes[:].bitcast(FP8X4), scales=y_scales[:], in_=y_bf[:].rearrange("p g t -> p (g t)"))

@@ -22,7 +22,7 @@ PACK = 4
 CORNERS = 4
 PAIRS = J // 2
 BLOCKS = 4
-PLAIN = 2
+PLAIN = 1
 PICKS = 3
 WO_FIRST = 6
 WO_EVERY = 2
@@ -51,17 +51,15 @@ def tile_attend_deformable_pl_kernel(tc, vals, ca, cb, cc, cd, aw, wo, offs, off
                 out=dst.rearrange("p (h u) -> p h u", u=2), in_=row.rearrange("o (h p u) -> p (o h) u", h=2, u=2)
             )
 
-        fused_first = list(range(PLAIN, CORNERS)) + list(range(PLAIN))
-        nc.sync.dma_start(out=planes[0][:], in_=vals_planes[:, 0, :])
         nc.sync.dma_start(lists[0][:], lists_hbm[0])
+        nc.sync.dma_start(out=planes[0][:], in_=vals_planes[:, 0, :])
         load_row(attn[:], aw)
-        for c in fused_first:
+        for c in (1, 0, 2, 3):
             load_row(corner[c][:], corner_rows[c])
         nc.sync.dma_start(lists[1][:], lists_hbm[1])
-        nc.sync.dma_start(out=planes[1][:], in_=vals_planes[:, 1, :])
         for c in range(2, CORNERS):
             nc.sync.dma_start(lists[c][:], lists_hbm[c])
-        for t in range(2, PACK):
+        for t in range(1, PACK):
             nc.sync.dma_start(out=planes[t][:], in_=vals_planes[:, t, :])
         nc.sync.dma_start(out=wo_raw[:], in_=wo.rearrange("(p t) f -> p t f", t=PACK))
 
@@ -69,11 +67,11 @@ def tile_attend_deformable_pl_kernel(tc, vals, ca, cb, cc, cd, aw, wo, offs, off
         make_identity(nc, ident[:])
 
         weight = {}
-        for c in fused_first:
+        for c in (1, 0, 2, 3):
             weight[c] = keep.tile([P, BLOCKS], F32, name="weight%d" % c)
             nc.gpsimd.tensor_tensor(weight[c][:], corner[c][:], attn[:], MULT)
         spread = {}
-        for c in range(PLAIN, CORNERS):
+        for c in (1, 2, 3, 0):
             spread_bank = turn.tile([P, BLOCKS, P], F32, name="spread_bank", tag="turn")
             for s in range(BLOCKS):
                 nc.tensor.transpose(spread_bank[:, s, :], weight[c][:, s : s + 1].to_broadcast([P, P]), ident[:])
@@ -100,7 +98,7 @@ def tile_attend_deformable_pl_kernel(tc, vals, ca, cb, cc, cd, aw, wo, offs, off
         for t in range(PACK):
             for c in range(CORNERS):
                 picked = picks[(t * CORNERS + c) % PICKS]
-                if c < PLAIN:
+                if t * CORNERS + c < PLAIN:
                     nc.vector.tensor_copy(picked[:], planes[t][:].indirect(lists[c][:]))
                     scaled = ring.tile([P, 2, 2, P], F32, name="scaled")
                     for h in range(2):
@@ -127,13 +125,14 @@ def tile_attend_deformable_pl_kernel(tc, vals, ca, cb, cc, cd, aw, wo, offs, off
                             spread[c][:, h * n : (h + 1) * n],
                             MULT,
                         )
-                    if c == PLAIN:
+                    first = PLAIN if t == 0 else 0
+                    if c == first:
                         added = [turn.tile([P, P], F32, name="added%d" % h, tag="turn") for h in range(2)]
                     for h in range(2):
                         for u in range(2):
                             nc.tensor.matmul(
                                 added[h][:], block(picked, h, u), ident[:], is_transpose=True,
-                                start=(c == PLAIN and u == 0), stop=(c == CORNERS - 1 and u == 1),
+                                start=(c == first and u == 0), stop=(c == CORNERS - 1 and u == 1),
                             )
                 step = t * CORNERS + c - WO_FIRST
                 if step >= 0 and step % WO_EVERY == 0 and step // WO_EVERY < PACK:
@@ -143,7 +142,7 @@ def tile_attend_deformable_pl_kernel(tc, vals, ca, cb, cc, cd, aw, wo, offs, off
             for h in range(2):
                 nc.scalar.copy(out=added_sb[:, h, :], in_=added[h][:])
                 nc.tensor.matmul(
-                    sums[t][:, h * P : (h + 1) * P], added_sb[:, h, :], ident[:], is_transpose=True, start=False, stop=(h == 1)
+                    sums[t][:, h * P : (h + 1) * P], added_sb[:, h, :], ident[:], is_transpose=True, start=(t > 0 and h == 0), stop=(h == 1)
                 )
 
         b_bf = keep.tile([P, G, PACK], BF16, tag="pick1", align_bytes=64)

@@ -22,41 +22,35 @@ PACK = 4
 CORNERS = 4
 PAIRS = J // 2
 BLOCKS = 4
-PLAIN = 1
-PICKS = 3
+ROW0 = P - 2 * (CORNERS + 1)
+PICKS = 5
+PLAIN = (2, 2, 2, 0)
 WO_FIRST = 6
-WO_EVERY = 2
+WO_PIECES = 8
 
 
 def tile_attend_deformable_pl_kernel(tc, vals, ca, cb, cc, cd, aw, wo, offs, offs2, offs3, offs4, out_0, out_1, out_2):
     nc = tc.nc
-    corner_rows = (ca, cb, cc, cd)
     lists_hbm = (offs, offs2, offs3, offs4)
 
     with ExitStack() as ctx:
         keep = ctx.enter_context(tc.tile_pool(name="keep", bufs=1))
-        ring = ctx.enter_context(tc.tile_pool(name="ring", bufs=3))
-        turn = ctx.enter_context(tc.psum_pool(name="turn", bufs=5))
         psum = ctx.enter_context(tc.psum_pool(name="psum", bufs=1))
 
         planes = [keep.tile([P, T], F32, name="plane%d" % t) for t in range(PACK)]
         lists = [keep.tile([P, J // 16], U16, name="list%d" % c) for c in range(CORNERS)]
-        corner = [keep.tile([P, BLOCKS], F32, name="corner%d" % c) for c in range(CORNERS)]
-        attn = keep.tile([P, BLOCKS], F32)
+        rows = keep.tile([P, PAIRS], F32)
         wo_raw = keep.tile([P, PACK, F], F32)
         vals_planes = vals.rearrange("(p t) c -> p t c", t=PACK)
 
-        def load_row(dst, row):
-            nc.sync.dma_start(
-                out=dst.rearrange("p (h u) -> p h u", u=2), in_=row.rearrange("o (h p u) -> p (o h) u", h=2, u=2)
-            )
+        def bank(i, shape, name):
+            return psum.tile(shape, F32, name=name, tag="bank%d" % i)
 
-        nc.sync.dma_start(lists[0][:], lists_hbm[0])
         nc.sync.dma_start(out=planes[0][:], in_=vals_planes[:, 0, :])
-        load_row(attn[:], aw)
-        for c in (1, 0, 2, 3):
-            load_row(corner[c][:], corner_rows[c])
-        nc.sync.dma_start(lists[1][:], lists_hbm[1])
+        for r, row in enumerate((ca, cb, cc, cd, aw)):
+            nc.scalar.dma_start(out=rows[ROW0 + 2 * r : ROW0 + 2 * r + 2, :], in_=row.rearrange("o (h m) -> (o h) m", h=2))
+        for c in range(2):
+            nc.sync.dma_start(lists[c][:], lists_hbm[c])
         for c in range(2, CORNERS):
             nc.sync.dma_start(lists[c][:], lists_hbm[c])
         for t in range(1, PACK):
@@ -66,97 +60,110 @@ def tile_attend_deformable_pl_kernel(tc, vals, ca, cb, cc, cd, aw, wo, offs, off
         ident = keep.tile([P, P], F32)
         make_identity(nc, ident[:])
 
-        weight = {}
-        for c in (1, 0, 2, 3):
-            weight[c] = keep.tile([P, BLOCKS], F32, name="weight%d" % c)
-            nc.gpsimd.tensor_tensor(weight[c][:], corner[c][:], attn[:], MULT)
+        nc.vector.memset(rows[0:ROW0, :], 0.0)
+        columns = bank(7, [P, 2, P], "columns")
+        for u in range(2):
+            nc.tensor.transpose(columns[:, u, :], rows[:, u:PAIRS:2], ident[:])
+        attn = keep.tile([P, 2, 2], F32)
+        nc.scalar.copy(out=attn[:], in_=columns[:, :, P - 2 : P].rearrange("p u h -> p h u"))
+        weight = keep.tile([P, BLOCKS, CORNERS], F32)
+        for s in range(BLOCKS):
+            h, u = divmod(s, 2)
+            nc.scalar.activation(
+                out=weight[:, s, :], in_=columns[:, u, ROW0 + h : P - 2 : 2], func=COPY, scale=attn[:, h, u : u + 1]
+            )
         spread = {}
-        for c in (1, 2, 3, 0):
-            spread_bank = turn.tile([P, BLOCKS, P], F32, name="spread_bank", tag="turn")
+        for c in (2, 3, 0, 1):
+            spread_bank = bank({2: 5, 3: 6, 0: 1, 1: 2}[c], [P, BLOCKS, P], "spread_bank")
             for s in range(BLOCKS):
-                nc.tensor.transpose(spread_bank[:, s, :], weight[c][:, s : s + 1].to_broadcast([P, P]), ident[:])
+                nc.tensor.transpose(spread_bank[:, s, :], weight[:, s, c : c + 1].to_broadcast([P, P]), ident[:])
             spread[c] = keep.tile([P, J], F32, name="spread%d" % c)
             nc.scalar.copy(
                 out=spread[c][:].rearrange("p (h m u) -> p h m u", h=2, u=2),
                 in_=spread_bank[:].rearrange("p (h u) m -> p h m u", u=2),
             )
 
-        wo_bf = keep.tile([P, PACK, P, PACK], BF16, align_bytes=64)
         wo_dealt = wo_raw[:].rearrange("p k (m t) -> p m t k", t=PACK)
-        wo_into = wo_bf[:].rearrange("p t m k -> p m t k")
-        piece = P // PACK
+        piece = P // WO_PIECES
 
-        sums01 = psum.tile([P, 2, PAIRS], F32, name="sums01", tag="bank0")
-        sums2 = psum.tile([P, PAIRS], F32, name="sums2", tag="bank1")
-        sums3 = psum.tile([P, PAIRS], F32, name="sums3", tag="bank2")
-        sums = (sums01[:, 0, :], sums01[:, 1, :], sums2[:], sums3[:])
+        sums01 = bank(0, [P, 2, PAIRS], "sums01")
+        sums23 = [bank(1 + h, [P, 2, P], "sums23") for h in range(2)]
+
+        def sums(t, h):
+            return sums01[:, t, h * P : (h + 1) * P] if t < 2 else sums23[h][:, t - 2, :]
 
         def block(tile, h, u):
             return tile[:, h * PAIRS + u : (h + 1) * PAIRS : 2]
 
         picks = [keep.tile([P, J], F32, name="pick%d" % i, tag="pick%d" % i, align_bytes=64) for i in range(PICKS)]
+        plain_steps = 0
         for t in range(PACK):
-            for c in range(CORNERS):
-                picked = picks[(t * CORNERS + c) % PICKS]
-                if t * CORNERS + c < PLAIN:
-                    nc.vector.tensor_copy(picked[:], planes[t][:].indirect(lists[c][:]))
-                    scaled = ring.tile([P, 2, 2, P], F32, name="scaled")
-                    for h in range(2):
-                        turned = turn.tile([P, 2, P], F32, name="turned", tag="turn")
-                        for u in range(2):
-                            nc.tensor.transpose(turned[:, u, :], block(picked, h, u), ident[:])
-                        for u in range(2):
-                            nc.scalar.activation(
-                                out=scaled[:, h, u, :], in_=turned[:, u, :], func=COPY, scale=weight[c][:, 2 * h + u : 2 * h + u + 1]
-                            )
-                    for h in range(2):
-                        for u in range(2):
-                            nc.tensor.matmul(
-                                sums[t][:, h * P : (h + 1) * P], scaled[:, h, u, :], ident[:], is_transpose=True,
-                                start=(c == 0 and h == 0 and u == 0), stop=False,
-                            )
-                else:
-                    cuts = 2 if (t, c) == (PACK - 1, CORNERS - 1) else 1
-                    n = J // cuts
-                    for h in range(cuts):
-                        nc.vector.tensor_tensor(
-                            picked[:, h * n : (h + 1) * n],
-                            planes[t][:].indirect(lists[c][:, h * n // 16 : (h + 1) * n // 16]),
-                            spread[c][:, h * n : (h + 1) * n],
-                            MULT,
-                        )
-                    first = PLAIN if t == 0 else 0
-                    if c == first:
-                        added = [turn.tile([P, P], F32, name="added%d" % h, tag="turn") for h in range(2)]
-                    for h in range(2):
-                        for u in range(2):
-                            nc.tensor.matmul(
-                                added[h][:], block(picked, h, u), ident[:], is_transpose=True,
-                                start=(c == first and u == 0), stop=(c == CORNERS - 1 and u == 1),
-                            )
-                step = t * CORNERS + c - WO_FIRST
-                if step >= 0 and step % WO_EVERY == 0 and step // WO_EVERY < PACK:
-                    m = slice(step // WO_EVERY * piece, (step // WO_EVERY + 1) * piece)
+            if t < PACK - 1:
+                both = bank(3 + t % 2, [P, 2, P], "added")
+                added = [both[:, h, :] for h in range(2)]
+            else:
+                added = [bank(4 + h, [P, P], "added")[:] for h in range(2)]
+            order = (0, 2, 1, 3) if t in (1, 2) else (0, 1, 2, 3)
+            fused = [c for c in order if c >= PLAIN[t]]
+            for i, c in enumerate(order):
+                step = t * CORNERS + i
+                picked = picks[step % PICKS]
+                if step == WO_FIRST:
+                    wo_bf = keep.tile([P, PACK, P, PACK], BF16, tag="added_sb0", align_bytes=64)
+                    wo_into = wo_bf[:].rearrange("p t m k -> p m t k")
+                if 0 <= step - WO_FIRST < WO_PIECES:
+                    m = slice((step - WO_FIRST) * piece, (step - WO_FIRST + 1) * piece)
                     nc.scalar.copy(out=wo_into[:, m, :, :], in_=wo_dealt[:, m, :, :])
-            added_sb = ring.tile([P, 2, P], F32, name="added_sb")
+                if c not in fused:
+                    nc.vector.tensor_copy(picked[:], planes[t][:].indirect(lists[c][:]))
+                    scaled = keep.tile([P, BLOCKS, P], F32, name="scaled%d" % plain_steps)
+                    turned = bank(5 + plain_steps % 3, [P, BLOCKS, P], "turned")
+                    plain_steps += 1
+                    for s in range(BLOCKS):
+                        nc.tensor.transpose(turned[:, s, :], block(picked, s // 2, s % 2), ident[:])
+                    for s in range(BLOCKS):
+                        nc.scalar.activation(out=scaled[:, s, :], in_=turned[:, s, :], func=COPY, scale=weight[:, s, c : c + 1])
+                    for s in range(BLOCKS):
+                        opens = c == 0 and ((t == 0 and s == 0) or (t == 2 and s % 2 == 0))
+                        nc.tensor.matmul(sums(t, s // 2), scaled[:, s, :], ident[:], is_transpose=True, start=opens, stop=False)
+                    continue
+                cuts = 2 if step == PACK * CORNERS - 1 else 1
+                n = J // cuts
+                for h in range(cuts):
+                    nc.vector.tensor_tensor(
+                        picked[:, h * n : (h + 1) * n],
+                        planes[t][:].indirect(lists[c][:, h * n // 16 : (h + 1) * n // 16]),
+                        spread[c][:, h * n : (h + 1) * n],
+                        MULT,
+                    )
+                for h in range(2):
+                    for u in range(2):
+                        opens = c == fused[0] and u == 0 and (h == 0 or t == PACK - 1)
+                        closes = c == fused[-1] and u == 1 and (h == 1 or t == PACK - 1)
+                        nc.tensor.matmul(added[h], block(picked, h, u), ident[:], is_transpose=True, start=opens, stop=closes)
+            added_sb = keep.tile([P, 2, P], F32, name="added_sb", tag="added_sb%d" % t, align_bytes=64)
             for h in range(2):
-                nc.scalar.copy(out=added_sb[:, h, :], in_=added[h][:])
+                nc.scalar.copy(out=added_sb[:, h, :], in_=added[h])
                 nc.tensor.matmul(
-                    sums[t][:, h * P : (h + 1) * P], added_sb[:, h, :], ident[:], is_transpose=True, start=(t > 0 and h == 0), stop=(h == 1)
+                    sums(t, h), added_sb[:, h, :], ident[:], is_transpose=True,
+                    start=False, stop=(t == PACK - 1 or (t, h) == (1, 1)),
                 )
 
-        b_bf = keep.tile([P, G, PACK], BF16, tag="pick1", align_bytes=64)
-        wo_codes = keep.tile([P, F], U32, tag="pick2", align_bytes=64)
+        b_bf = keep.tile([P, G, PACK], BF16, tag="pick%d" % ((PACK * CORNERS - 2) % PICKS), align_bytes=64)
+        wo_codes = keep.tile([P, F], U32, tag="pick%d" % ((PACK * CORNERS - 3) % PICKS), align_bytes=64)
         wo_scales = keep.tile([P, F], U8, align_bytes=64)
+        nc.vector.quantize_mx(
+            out=wo_codes[:].bitcast(FP8X4), scales=wo_scales[:], in_=wo_bf[:].rearrange("p t m k -> p (t m k)")
+        )
         with nc.allow_low_precision(reason="float32 sums, rounded once on the way to the quantiser"):
             nc.vector.tensor_reduce(
                 b_bf[:, :, 0:2], sums01[:].rearrange("p t (g v) -> p g t v", v=2), mybir.AxisListType.X, ADD
             )
-            nc.vector.tensor_reduce(b_bf[:, :, 2], sums2[:].rearrange("p (g v) -> p g v", v=2), mybir.AxisListType.X, ADD)
-            nc.vector.quantize_mx(
-                out=wo_codes[:].bitcast(FP8X4), scales=wo_scales[:], in_=wo_bf[:].rearrange("p t m k -> p (t m k)")
-            )
-            nc.vector.tensor_reduce(b_bf[:, :, 3], sums3[:].rearrange("p (g v) -> p g v", v=2), mybir.AxisListType.X, ADD)
+            for h in range(2):
+                nc.vector.tensor_reduce(
+                    b_bf[:, h * G // 2 : (h + 1) * G // 2, 2:4],
+                    sums23[h][:].rearrange("p t (g v) -> p g t v", v=2), mybir.AxisListType.X, ADD,
+                )
 
         b_codes = keep.tile([P, G], U32, align_bytes=64)
         b_scales = keep.tile([P, G], U8, align_bytes=64)
@@ -167,7 +174,7 @@ def tile_attend_deformable_pl_kernel(tc, vals, ca, cb, cc, cd, aw, wo, offs, off
         out_planes = out_0.rearrange("(p t) g -> p t g", t=PACK)
         for h in range(2):
             two = slice(2 * h, 2 * h + 2)
-            y_bank = psum.tile([P, 2, G], F32, name="y_bank", tag="bank%d" % h)
+            y_bank = bank(6 + h, [P, 2, G], "y_bank")
             for u in range(2):
                 cols = slice((2 * h + u) * P, (2 * h + u + 1) * P)
                 nc.tensor.matmul_mx(

@@ -24,7 +24,7 @@ PAIRS = J // 2
 BLOCKS = 4
 ROW0 = P - 2 * (CORNERS + 1)
 PICKS = 5
-PLAIN = (2, 2, 2, 0)
+PLAIN = (2, 2, 1, 1)
 WO_FIRST = 6
 WO_PIECES = 8
 
@@ -46,12 +46,11 @@ def tile_attend_deformable_pl_kernel(tc, vals, ca, cb, cc, cd, aw, wo, offs, off
         def bank(i, shape, name):
             return psum.tile(shape, F32, name=name, tag="bank%d" % i)
 
+        nc.sync.dma_start(lists[0][:], lists_hbm[0])
         nc.sync.dma_start(out=planes[0][:], in_=vals_planes[:, 0, :])
         for r, row in enumerate((ca, cb, cc, cd, aw)):
             nc.scalar.dma_start(out=rows[ROW0 + 2 * r : ROW0 + 2 * r + 2, :], in_=row.rearrange("o (h m) -> (o h) m", h=2))
-        for c in range(2):
-            nc.sync.dma_start(lists[c][:], lists_hbm[c])
-        for c in range(2, CORNERS):
+        for c in range(1, CORNERS):
             nc.sync.dma_start(lists[c][:], lists_hbm[c])
         for t in range(1, PACK):
             nc.sync.dma_start(out=planes[t][:], in_=vals_planes[:, t, :])
@@ -72,9 +71,11 @@ def tile_attend_deformable_pl_kernel(tc, vals, ca, cb, cc, cd, aw, wo, offs, off
             nc.scalar.activation(
                 out=weight[:, s, :], in_=columns[:, u, ROW0 + h : P - 2 : 2], func=COPY, scale=attn[:, h, u : u + 1]
             )
+
         spread = {}
-        for c in (2, 3, 0, 1):
-            spread_bank = bank({2: 5, 3: 6, 0: 1, 1: 2}[c], [P, BLOCKS, P], "spread_bank")
+
+        def spread_row(c, i):
+            spread_bank = bank(i, [P, BLOCKS, P], "spread_bank")
             for s in range(BLOCKS):
                 nc.tensor.transpose(spread_bank[:, s, :], weight[:, s, c : c + 1].to_broadcast([P, P]), ident[:])
             spread[c] = keep.tile([P, J], F32, name="spread%d" % c)
@@ -82,6 +83,9 @@ def tile_attend_deformable_pl_kernel(tc, vals, ca, cb, cc, cd, aw, wo, offs, off
                 out=spread[c][:].rearrange("p (h m u) -> p h m u", h=2, u=2),
                 in_=spread_bank[:].rearrange("p (h u) m -> p h m u", u=2),
             )
+
+        spread_row(2, 5)
+        spread_row(3, 6)
 
         wo_dealt = wo_raw[:].rearrange("p k (m t) -> p m t k", t=PACK)
         piece = P // WO_PIECES
@@ -98,12 +102,10 @@ def tile_attend_deformable_pl_kernel(tc, vals, ca, cb, cc, cd, aw, wo, offs, off
         picks = [keep.tile([P, J], F32, name="pick%d" % i, tag="pick%d" % i, align_bytes=64) for i in range(PICKS)]
         plain_steps = 0
         for t in range(PACK):
-            if t < PACK - 1:
-                both = bank(3 + t % 2, [P, 2, P], "added")
-                added = [both[:, h, :] for h in range(2)]
-            else:
-                added = [bank(4 + h, [P, P], "added")[:] for h in range(2)]
-            order = (0, 2, 1, 3) if t in (1, 2) else (0, 1, 2, 3)
+            last = t == PACK - 1
+            if t == 1:
+                spread_row(1, 3)
+            order = (0, 2, 1, 3) if t == 1 else (0, 1, 2, 3) if t else (0, 1, 2, 3)
             fused = [c for c in order if c >= PLAIN[t]]
             for i, c in enumerate(order):
                 step = t * CORNERS + i
@@ -117,16 +119,28 @@ def tile_attend_deformable_pl_kernel(tc, vals, ca, cb, cc, cd, aw, wo, offs, off
                 if c not in fused:
                     nc.vector.tensor_copy(picked[:], planes[t][:].indirect(lists[c][:]))
                     scaled = keep.tile([P, BLOCKS, P], F32, name="scaled%d" % plain_steps)
-                    turned = bank(5 + plain_steps % 3, [P, BLOCKS, P], "turned")
+                    if last:
+                        turned = [bank(i, [P, 2, P], "turned") for i in (7, 4)]
+                    else:
+                        whole = bank(5 + plain_steps % 3, [P, 2, 2, P], "turned")
+                        turned = [whole[:, h] for h in range(2)]
                     plain_steps += 1
                     for s in range(BLOCKS):
-                        nc.tensor.transpose(turned[:, s, :], block(picked, s // 2, s % 2), ident[:])
+                        nc.tensor.transpose(turned[s // 2][:, s % 2, :], block(picked, s // 2, s % 2), ident[:])
                     for s in range(BLOCKS):
-                        nc.scalar.activation(out=scaled[:, s, :], in_=turned[:, s, :], func=COPY, scale=weight[:, s, c : c + 1])
-                    for s in range(BLOCKS):
-                        opens = c == 0 and ((t == 0 and s == 0) or (t == 2 and s % 2 == 0))
+                        nc.scalar.activation(
+                            out=scaled[:, s, :], in_=turned[s // 2][:, s % 2, :], func=COPY, scale=weight[:, s, c : c + 1]
+                        )
+                    for s in reversed(range(BLOCKS)):
+                        opens = c == 0 and ((t == 0 and s == 3) or (t == 2 and s % 2 == 1))
                         nc.tensor.matmul(sums(t, s // 2), scaled[:, s, :], ident[:], is_transpose=True, start=opens, stop=False)
                     continue
+                if c == fused[0]:
+                    if last:
+                        added = [bank(i, [P, P], "added")[:] for i in (7, 4)]
+                    else:
+                        both = bank(3 + t % 2, [P, 2, P], "added")
+                        added = [both[:, h, :] for h in range(2)]
                 cuts = 2 if step == PACK * CORNERS - 1 else 1
                 n = J // cuts
                 for h in range(cuts):
@@ -138,15 +152,18 @@ def tile_attend_deformable_pl_kernel(tc, vals, ca, cb, cc, cd, aw, wo, offs, off
                     )
                 for h in range(2):
                     for u in range(2):
-                        opens = c == fused[0] and u == 0 and (h == 0 or t == PACK - 1)
-                        closes = c == fused[-1] and u == 1 and (h == 1 or t == PACK - 1)
+                        opens = c == fused[0] and u == 0 and (h == 0 or last)
+                        closes = c == fused[-1] and u == 1 and (h == 1 or last)
                         nc.tensor.matmul(added[h], block(picked, h, u), ident[:], is_transpose=True, start=opens, stop=closes)
             added_sb = keep.tile([P, 2, P], F32, name="added_sb", tag="added_sb%d" % t, align_bytes=64)
+            if last:
+                for h in range(2):
+                    nc.scalar.copy(out=added_sb[:, h, :], in_=added[h])
+            else:
+                nc.scalar.copy(out=added_sb[:], in_=both[:])
             for h in range(2):
-                nc.scalar.copy(out=added_sb[:, h, :], in_=added[h])
                 nc.tensor.matmul(
-                    sums(t, h), added_sb[:, h, :], ident[:], is_transpose=True,
-                    start=False, stop=(t == PACK - 1 or (t, h) == (1, 1)),
+                    sums(t, h), added_sb[:, h, :], ident[:], is_transpose=True, start=False, stop=(last or (t, h) == (1, 1))
                 )
 
         b_bf = keep.tile([P, G, PACK], BF16, tag="pick%d" % ((PACK * CORNERS - 2) % PICKS), align_bytes=64)
@@ -174,7 +191,7 @@ def tile_attend_deformable_pl_kernel(tc, vals, ca, cb, cc, cd, aw, wo, offs, off
         out_planes = out_0.rearrange("(p t) g -> p t g", t=PACK)
         for h in range(2):
             two = slice(2 * h, 2 * h + 2)
-            y_bank = bank(6 + h, [P, 2, G], "y_bank")
+            y_bank = bank(5 + h, [P, 2, G], "y_bank")
             for u in range(2):
                 cols = slice((2 * h + u) * P, (2 * h + u + 1) * P)
                 nc.tensor.matmul_mx(
@@ -186,8 +203,9 @@ def tile_attend_deformable_pl_kernel(tc, vals, ca, cb, cc, cd, aw, wo, offs, off
                     start=True,
                     stop=True,
                 )
-            nc.vector.tensor_copy(out=y_bf[:, :, two], in_=y_bank[:].rearrange("p t g -> p g t"))
-            nc.scalar.copy(out=y[:, two, :], in_=y_bank[:])
+            copy = nc.vector.tensor_copy if h == 0 else nc.scalar.copy
+            copy(out=y_bf[:, :, two], in_=y_bank[:].rearrange("p t g -> p g t"))
+            copy(out=y[:, two, :], in_=y_bank[:])
             queue = nc.sync if h == 0 else nc.scalar
             queue.dma_start(out=out_planes[:, two, :], in_=y[:, two, :])
 

@@ -24,7 +24,7 @@ PAIRS = J // 2
 BLOCKS = 4
 ROW0 = P - 2 * (CORNERS + 1)
 PICKS = 5
-PLAIN = (2, 2, 1, 1)
+PLAIN = (2, 2, 1, 0)
 WO_FIRST = 6
 WO_PIECES = 8
 
@@ -46,15 +46,19 @@ def tile_attend_deformable_pl_kernel(tc, vals, ca, cb, cc, cd, aw, wo, offs, off
         def bank(i, shape, name):
             return psum.tile(shape, F32, name=name, tag="bank%d" % i)
 
-        nc.sync.dma_start(lists[0][:], lists_hbm[0])
+        def load_row(queue, r, row):
+            queue.dma_start(out=rows[ROW0 + 2 * r : ROW0 + 2 * r + 2, :], in_=row.rearrange("o (h m) -> (o h) m", h=2))
+
+        load_row(nc.sync, CORNERS, aw)
         nc.sync.dma_start(out=planes[0][:], in_=vals_planes[:, 0, :])
-        for r, row in enumerate((ca, cb, cc, cd, aw)):
-            nc.scalar.dma_start(out=rows[ROW0 + 2 * r : ROW0 + 2 * r + 2, :], in_=row.rearrange("o (h m) -> (o h) m", h=2))
-        for c in range(1, CORNERS):
+        for r, row in enumerate((ca, cb, cc, cd)):
+            load_row(nc.scalar, r, row)
+        for c in range(CORNERS):
             nc.sync.dma_start(lists[c][:], lists_hbm[c])
-        for t in range(1, PACK):
-            nc.sync.dma_start(out=planes[t][:], in_=vals_planes[:, t, :])
+        nc.sync.dma_start(out=planes[1][:], in_=vals_planes[:, 1, :])
         nc.sync.dma_start(out=wo_raw[:], in_=wo.rearrange("(p t) f -> p t f", t=PACK))
+        for t in range(2, PACK):
+            nc.sync.dma_start(out=planes[t][:], in_=vals_planes[:, t, :])
 
         ident = keep.tile([P, P], F32)
         make_identity(nc, ident[:])
@@ -84,8 +88,8 @@ def tile_attend_deformable_pl_kernel(tc, vals, ca, cb, cc, cd, aw, wo, offs, off
                 in_=spread_bank[:].rearrange("p (h u) m -> p h m u", u=2),
             )
 
-        spread_row(2, 5)
-        spread_row(3, 6)
+        for c, i in ((2, 3), (3, 4), (1, 1), (0, 2)):
+            spread_row(c, i)
 
         wo_dealt = wo_raw[:].rearrange("p k (m t) -> p m t k", t=PACK)
         piece = P // WO_PIECES
@@ -100,15 +104,12 @@ def tile_attend_deformable_pl_kernel(tc, vals, ca, cb, cc, cd, aw, wo, offs, off
             return tile[:, h * PAIRS + u : (h + 1) * PAIRS : 2]
 
         picks = [keep.tile([P, J], F32, name="pick%d" % i, tag="pick%d" % i, align_bytes=64) for i in range(PICKS)]
-        plain_steps = 0
+        first_bank = 3
         for t in range(PACK):
             last = t == PACK - 1
-            if t == 1:
-                spread_row(1, 3)
-            order = (0, 2, 1, 3) if t == 1 else (0, 1, 2, 3) if t else (0, 1, 2, 3)
-            fused = [c for c in order if c >= PLAIN[t]]
-            for i, c in enumerate(order):
-                step = t * CORNERS + i
+            other_bank = 7 - first_bank
+            for c in range(CORNERS):
+                step = t * CORNERS + c
                 picked = picks[step % PICKS]
                 if step == WO_FIRST:
                     wo_bf = keep.tile([P, PACK, P, PACK], BF16, tag="added_sb0", align_bytes=64)
@@ -116,30 +117,29 @@ def tile_attend_deformable_pl_kernel(tc, vals, ca, cb, cc, cd, aw, wo, offs, off
                 if 0 <= step - WO_FIRST < WO_PIECES:
                     m = slice((step - WO_FIRST) * piece, (step - WO_FIRST + 1) * piece)
                     nc.scalar.copy(out=wo_into[:, m, :, :], in_=wo_dealt[:, m, :, :])
-                if c not in fused:
+                if c < PLAIN[t]:
                     nc.vector.tensor_copy(picked[:], planes[t][:].indirect(lists[c][:]))
-                    scaled = keep.tile([P, BLOCKS, P], F32, name="scaled%d" % plain_steps)
-                    if last:
-                        turned = [bank(i, [P, 2, P], "turned") for i in (7, 4)]
-                    else:
-                        whole = bank(5 + plain_steps % 3, [P, 2, 2, P], "turned")
+                    scaled = keep.tile([P, BLOCKS, P], F32, name="scaled%d" % step)
+                    if t < 2:
+                        whole = bank(first_bank if c == 0 else other_bank, [P, 2, 2, P], "turned")
                         turned = [whole[:, h] for h in range(2)]
-                    plain_steps += 1
+                    else:
+                        turned = [bank(3 + h, [P, 2, P], "turned") for h in range(2)]
                     for s in range(BLOCKS):
                         nc.tensor.transpose(turned[s // 2][:, s % 2, :], block(picked, s // 2, s % 2), ident[:])
                     for s in range(BLOCKS):
                         nc.scalar.activation(
                             out=scaled[:, s, :], in_=turned[s // 2][:, s % 2, :], func=COPY, scale=weight[:, s, c : c + 1]
                         )
-                    for s in reversed(range(BLOCKS)):
-                        opens = c == 0 and ((t == 0 and s == 3) or (t == 2 and s % 2 == 1))
+                    for s in range(BLOCKS):
+                        opens = c == 0 and ((t == 0 and s == 0) or (t == 2 and s % 2 == 0))
                         nc.tensor.matmul(sums(t, s // 2), scaled[:, s, :], ident[:], is_transpose=True, start=opens, stop=False)
                     continue
-                if c == fused[0]:
-                    if last:
-                        added = [bank(i, [P, P], "added")[:] for i in (7, 4)]
+                if c == PLAIN[t]:
+                    if t >= 2:
+                        added = [bank(3 + h, [P, P], "added")[:] for h in range(2)]
                     else:
-                        both = bank(3 + t % 2, [P, 2, P], "added")
+                        both = bank(first_bank, [P, 2, P], "added")
                         added = [both[:, h, :] for h in range(2)]
                 cuts = 2 if step == PACK * CORNERS - 1 else 1
                 n = J // cuts
@@ -152,11 +152,12 @@ def tile_attend_deformable_pl_kernel(tc, vals, ca, cb, cc, cd, aw, wo, offs, off
                     )
                 for h in range(2):
                     for u in range(2):
-                        opens = c == fused[0] and u == 0 and (h == 0 or last)
-                        closes = c == fused[-1] and u == 1 and (h == 1 or last)
+                        opens = c == PLAIN[t] and u == 0 and (h == 0 or t >= 2)
+                        closes = c == CORNERS - 1 and u == 1 and (h == 1 or t >= 2)
                         nc.tensor.matmul(added[h], block(picked, h, u), ident[:], is_transpose=True, start=opens, stop=closes)
+            first_bank = other_bank
             added_sb = keep.tile([P, 2, P], F32, name="added_sb", tag="added_sb%d" % t, align_bytes=64)
-            if last:
+            if t >= 2:
                 for h in range(2):
                     nc.scalar.copy(out=added_sb[:, h, :], in_=added[h])
             else:

@@ -24,8 +24,7 @@ PAIRS = J // 2
 BLOCKS = 4
 ROW0 = P - 2 * (CORNERS + 1)
 PICKS = 5
-PLAIN = (2, 2, 1, 0)
-WO_FIRST = 6
+PLAIN = 2
 WO_PIECES = 8
 
 
@@ -49,22 +48,29 @@ def tile_attend_deformable_pl_kernel(tc, vals, ca, cb, cc, cd, aw, wo, offs, off
         def load_row(queue, r, row):
             queue.dma_start(out=rows[ROW0 + 2 * r : ROW0 + 2 * r + 2, :], in_=row.rearrange("o (h m) -> (o h) m", h=2))
 
+        def load_plane(t):
+            nc.sync.dma_start(out=planes[t][:], in_=vals_planes[:, t, :])
+
+        def load_list(c):
+            nc.sync.dma_start(lists[c][:], lists_hbm[c])
+
         load_row(nc.sync, CORNERS, aw)
-        nc.sync.dma_start(out=planes[0][:], in_=vals_planes[:, 0, :])
+        load_plane(0)
         for r, row in enumerate((ca, cb, cc, cd)):
             load_row(nc.scalar, r, row)
-        for c in range(CORNERS):
-            nc.sync.dma_start(lists[c][:], lists_hbm[c])
-        nc.sync.dma_start(out=planes[1][:], in_=vals_planes[:, 1, :])
+        load_list(0)
+        load_list(1)
+        for t in range(1, PACK):
+            load_plane(t)
+        load_list(2)
+        load_list(3)
         nc.sync.dma_start(out=wo_raw[:], in_=wo.rearrange("(p t) f -> p t f", t=PACK))
-        for t in range(2, PACK):
-            nc.sync.dma_start(out=planes[t][:], in_=vals_planes[:, t, :])
 
         ident = keep.tile([P, P], F32)
         make_identity(nc, ident[:])
 
         nc.vector.memset(rows[0:ROW0, :], 0.0)
-        columns = bank(7, [P, 2, P], "columns")
+        columns = bank(3, [P, 2, P], "columns")
         for u in range(2):
             nc.tensor.transpose(columns[:, u, :], rows[:, u:PAIRS:2], ident[:])
         attn = keep.tile([P, 2, 2], F32)
@@ -88,8 +94,8 @@ def tile_attend_deformable_pl_kernel(tc, vals, ca, cb, cc, cd, aw, wo, offs, off
                 in_=spread_bank[:].rearrange("p (h u) m -> p h m u", u=2),
             )
 
-        for c, i in ((2, 3), (3, 4), (1, 1), (0, 2)):
-            spread_row(c, i)
+        spread_row(2, 4)
+        spread_row(3, 5)
 
         wo_dealt = wo_raw[:].rearrange("p k (m t) -> p m t k", t=PACK)
         piece = P // WO_PIECES
@@ -104,43 +110,40 @@ def tile_attend_deformable_pl_kernel(tc, vals, ca, cb, cc, cd, aw, wo, offs, off
             return tile[:, h * PAIRS + u : (h + 1) * PAIRS : 2]
 
         picks = [keep.tile([P, J], F32, name="pick%d" % i, tag="pick%d" % i, align_bytes=64) for i in range(PICKS)]
-        first_bank = 3
+        for step in range(PLAIN * PACK):
+            t, c = divmod(step, PLAIN)
+            picked = picks[step % PICKS]
+            nc.vector.tensor_copy(picked[:], planes[t][:].indirect(lists[c][:]))
+            scaled = keep.tile([P, BLOCKS, P], F32, name="scaled", tag="scaled%d" % step, align_bytes=64)
+            if step < PLAIN * PACK - 1:
+                whole = bank(3 + step % 3, [P, BLOCKS, P], "turned")
+                turned = [whole[:, s, :] for s in range(BLOCKS)]
+            else:
+                two = bank(4, [P, 2, P], "turned")
+                turned = [two[:, 0, :], two[:, 1, :], bank(5, [P, P], "turned")[:], bank(3, [P, P], "turned")[:]]
+            for s in range(BLOCKS):
+                nc.tensor.transpose(turned[s], block(picked, s // 2, s % 2), ident[:])
+            for s in range(BLOCKS):
+                nc.scalar.activation(out=scaled[:, s, :], in_=turned[s], func=COPY, scale=weight[:, s, c : c + 1])
+            for s in range(BLOCKS):
+                opens = (step, s) == (0, 0) or (t == 2 and c == 0 and s % 2 == 0)
+                nc.tensor.matmul(sums(t, s // 2), scaled[:, s, :], ident[:], is_transpose=True, start=opens, stop=False)
+
+        wo_bf = keep.tile([P, PACK, P, PACK], BF16, tag="scaled6", align_bytes=64)
+        wo_into = wo_bf[:].rearrange("p t m k -> p m t k")
         for t in range(PACK):
             last = t == PACK - 1
-            other_bank = 7 - first_bank
-            for c in range(CORNERS):
-                step = t * CORNERS + c
+            if last:
+                added = [bank(4 + h, [P, P], "added")[:] for h in range(2)]
+            else:
+                both = bank((4, 5, 3)[t], [P, 2, P], "added")
+                added = [both[:, h, :] for h in range(2)]
+            for c in range(PLAIN, CORNERS):
+                i = t * (CORNERS - PLAIN) + c - PLAIN
+                step = PLAIN * PACK + i
                 picked = picks[step % PICKS]
-                if step == WO_FIRST:
-                    wo_bf = keep.tile([P, PACK, P, PACK], BF16, tag="added_sb0", align_bytes=64)
-                    wo_into = wo_bf[:].rearrange("p t m k -> p m t k")
-                if 0 <= step - WO_FIRST < WO_PIECES:
-                    m = slice((step - WO_FIRST) * piece, (step - WO_FIRST + 1) * piece)
-                    nc.scalar.copy(out=wo_into[:, m, :, :], in_=wo_dealt[:, m, :, :])
-                if c < PLAIN[t]:
-                    nc.vector.tensor_copy(picked[:], planes[t][:].indirect(lists[c][:]))
-                    scaled = keep.tile([P, BLOCKS, P], F32, name="scaled%d" % step)
-                    if t < 2:
-                        whole = bank(first_bank if c == 0 else other_bank, [P, 2, 2, P], "turned")
-                        turned = [whole[:, h] for h in range(2)]
-                    else:
-                        turned = [bank(3 + h, [P, 2, P], "turned") for h in range(2)]
-                    for s in range(BLOCKS):
-                        nc.tensor.transpose(turned[s // 2][:, s % 2, :], block(picked, s // 2, s % 2), ident[:])
-                    for s in range(BLOCKS):
-                        nc.scalar.activation(
-                            out=scaled[:, s, :], in_=turned[s // 2][:, s % 2, :], func=COPY, scale=weight[:, s, c : c + 1]
-                        )
-                    for s in range(BLOCKS):
-                        opens = c == 0 and ((t == 0 and s == 0) or (t == 2 and s % 2 == 0))
-                        nc.tensor.matmul(sums(t, s // 2), scaled[:, s, :], ident[:], is_transpose=True, start=opens, stop=False)
-                    continue
-                if c == PLAIN[t]:
-                    if t >= 2:
-                        added = [bank(3 + h, [P, P], "added")[:] for h in range(2)]
-                    else:
-                        both = bank(first_bank, [P, 2, P], "added")
-                        added = [both[:, h, :] for h in range(2)]
+                m = slice(i * piece, (i + 1) * piece)
+                nc.scalar.copy(out=wo_into[:, m, :, :], in_=wo_dealt[:, m, :, :])
                 cuts = 2 if step == PACK * CORNERS - 1 else 1
                 n = J // cuts
                 for h in range(cuts):
@@ -152,12 +155,11 @@ def tile_attend_deformable_pl_kernel(tc, vals, ca, cb, cc, cd, aw, wo, offs, off
                     )
                 for h in range(2):
                     for u in range(2):
-                        opens = c == PLAIN[t] and u == 0 and (h == 0 or t >= 2)
-                        closes = c == CORNERS - 1 and u == 1 and (h == 1 or t >= 2)
+                        opens = (c, u) == (PLAIN, 0) and (h == 0 or last)
+                        closes = (c, u) == (CORNERS - 1, 1) and (h == 1 or last)
                         nc.tensor.matmul(added[h], block(picked, h, u), ident[:], is_transpose=True, start=opens, stop=closes)
-            first_bank = other_bank
-            added_sb = keep.tile([P, 2, P], F32, name="added_sb", tag="added_sb%d" % t, align_bytes=64)
-            if t >= 2:
+            added_sb = keep.tile([P, 2, P], F32, name="added_sb%d" % t)
+            if last:
                 for h in range(2):
                     nc.scalar.copy(out=added_sb[:, h, :], in_=added[h])
             else:
@@ -192,7 +194,7 @@ def tile_attend_deformable_pl_kernel(tc, vals, ca, cb, cc, cd, aw, wo, offs, off
         out_planes = out_0.rearrange("(p t) g -> p t g", t=PACK)
         for h in range(2):
             two = slice(2 * h, 2 * h + 2)
-            y_bank = bank(5 + h, [P, 2, G], "y_bank")
+            y_bank = bank(6 + h, [P, 2, G], "y_bank")
             for u in range(2):
                 cols = slice((2 * h + u) * P, (2 * h + u + 1) * P)
                 nc.tensor.matmul_mx(

@@ -24,7 +24,6 @@ PAIRS = J // 2
 BLOCKS = 4
 ROW0 = P - 2 * (CORNERS + 1)
 PICKS = 5
-PLAIN = 2
 WO_PIECES = 8
 
 
@@ -96,6 +95,7 @@ def tile_attend_deformable_pl_kernel(tc, vals, ca, cb, cc, cd, aw, wo, offs, off
 
         spread_row(2, 4)
         spread_row(3, 5)
+        spread_row(1, 1)
 
         wo_dealt = wo_raw[:].rearrange("p k (m t) -> p m t k", t=PACK)
         piece = P // WO_PIECES
@@ -110,12 +110,12 @@ def tile_attend_deformable_pl_kernel(tc, vals, ca, cb, cc, cd, aw, wo, offs, off
             return tile[:, h * PAIRS + u : (h + 1) * PAIRS : 2]
 
         picks = [keep.tile([P, J], F32, name="pick%d" % i, tag="pick%d" % i, align_bytes=64) for i in range(PICKS)]
-        for step in range(PLAIN * PACK):
-            t, c = divmod(step, PLAIN)
+        plain = [(0, 0), (0, 1), (1, 0), (2, 0), (3, 0)]
+        for step, (t, c) in enumerate(plain):
             picked = picks[step % PICKS]
             nc.vector.tensor_copy(picked[:], planes[t][:].indirect(lists[c][:]))
             scaled = keep.tile([P, BLOCKS, P], F32, name="scaled", tag="scaled%d" % step, align_bytes=64)
-            if step < PLAIN * PACK - 1:
+            if step < len(plain) - 1:
                 whole = bank(3 + step % 3, [P, BLOCKS, P], "turned")
                 turned = [whole[:, s, :] for s in range(BLOCKS)]
             else:
@@ -129,21 +129,24 @@ def tile_attend_deformable_pl_kernel(tc, vals, ca, cb, cc, cd, aw, wo, offs, off
                 opens = (step, s) == (0, 0) or (t == 2 and c == 0 and s % 2 == 0)
                 nc.tensor.matmul(sums(t, s // 2), scaled[:, s, :], ident[:], is_transpose=True, start=opens, stop=False)
 
-        wo_bf = keep.tile([P, PACK, P, PACK], BF16, tag="scaled6", align_bytes=64)
+        wo_bf = keep.tile([P, PACK, P, PACK], BF16, tag="scaled3", align_bytes=64)
         wo_into = wo_bf[:].rearrange("p t m k -> p m t k")
+        step = len(plain) - 1
         for t in range(PACK):
             last = t == PACK - 1
+            fused = [c for c in (2, 3, 1) if (t, c) not in plain]
             if last:
                 added = [bank(4 + h, [P, P], "added")[:] for h in range(2)]
             else:
                 both = bank((4, 5, 3)[t], [P, 2, P], "added")
                 added = [both[:, h, :] for h in range(2)]
-            for c in range(PLAIN, CORNERS):
-                i = t * (CORNERS - PLAIN) + c - PLAIN
-                step = PLAIN * PACK + i
+            for c in fused:
+                step += 1
                 picked = picks[step % PICKS]
-                m = slice(i * piece, (i + 1) * piece)
-                nc.scalar.copy(out=wo_into[:, m, :, :], in_=wo_dealt[:, m, :, :])
+                i = step - len(plain)
+                if i < WO_PIECES:
+                    m = slice(i * piece, (i + 1) * piece)
+                    nc.scalar.copy(out=wo_into[:, m, :, :], in_=wo_dealt[:, m, :, :])
                 cuts = 2 if step == PACK * CORNERS - 1 else 1
                 n = J // cuts
                 for h in range(cuts):
@@ -155,8 +158,8 @@ def tile_attend_deformable_pl_kernel(tc, vals, ca, cb, cc, cd, aw, wo, offs, off
                     )
                 for h in range(2):
                     for u in range(2):
-                        opens = (c, u) == (PLAIN, 0) and (h == 0 or last)
-                        closes = (c, u) == (CORNERS - 1, 1) and (h == 1 or last)
+                        opens = (c, u) == (fused[0], 0) and (h == 0 or last)
+                        closes = (c, u) == (fused[-1], 1) and (h == 1 or last)
                         nc.tensor.matmul(added[h], block(picked, h, u), ident[:], is_transpose=True, start=opens, stop=closes)
             added_sb = keep.tile([P, 2, P], F32, name="added_sb%d" % t)
             if last:

@@ -58,11 +58,10 @@ def tile_attend_deformable_pl_kernel(tc, vals, ca, cb, cc, cd, aw, wo, offs, off
         for r, row in enumerate((ca, cb, cc, cd)):
             load_row(nc.scalar, r, row)
         load_list(0)
-        load_list(1)
         for t in range(1, PACK):
             load_plane(t)
-        load_list(2)
-        load_list(3)
+        for c in (2, 3, 1):
+            load_list(c)
         nc.sync.dma_start(out=wo_raw[:], in_=wo.rearrange("(p t) f -> p t f", t=PACK))
 
         ident = keep.tile([P, P], F32)
@@ -110,7 +109,7 @@ def tile_attend_deformable_pl_kernel(tc, vals, ca, cb, cc, cd, aw, wo, offs, off
             return tile[:, h * PAIRS + u : (h + 1) * PAIRS : 2]
 
         picks = [keep.tile([P, J], F32, name="pick%d" % i, tag="pick%d" % i, align_bytes=64) for i in range(PICKS)]
-        plain = [(0, 0), (0, 1), (1, 0), (2, 0), (3, 0)]
+        plain = [(t, 0) for t in range(PACK)]
         for step, (t, c) in enumerate(plain):
             picked = picks[step % PICKS]
             nc.vector.tensor_copy(picked[:], planes[t][:].indirect(lists[c][:]))
@@ -129,7 +128,7 @@ def tile_attend_deformable_pl_kernel(tc, vals, ca, cb, cc, cd, aw, wo, offs, off
                 opens = (step, s) == (0, 0) or (t == 2 and c == 0 and s % 2 == 0)
                 nc.tensor.matmul(sums(t, s // 2), scaled[:, s, :], ident[:], is_transpose=True, start=opens, stop=False)
 
-        wo_bf = keep.tile([P, PACK, P, PACK], BF16, tag="scaled3", align_bytes=64)
+        wo_bf = keep.tile([P, PACK, P, PACK], BF16, tag="scaled2", align_bytes=64)
         wo_into = wo_bf[:].rearrange("p t m k -> p m t k")
         step = len(plain) - 1
         for t in range(PACK):

@@ -20,11 +20,11 @@ COPY = mybir.ActivationFunctionType.Copy
 P = 128
 PACK = 4
 CORNERS = 4
-PAIRS = J // 2
-BLOCKS = 4
-ROW0 = P - 2 * (CORNERS + 1)
-PICKS = 5
-WO_PIECES = 8
+POINTS = 4
+STEPS = PACK * CORNERS
+ROW0 = P - (CORNERS + 1)
+PICKS = 4
+SCALED = 3
 
 
 def tile_attend_deformable_pl_kernel(tc, vals, ca, cb, cc, cd, aw, wo, offs, offs2, offs3, offs4, out_0, out_1, out_2):
@@ -37,7 +37,7 @@ def tile_attend_deformable_pl_kernel(tc, vals, ca, cb, cc, cd, aw, wo, offs, off
 
         planes = [keep.tile([P, T], F32, name="plane%d" % t) for t in range(PACK)]
         lists = [keep.tile([P, J // 16], U16, name="list%d" % c) for c in range(CORNERS)]
-        rows = keep.tile([P, PAIRS], F32)
+        rows = keep.tile([P, J], F32)
         wo_raw = keep.tile([P, PACK, F], F32)
         vals_planes = vals.rearrange("(p t) c -> p t c", t=PACK)
 
@@ -45,7 +45,7 @@ def tile_attend_deformable_pl_kernel(tc, vals, ca, cb, cc, cd, aw, wo, offs, off
             return psum.tile(shape, F32, name=name, tag="bank%d" % i)
 
         def load_row(queue, r, row):
-            queue.dma_start(out=rows[ROW0 + 2 * r : ROW0 + 2 * r + 2, :], in_=row.rearrange("o (h m) -> (o h) m", h=2))
+            queue.dma_start(out=rows[ROW0 + r : ROW0 + r + 1, :], in_=row)
 
         def load_plane(t):
             nc.sync.dma_start(out=planes[t][:], in_=vals_planes[:, t, :])
@@ -57,135 +57,77 @@ def tile_attend_deformable_pl_kernel(tc, vals, ca, cb, cc, cd, aw, wo, offs, off
         load_plane(0)
         for r, row in enumerate((ca, cb, cc, cd)):
             load_row(nc.scalar, r, row)
-        load_list(0)
+        for c in range(CORNERS):
+            load_list(c)
         for t in range(1, PACK):
             load_plane(t)
-        for c in (2, 3, 1):
-            load_list(c)
         nc.sync.dma_start(out=wo_raw[:], in_=wo.rearrange("(p t) f -> p t f", t=PACK))
 
         ident = keep.tile([P, P], F32)
         make_identity(nc, ident[:])
 
         nc.vector.memset(rows[0:ROW0, :], 0.0)
-        columns = bank(3, [P, 2, P], "columns")
-        for u in range(2):
-            nc.tensor.transpose(columns[:, u, :], rows[:, u:PAIRS:2], ident[:])
-        attn = keep.tile([P, 2, 2], F32)
-        nc.scalar.copy(out=attn[:], in_=columns[:, :, P - 2 : P].rearrange("p u h -> p h u"))
-        weight = keep.tile([P, BLOCKS, CORNERS], F32)
-        for s in range(BLOCKS):
-            h, u = divmod(s, 2)
-            nc.scalar.activation(
-                out=weight[:, s, :], in_=columns[:, u, ROW0 + h : P - 2 : 2], func=COPY, scale=attn[:, h, u : u + 1]
-            )
-
-        spread = {}
-
-        def spread_row(c, i):
-            spread_bank = bank(i, [P, BLOCKS, P], "spread_bank")
-            for s in range(BLOCKS):
-                nc.tensor.transpose(spread_bank[:, s, :], weight[:, s, c : c + 1].to_broadcast([P, P]), ident[:])
-            spread[c] = keep.tile([P, J], F32, name="spread%d" % c)
-            nc.scalar.copy(
-                out=spread[c][:].rearrange("p (h m u) -> p h m u", h=2, u=2),
-                in_=spread_bank[:].rearrange("p (h u) m -> p h m u", u=2),
-            )
-
-        spread_row(2, 4)
-        spread_row(3, 5)
-        spread_row(1, 1)
-
-        wo_dealt = wo_raw[:].rearrange("p k (m t) -> p m t k", t=PACK)
-        piece = P // WO_PIECES
-
-        sums01 = bank(0, [P, 2, PAIRS], "sums01")
-        sums23 = [bank(1 + h, [P, 2, P], "sums23") for h in range(2)]
-
-        def sums(t, h):
-            return sums01[:, t, h * P : (h + 1) * P] if t < 2 else sums23[h][:, t - 2, :]
-
-        def block(tile, h, u):
-            return tile[:, h * PAIRS + u : (h + 1) * PAIRS : 2]
-
-        picks = [keep.tile([P, J], F32, name="pick%d" % i, tag="pick%d" % i, align_bytes=64) for i in range(PICKS)]
-        plain = [(t, 0) for t in range(PACK)]
-        for step, (t, c) in enumerate(plain):
-            picked = picks[step % PICKS]
-            nc.vector.tensor_copy(picked[:], planes[t][:].indirect(lists[c][:]))
-            scaled = keep.tile([P, BLOCKS, P], F32, name="scaled", tag="scaled%d" % step, align_bytes=64)
-            if step < len(plain) - 1:
-                whole = bank(3 + step % 3, [P, BLOCKS, P], "turned")
-                turned = [whole[:, s, :] for s in range(BLOCKS)]
-            else:
-                two = bank(4, [P, 2, P], "turned")
-                turned = [two[:, 0, :], two[:, 1, :], bank(5, [P, P], "turned")[:], bank(3, [P, P], "turned")[:]]
-            for s in range(BLOCKS):
-                nc.tensor.transpose(turned[s], block(picked, s // 2, s % 2), ident[:])
-            for s in range(BLOCKS):
-                nc.scalar.activation(out=scaled[:, s, :], in_=turned[s], func=COPY, scale=weight[:, s, c : c + 1])
-            for s in range(BLOCKS):
-                opens = (step, s) == (0, 0) or (t == 2 and c == 0 and s % 2 == 0)
-                nc.tensor.matmul(sums(t, s // 2), scaled[:, s, :], ident[:], is_transpose=True, start=opens, stop=False)
-
-        wo_bf = keep.tile([P, PACK, P, PACK], BF16, tag="scaled2", align_bytes=64)
-        wo_into = wo_bf[:].rearrange("p t m k -> p m t k")
-        step = len(plain) - 1
-        for t in range(PACK):
-            last = t == PACK - 1
-            fused = [c for c in (2, 3, 1) if (t, c) not in plain]
-            if last:
-                added = [bank(4 + h, [P, P], "added")[:] for h in range(2)]
-            else:
-                both = bank((4, 5, 3)[t], [P, 2, P], "added")
-                added = [both[:, h, :] for h in range(2)]
-            for c in fused:
-                step += 1
-                picked = picks[step % PICKS]
-                i = step - len(plain)
-                if i < WO_PIECES:
-                    m = slice(i * piece, (i + 1) * piece)
-                    nc.scalar.copy(out=wo_into[:, m, :, :], in_=wo_dealt[:, m, :, :])
-                cuts = 2 if step == PACK * CORNERS - 1 else 1
-                n = J // cuts
-                for h in range(cuts):
-                    nc.vector.tensor_tensor(
-                        picked[:, h * n : (h + 1) * n],
-                        planes[t][:].indirect(lists[c][:, h * n // 16 : (h + 1) * n // 16]),
-                        spread[c][:, h * n : (h + 1) * n],
-                        MULT,
-                    )
-                for h in range(2):
-                    for u in range(2):
-                        opens = (c, u) == (fused[0], 0) and (h == 0 or last)
-                        closes = (c, u) == (fused[-1], 1) and (h == 1 or last)
-                        nc.tensor.matmul(added[h], block(picked, h, u), ident[:], is_transpose=True, start=opens, stop=closes)
-            added_sb = keep.tile([P, 2, P], F32, name="added_sb%d" % t)
-            if last:
-                for h in range(2):
-                    nc.scalar.copy(out=added_sb[:, h, :], in_=added[h])
-            else:
-                nc.scalar.copy(out=added_sb[:], in_=both[:])
-            for h in range(2):
-                nc.tensor.matmul(
-                    sums(t, h), added_sb[:, h, :], ident[:], is_transpose=True, start=False, stop=(last or (t, h) == (1, 1))
+        attn = keep.tile([P, POINTS], F32)
+        weight = keep.tile([P, POINTS, CORNERS], F32)
+        for i in range(2):
+            columns = bank(2 + i, [P, 2, P], "columns")
+            for v in range(2):
+                nc.tensor.transpose(columns[:, v, :], rows[:, 2 * i + v : J : POINTS], ident[:])
+            nc.scalar.copy(out=attn[:, 2 * i : 2 * i + 2], in_=columns[:, :, P - 1])
+            for v in range(2):
+                u = 2 * i + v
+                nc.scalar.activation(
+                    out=weight[:, u, :], in_=columns[:, v, ROW0 : P - 1], func=COPY, scale=attn[:, u : u + 1]
                 )
 
-        b_bf = keep.tile([P, G, PACK], BF16, tag="pick%d" % ((PACK * CORNERS - 2) % PICKS), align_bytes=64)
-        wo_codes = keep.tile([P, F], U32, tag="pick%d" % ((PACK * CORNERS - 3) % PICKS), align_bytes=64)
+        sums = [bank(i, [P, 2, G], "sums") for i in range(2)]
+        picks = [keep.tile([P, POINTS, G], F32, name="pick%d" % i, tag="pick%d" % i, align_bytes=64) for i in range(PICKS)]
+        scaled = {}
+
+        def turn(step):
+            t, c = divmod(step, CORNERS)
+            picked = picks[step % PICKS]
+            nc.vector.tensor_copy(
+                picked[:].bitcast(U32).rearrange("p u g -> p g u"), planes[t][:].bitcast(U32).indirect(lists[c][:])
+            )
+            if step < STEPS - 1:
+                whole = bank(2 + step % 2, [P, POINTS, P], "turned")
+                turned = [whole[:, u, :] for u in range(POINTS)]
+            else:
+                turned = [bank(i, [P, P], "turned")[:] for i in (4, 5, 3, 2)]
+            for u in range(POINTS):
+                nc.tensor.transpose(turned[u], picked[:, u, :], ident[:])
+            scaled[step] = keep.tile([P, POINTS, P], F32, name="scaled", tag="scaled%d" % (step % SCALED))
+            for u in range(POINTS):
+                nc.scalar.activation(out=scaled[step][:, u, :], in_=turned[u], func=COPY, scale=weight[:, u, c : c + 1])
+
+        def turn_back(step):
+            t, c = divmod(step, CORNERS)
+            for u in range(POINTS):
+                first = (t % 2, c, u) == (0, 0, 0)
+                last = (t % 2, c, u) == (1, CORNERS - 1, POINTS - 1)
+                nc.tensor.matmul(
+                    sums[t // 2][:, t % 2, :], scaled[step][:, u, :], ident[:], is_transpose=True, start=first, stop=last
+                )
+
+        turn(0)
+        for step in range(1, STEPS):
+            turn(step)
+            turn_back(step - 1)
+        turn_back(STEPS - 1)
+
+        b_bf = keep.tile([P, G, PACK], BF16, align_bytes=64)
+        wo_bf = keep.tile([P, PACK, P, PACK], BF16, tag="pick%d" % ((STEPS - 3) % PICKS), align_bytes=64)
+        nc.vector.tensor_copy(
+            out=wo_bf[:].rearrange("p t m k -> p m t k"), in_=wo_raw[:].rearrange("p k (m t) -> p m t k", t=PACK)
+        )
+        wo_codes = keep.tile([P, F], U32, align_bytes=64)
         wo_scales = keep.tile([P, F], U8, align_bytes=64)
         nc.vector.quantize_mx(
             out=wo_codes[:].bitcast(FP8X4), scales=wo_scales[:], in_=wo_bf[:].rearrange("p t m k -> p (t m k)")
         )
-        with nc.allow_low_precision(reason="float32 sums, rounded once on the way to the quantiser"):
-            nc.vector.tensor_reduce(
-                b_bf[:, :, 0:2], sums01[:].rearrange("p t (g v) -> p g t v", v=2), mybir.AxisListType.X, ADD
-            )
-            for h in range(2):
-                nc.vector.tensor_reduce(
-                    b_bf[:, h * G // 2 : (h + 1) * G // 2, 2:4],
-                    sums23[h][:].rearrange("p t (g v) -> p g t v", v=2), mybir.AxisListType.X, ADD,
-                )
+        nc.scalar.copy(out=b_bf[:, :, 0:2], in_=sums[0][:].rearrange("p t g -> p g t"))
+        nc.scalar.copy(out=b_bf[:, :, 2:4], in_=sums[1][:].rearrange("p t g -> p g t"))
 
         b_codes = keep.tile([P, G], U32, align_bytes=64)
         b_scales = keep.tile([P, G], U8, align_bytes=64)

@@ -23,8 +23,8 @@ CORNERS = 4
 POINTS = 4
 STEPS = PACK * CORNERS
 ROW0 = P - (CORNERS + 1)
-PICKS = 4
-SCALED = 3
+PICKS = 5
+WO_PIECES = 8
 
 
 def tile_attend_deformable_pl_kernel(tc, vals, ca, cb, cc, cd, aw, wo, offs, offs2, offs3, offs4, out_0, out_1, out_2):
@@ -57,77 +57,114 @@ def tile_attend_deformable_pl_kernel(tc, vals, ca, cb, cc, cd, aw, wo, offs, off
         load_plane(0)
         for r, row in enumerate((ca, cb, cc, cd)):
             load_row(nc.scalar, r, row)
-        for c in range(CORNERS):
-            load_list(c)
+        load_list(0)
+        load_list(1)
         for t in range(1, PACK):
             load_plane(t)
+        load_list(2)
+        load_list(3)
         nc.sync.dma_start(out=wo_raw[:], in_=wo.rearrange("(p t) f -> p t f", t=PACK))
 
         ident = keep.tile([P, P], F32)
         make_identity(nc, ident[:])
 
         nc.vector.memset(rows[0:ROW0, :], 0.0)
+        columns = bank(3, [P, POINTS, P], "columns")
+        for u in range(POINTS):
+            nc.tensor.transpose(columns[:, u, :], rows[:, u:J:POINTS], ident[:])
         attn = keep.tile([P, POINTS], F32)
+        nc.scalar.copy(out=attn[:], in_=columns[:, :, P - 1])
         weight = keep.tile([P, POINTS, CORNERS], F32)
-        for i in range(2):
-            columns = bank(2 + i, [P, 2, P], "columns")
-            for v in range(2):
-                nc.tensor.transpose(columns[:, v, :], rows[:, 2 * i + v : J : POINTS], ident[:])
-            nc.scalar.copy(out=attn[:, 2 * i : 2 * i + 2], in_=columns[:, :, P - 1])
-            for v in range(2):
-                u = 2 * i + v
-                nc.scalar.activation(
-                    out=weight[:, u, :], in_=columns[:, v, ROW0 : P - 1], func=COPY, scale=attn[:, u : u + 1]
-                )
+        for u in range(POINTS):
+            nc.scalar.activation(out=weight[:, u, :], in_=columns[:, u, ROW0 : P - 1], func=COPY, scale=attn[:, u : u + 1])
+
+        spread = {}
+        for c, i in ((2, 4), (3, 5), (1, 1)):
+            spread_bank = bank(i, [P, POINTS, G], "spread_bank")
+            for u in range(POINTS):
+                nc.tensor.transpose(spread_bank[:, u, :], weight[:, u, c : c + 1].to_broadcast([P, P]), ident[:])
+            spread[c] = keep.tile([P, J], F32, name="spread%d" % c)
+            nc.scalar.copy(out=spread[c][:].rearrange("p (g u) -> p g u", u=POINTS), in_=spread_bank[:].rearrange("p u g -> p g u"))
 
         sums = [bank(i, [P, 2, G], "sums") for i in range(2)]
-        picks = [keep.tile([P, POINTS, G], F32, name="pick%d" % i, tag="pick%d" % i, align_bytes=64) for i in range(PICKS)]
-        scaled = {}
+        picks = [keep.tile([P, J], F32, name="pick%d" % i, tag="pick%d" % i, align_bytes=64) for i in range(PICKS)]
+        direct = keep.tile([P, 2, G], F32)
+        nc.vector.memset(direct[:, 0, :], 0.0)
 
-        def turn(step):
-            t, c = divmod(step, CORNERS)
+        plain = [(0, 0), (0, 1), (1, 0), (2, 0), (3, 0)]
+        for step, (t, c) in enumerate(plain):
             picked = picks[step % PICKS]
             nc.vector.tensor_copy(
-                picked[:].bitcast(U32).rearrange("p u g -> p g u"), planes[t][:].bitcast(U32).indirect(lists[c][:])
+                picked[:].bitcast(U32).rearrange("p (u g) -> p g u", u=POINTS),
+                planes[t][:].bitcast(U32).indirect(lists[c][:]),
             )
-            if step < STEPS - 1:
-                whole = bank(2 + step % 2, [P, POINTS, P], "turned")
+            scaled = keep.tile([P, POINTS, P], F32, name="scaled", tag="scaled%d" % step, align_bytes=64)
+            if step < len(plain) - 1:
+                whole = bank(3 + step % 3, [P, POINTS, P], "turned")
                 turned = [whole[:, u, :] for u in range(POINTS)]
             else:
-                turned = [bank(i, [P, P], "turned")[:] for i in (4, 5, 3, 2)]
+                two = bank(4, [P, 2, P], "turned")
+                turned = [two[:, 0, :], two[:, 1, :], bank(5, [P, P], "turned")[:], bank(3, [P, P], "turned")[:]]
             for u in range(POINTS):
-                nc.tensor.transpose(turned[u], picked[:, u, :], ident[:])
-            scaled[step] = keep.tile([P, POINTS, P], F32, name="scaled", tag="scaled%d" % (step % SCALED))
+                nc.tensor.transpose(turned[u], picked[:, u * G : (u + 1) * G], ident[:])
             for u in range(POINTS):
-                nc.scalar.activation(out=scaled[step][:, u, :], in_=turned[u], func=COPY, scale=weight[:, u, c : c + 1])
-
-        def turn_back(step):
-            t, c = divmod(step, CORNERS)
+                nc.scalar.activation(out=scaled[:, u, :], in_=turned[u], func=COPY, scale=weight[:, u, c : c + 1])
             for u in range(POINTS):
-                first = (t % 2, c, u) == (0, 0, 0)
-                last = (t % 2, c, u) == (1, CORNERS - 1, POINTS - 1)
-                nc.tensor.matmul(
-                    sums[t // 2][:, t % 2, :], scaled[step][:, u, :], ident[:], is_transpose=True, start=first, stop=last
-                )
+                opens = (t % 2, c, u) == (0, 0, 0)
+                nc.tensor.matmul(sums[t // 2][:, t % 2, :], scaled[:, u, :], ident[:], is_transpose=True, start=opens, stop=False)
 
-        turn(0)
-        for step in range(1, STEPS):
-            turn(step)
-            turn_back(step - 1)
-        turn_back(STEPS - 1)
-
+        wo_dealt = wo_raw[:].rearrange("p k (m t) -> p m t k", t=PACK)
+        wo_bf = keep.tile([P, PACK, P, PACK], BF16, tag="scaled3", align_bytes=64)
+        wo_into = wo_bf[:].rearrange("p t m k -> p m t k")
+        piece = P // WO_PIECES
         b_bf = keep.tile([P, G, PACK], BF16, align_bytes=64)
-        wo_bf = keep.tile([P, PACK, P, PACK], BF16, tag="pick%d" % ((STEPS - 3) % PICKS), align_bytes=64)
-        nc.vector.tensor_copy(
-            out=wo_bf[:].rearrange("p t m k -> p m t k"), in_=wo_raw[:].rearrange("p k (m t) -> p m t k", t=PACK)
-        )
-        wo_codes = keep.tile([P, F], U32, align_bytes=64)
+        step = len(plain) - 1
+        for t in range(PACK):
+            fused = [c for c in (2, 3, 1) if (t, c) not in plain]
+            turned_lists = fused if t < PACK - 1 else fused[:-1]
+            added = bank((4, 5, 3, 4)[t], [P, P], "added")
+            for c in fused:
+                step += 1
+                picked = picks[step % PICKS]
+                i = step - len(plain)
+                if i < WO_PIECES:
+                    m = slice(i * piece, (i + 1) * piece)
+                    nc.scalar.copy(out=wo_into[:, m, :, :], in_=wo_dealt[:, m, :, :])
+                nc.vector.tensor_tensor(picked[:], planes[t][:].indirect(lists[c][:]), spread[c][:], MULT)
+                if c in turned_lists:
+                    for u in range(POINTS):
+                        opens = (c, u) == (turned_lists[0], 0)
+                        closes = (c, u) == (turned_lists[-1], POINTS - 1)
+                        nc.tensor.matmul(
+                            added[:], picked[:, u:J:POINTS], ident[:], is_transpose=True, start=opens, stop=closes
+                        )
+            added_sb = keep.tile([P, P], F32, name="added_sb%d" % t)
+            nc.scalar.copy(out=added_sb[:], in_=added[:])
+            nc.tensor.matmul(
+                sums[t // 2][:, t % 2, :], added_sb[:], ident[:], is_transpose=True, start=False, stop=(t % 2 == 1)
+            )
+            if t == 1:
+                nc.scalar.copy(out=b_bf[:, :, 0:2], in_=sums[0][:].rearrange("p t g -> p g t"))
+
+        wo_codes = keep.tile([P, F], U32, tag="pick%d" % ((STEPS - PICKS) % PICKS), align_bytes=64)
         wo_scales = keep.tile([P, F], U8, align_bytes=64)
-        nc.vector.quantize_mx(
-            out=wo_codes[:].bitcast(FP8X4), scales=wo_scales[:], in_=wo_bf[:].rearrange("p t m k -> p (t m k)")
+
+        def quantize_wo(h):
+            cols = slice(h * F // 2, (h + 1) * F // 2)
+            nc.vector.quantize_mx(
+                out=wo_codes[:, cols].bitcast(FP8X4),
+                scales=wo_scales[:, cols],
+                in_=wo_bf[:, 2 * h : 2 * h + 2, :, :].rearrange("p t m k -> p (t m k)"),
+            )
+
+        quantize_wo(0)
+        nc.vector.tensor_reduce(
+            direct[:, 1, :], picked[:].rearrange("p (g u) -> p g u", u=POINTS), mybir.AxisListType.X, ADD
         )
-        nc.scalar.copy(out=b_bf[:, :, 0:2], in_=sums[0][:].rearrange("p t g -> p g t"))
-        nc.scalar.copy(out=b_bf[:, :, 2:4], in_=sums[1][:].rearrange("p t g -> p g t"))
+        quantize_wo(1)
+        nc.vector.tensor_tensor(
+            b_bf[:, :, 2:4], sums[1][:].rearrange("p t g -> p g t"), direct[:].rearrange("p t g -> p g t"), ADD
+        )
 
         b_codes = keep.tile([P, G], U32, align_bytes=64)
         b_scales = keep.tile([P, G], U8, align_bytes=64)

@@ -23,7 +23,8 @@ CORNERS = 4
 POINTS = 4
 STEPS = PACK * CORNERS
 ROW0 = P - (CORNERS + 1)
-PICKS = 5
+PICKS = 16
+DEALT = (7, 9, 10, 12, 13)
 WO_PIECES = 8
 
 
@@ -117,7 +118,7 @@ def tile_attend_deformable_pl_kernel(tc, vals, ca, cb, cc, cd, aw, wo, offs, off
         wo_bf = keep.tile([P, PACK, P, PACK], BF16, tag="scaled3", align_bytes=64)
         wo_into = wo_bf[:].rearrange("p t m k -> p m t k")
         piece = P // WO_PIECES
-        b_bf = keep.tile([P, G, PACK], BF16, align_bytes=64)
+        b_bf = keep.tile([P, G, PACK], BF16, tag="b_bf", align_bytes=64)
         step = len(plain) - 1
         for t in range(PACK):
             fused = [c for c in (2, 3, 1) if (t, c) not in plain]
@@ -130,13 +131,24 @@ def tile_attend_deformable_pl_kernel(tc, vals, ca, cb, cc, cd, aw, wo, offs, off
                 if i < WO_PIECES:
                     m = slice(i * piece, (i + 1) * piece)
                     nc.scalar.copy(out=wo_into[:, m, :, :], in_=wo_dealt[:, m, :, :])
-                nc.vector.tensor_tensor(picked[:], planes[t][:].indirect(lists[c][:]), spread[c][:], MULT)
+                parts = 2 if step == STEPS - 1 else 1
+                for h in range(parts):
+                    j = slice(h * J // parts, (h + 1) * J // parts)
+                    offsets = lists[c][:, j.start // 16 : j.stop // 16]
+                    nc.vector.tensor_tensor(picked[:, j], planes[t][:].indirect(offsets), spread[c][:, j], MULT)
                 if c in turned_lists:
+                    blocks = [picked[:, u:J:POINTS] for u in range(POINTS)]
+                    if step in DEALT:
+                        work = keep.tile([P, POINTS, G], F32, name="work", tag="scaled4", align_bytes=64)
+                        nc.scalar.copy(
+                            out=work[:].rearrange("p u g -> p g u"), in_=picked[:].rearrange("p (g u) -> p g u", u=POINTS)
+                        )
+                        blocks = [work[:, u, :] for u in range(POINTS)]
                     for u in range(POINTS):
                         opens = (c, u) == (turned_lists[0], 0)
                         closes = (c, u) == (turned_lists[-1], POINTS - 1)
                         nc.tensor.matmul(
-                            added[:], picked[:, u:J:POINTS], ident[:], is_transpose=True, start=opens, stop=closes
+                            added[:], blocks[u], ident[:], is_transpose=True, start=opens, stop=closes
                         )
             added_sb = keep.tile([P, P], F32, name="added_sb%d" % t)
             nc.scalar.copy(out=added_sb[:], in_=added[:])
@@ -146,29 +158,35 @@ def tile_attend_deformable_pl_kernel(tc, vals, ca, cb, cc, cd, aw, wo, offs, off
             if t == 1:
                 nc.scalar.copy(out=b_bf[:, :, 0:2], in_=sums[0][:].rearrange("p t g -> p g t"))
 
-        wo_codes = keep.tile([P, F], U32, tag="pick%d" % ((STEPS - PICKS) % PICKS), align_bytes=64)
+        halves = [slice(h * G // 2, (h + 1) * G // 2) for h in range(2)]
         wo_scales = keep.tile([P, F], U8, align_bytes=64)
+        wo_codes = {}
 
-        def quantize_wo(h):
-            cols = slice(h * F // 2, (h + 1) * F // 2)
+        def quantize_wo(h, tag):
+            wo_codes[h] = keep.tile([P, F // 2], U32, name="wo_codes", tag=tag, align_bytes=64)
             nc.vector.quantize_mx(
-                out=wo_codes[:, cols].bitcast(FP8X4),
-                scales=wo_scales[:, cols],
+                out=wo_codes[h][:].bitcast(FP8X4),
+                scales=wo_scales[:, h * F // 2 : (h + 1) * F // 2],
                 in_=wo_bf[:, 2 * h : 2 * h + 2, :, :].rearrange("p t m k -> p (t m k)"),
             )
 
-        quantize_wo(0)
-        nc.vector.tensor_reduce(
-            direct[:, 1, :], picked[:].rearrange("p (g u) -> p g u", u=POINTS), mybir.AxisListType.X, ADD
-        )
-        quantize_wo(1)
-        nc.vector.tensor_tensor(
-            b_bf[:, :, 2:4], sums[1][:].rearrange("p t g -> p g t"), direct[:].rearrange("p t g -> p g t"), ADD
-        )
-
+        for g in halves:
+            nc.vector.tensor_reduce(
+                direct[:, 1, g], picked[:].rearrange("p (g u) -> p g u", u=POINTS)[:, g, :], mybir.AxisListType.X, ADD
+            )
+        quantize_wo(0, "wo_codes")
+        for g in halves:
+            nc.vector.tensor_tensor(
+                b_bf[:, g, 2:4], sums[1][:].rearrange("p t g -> p g t")[:, g, :],
+                direct[:].rearrange("p t g -> p g t")[:, g, :], ADD,
+            )
         b_codes = keep.tile([P, G], U32, align_bytes=64)
         b_scales = keep.tile([P, G], U8, align_bytes=64)
-        nc.vector.quantize_mx(out=b_codes[:].bitcast(FP8X4), scales=b_scales[:], in_=b_bf[:].rearrange("p g t -> p (g t)"))
+        for g in halves:
+            nc.vector.quantize_mx(
+                out=b_codes[:, g].bitcast(FP8X4), scales=b_scales[:, g], in_=b_bf[:, g, :].rearrange("p g t -> p (g t)")
+            )
+        quantize_wo(1, "b_bf")
 
         y = keep.tile([P, PACK, G], F32)
         y_bf = keep.tile([P, G, PACK], BF16, align_bytes=64)
@@ -180,7 +198,7 @@ def tile_attend_deformable_pl_kernel(tc, vals, ca, cb, cc, cd, aw, wo, offs, off
                 cols = slice((2 * h + u) * P, (2 * h + u + 1) * P)
                 nc.tensor.matmul_mx(
                     out=y_bank[:, u, :],
-                    lhsT=wo_codes[:, cols].bitcast(FP8X4),
+                    lhsT=wo_codes[h][:, u * P : (u + 1) * P].bitcast(FP8X4),
                     lhsT_scale=wo_scales[:, cols],
                     rhs=b_codes[:].bitcast(FP8X4),
                     rhs_scale=b_scales[:],

@@ -22,9 +22,8 @@ PACK = 4
 CORNERS = 4
 POINTS = 4
 STEPS = PACK * CORNERS
-ROW0 = P - (CORNERS + 1)
-PICKS = 16
-DEALT = (7, 9, 10, 12, 13)
+BLOCKS = J // P
+ROW0 = P - BLOCKS * (CORNERS + 1)
 WO_PIECES = 8
 
 
@@ -38,96 +37,83 @@ def tile_attend_deformable_pl_kernel(tc, vals, ca, cb, cc, cd, aw, wo, offs, off
 
         planes = [keep.tile([P, T], F32, name="plane%d" % t) for t in range(PACK)]
         lists = [keep.tile([P, J // 16], U16, name="list%d" % c) for c in range(CORNERS)]
-        rows = keep.tile([P, J], F32)
+        rows = keep.tile([P, P], F32)
         wo_raw = keep.tile([P, PACK, F], F32)
         vals_planes = vals.rearrange("(p t) c -> p t c", t=PACK)
 
         def bank(i, shape, name):
             return psum.tile(shape, F32, name=name, tag="bank%d" % i)
 
-        def load_row(queue, r, row):
-            queue.dma_start(out=rows[ROW0 + r : ROW0 + r + 1, :], in_=row)
-
         def load_plane(t):
             nc.sync.dma_start(out=planes[t][:], in_=vals_planes[:, t, :])
 
-        def load_list(c):
-            nc.sync.dma_start(lists[c][:], lists_hbm[c])
-
-        load_row(nc.sync, CORNERS, aw)
         load_plane(0)
-        for r, row in enumerate((ca, cb, cc, cd)):
-            load_row(nc.scalar, r, row)
-        load_list(0)
-        load_list(1)
+        for r, row in enumerate((aw, ca, cb, cc, cd)):
+            first = ROW0 + BLOCKS * r
+            nc.scalar.dma_start(out=rows[first : first + BLOCKS, :], in_=row.rearrange("o (q m) -> (o q) m", m=P))
+        for c in range(CORNERS):
+            nc.sync.dma_start(lists[c][:], lists_hbm[c])
         for t in range(1, PACK):
             load_plane(t)
-        load_list(2)
-        load_list(3)
         nc.sync.dma_start(out=wo_raw[:], in_=wo.rearrange("(p t) f -> p t f", t=PACK))
 
         ident = keep.tile([P, P], F32)
         make_identity(nc, ident[:])
 
         nc.vector.memset(rows[0:ROW0, :], 0.0)
-        columns = bank(3, [P, POINTS, P], "columns")
-        for u in range(POINTS):
-            nc.tensor.transpose(columns[:, u, :], rows[:, u:J:POINTS], ident[:])
-        attn = keep.tile([P, POINTS], F32)
-        nc.scalar.copy(out=attn[:], in_=columns[:, :, P - 1])
-        weight = keep.tile([P, POINTS, CORNERS], F32)
-        for u in range(POINTS):
-            nc.scalar.activation(out=weight[:, u, :], in_=columns[:, u, ROW0 : P - 1], func=COPY, scale=attn[:, u : u + 1])
+        columns = bank(3, [P, P], "columns")
+        nc.tensor.transpose(columns[:], rows[:], ident[:])
+        attn = keep.tile([P, BLOCKS], F32)
+        nc.scalar.copy(out=attn[:], in_=columns[:, ROW0 : ROW0 + BLOCKS])
+        weight = keep.tile([P, BLOCKS, CORNERS], F32)
+        for q in range(BLOCKS):
+            nc.scalar.activation(
+                out=weight[:, q, :], in_=columns[:, ROW0 + BLOCKS + q : P : BLOCKS], func=COPY, scale=attn[:, q : q + 1]
+            )
 
-        spread = {}
-        for c, i in ((2, 4), (3, 5), (1, 1)):
-            spread_bank = bank(i, [P, POINTS, G], "spread_bank")
-            for u in range(POINTS):
-                nc.tensor.transpose(spread_bank[:, u, :], weight[:, u, c : c + 1].to_broadcast([P, P]), ident[:])
-            spread[c] = keep.tile([P, J], F32, name="spread%d" % c)
-            nc.scalar.copy(out=spread[c][:].rearrange("p (g u) -> p g u", u=POINTS), in_=spread_bank[:].rearrange("p u g -> p g u"))
+        spread = []
+        for c, i in enumerate((5, 6, 7, 1)):
+            spread_bank = bank(i, [P, BLOCKS, P], "spread_bank")
+            for q in range(BLOCKS):
+                nc.tensor.transpose(spread_bank[:, q, :], weight[:, q, c : c + 1].to_broadcast([P, P]), ident[:])
+            spread.append(keep.tile([P, J], F32, name="spread%d" % c))
+            nc.scalar.copy(out=spread[c][:], in_=spread_bank[:].rearrange("p q m -> p (q m)"))
 
         sums = [bank(i, [P, 2, G], "sums") for i in range(2)]
-        picks = [keep.tile([P, J], F32, name="pick%d" % i, tag="pick%d" % i, align_bytes=64) for i in range(PICKS)]
+        picks = [keep.tile([P, J], F32, name="pick%d" % i, align_bytes=64) for i in range(STEPS)]
         direct = keep.tile([P, 2, G], F32)
         nc.vector.memset(direct[:, 0, :], 0.0)
 
-        plain = [(0, 0), (0, 1), (1, 0), (2, 0), (3, 0)]
-        for step, (t, c) in enumerate(plain):
-            picked = picks[step % PICKS]
-            nc.vector.tensor_copy(
-                picked[:].bitcast(U32).rearrange("p (u g) -> p g u", u=POINTS),
-                planes[t][:].bitcast(U32).indirect(lists[c][:]),
-            )
-            scaled = keep.tile([P, POINTS, P], F32, name="scaled", tag="scaled%d" % step, align_bytes=64)
-            if step < len(plain) - 1:
-                whole = bank(3 + step % 3, [P, POINTS, P], "turned")
-                turned = [whole[:, u, :] for u in range(POINTS)]
-            else:
-                two = bank(4, [P, 2, P], "turned")
-                turned = [two[:, 0, :], two[:, 1, :], bank(5, [P, P], "turned")[:], bank(3, [P, P], "turned")[:]]
-            for u in range(POINTS):
-                nc.tensor.transpose(turned[u], picked[:, u * G : (u + 1) * G], ident[:])
-            for u in range(POINTS):
-                nc.scalar.activation(out=scaled[:, u, :], in_=turned[u], func=COPY, scale=weight[:, u, c : c + 1])
-            for u in range(POINTS):
-                opens = (t % 2, c, u) == (0, 0, 0)
-                nc.tensor.matmul(sums[t // 2][:, t % 2, :], scaled[:, u, :], ident[:], is_transpose=True, start=opens, stop=False)
+        samples = bank(2, [P, BLOCKS, P], "samples")
+        for c in range(CORNERS):
+            picked = picks[c]
+            nc.vector.tensor_copy(picked[:], planes[0][:].indirect(lists[c][:]))
+            turned = bank((3, 5, 6, 3)[c], [P, BLOCKS, P], "turned")
+            scaled = keep.tile([P, BLOCKS, P], F32, name="scaled", tag="scaled%d" % c, align_bytes=64)
+            for q in range(BLOCKS):
+                nc.tensor.transpose(turned[:, q, :], picked[:, q * P : (q + 1) * P], ident[:])
+            for q in range(BLOCKS):
+                nc.scalar.activation(out=scaled[:, q, :], in_=turned[:, q, :], func=COPY, scale=weight[:, q, c : c + 1])
+            for q in range(BLOCKS):
+                nc.tensor.matmul(
+                    samples[:, q, :], scaled[:, q, :], ident[:], is_transpose=True,
+                    start=(c, q) == (0, 0), stop=(c, q) == (CORNERS - 1, BLOCKS - 1),
+                )
+        dealt = keep.tile([P, POINTS, G], F32)
+        nc.scalar.copy(out=dealt[:], in_=samples[:].rearrange("p q m -> p (q m)").rearrange("p (g u) -> p u g", u=POINTS))
 
         wo_dealt = wo_raw[:].rearrange("p k (m t) -> p m t k", t=PACK)
-        wo_bf = keep.tile([P, PACK, P, PACK], BF16, tag="scaled3", align_bytes=64)
+        wo_bf = keep.tile([P, PACK, P, PACK], BF16, tag="scaled2", align_bytes=64)
         wo_into = wo_bf[:].rearrange("p t m k -> p m t k")
         piece = P // WO_PIECES
         b_bf = keep.tile([P, G, PACK], BF16, tag="b_bf", align_bytes=64)
-        step = len(plain) - 1
         for t in range(PACK):
-            fused = [c for c in (2, 3, 1) if (t, c) not in plain]
-            turned_lists = fused if t < PACK - 1 else fused[:-1]
-            added = bank((4, 5, 3, 4)[t], [P, P], "added")
-            for c in fused:
-                step += 1
-                picked = picks[step % PICKS]
-                i = step - len(plain)
+            added = bank((3, 6)[t % 2], [P, P], "added")
+            terms = [[dealt[:, u, :] for u in range(POINTS)]] if t == 0 else []
+            for c in range(CORNERS if t > 0 else 0):
+                step = CORNERS * t + c
+                picked = picks[step]
+                i = step - CORNERS
                 if i < WO_PIECES:
                     m = slice(i * piece, (i + 1) * piece)
                     nc.scalar.copy(out=wo_into[:, m, :, :], in_=wo_dealt[:, m, :, :])
@@ -136,24 +122,18 @@ def tile_attend_deformable_pl_kernel(tc, vals, ca, cb, cc, cd, aw, wo, offs, off
                     j = slice(h * J // parts, (h + 1) * J // parts)
                     offsets = lists[c][:, j.start // 16 : j.stop // 16]
                     nc.vector.tensor_tensor(picked[:, j], planes[t][:].indirect(offsets), spread[c][:, j], MULT)
-                if c in turned_lists:
-                    blocks = [picked[:, u:J:POINTS] for u in range(POINTS)]
-                    if step in DEALT:
-                        work = keep.tile([P, POINTS, G], F32, name="work", tag="scaled4", align_bytes=64)
-                        nc.scalar.copy(
-                            out=work[:].rearrange("p u g -> p g u"), in_=picked[:].rearrange("p (g u) -> p g u", u=POINTS)
-                        )
-                        blocks = [work[:, u, :] for u in range(POINTS)]
-                    for u in range(POINTS):
-                        opens = (c, u) == (turned_lists[0], 0)
-                        closes = (c, u) == (turned_lists[-1], POINTS - 1)
-                        nc.tensor.matmul(
-                            added[:], blocks[u], ident[:], is_transpose=True, start=opens, stop=closes
-                        )
+                if step < STEPS - 1:
+                    terms.append([picked[:, u:J:POINTS] for u in range(POINTS)])
+            for n, blocks in enumerate(terms):
+                for u in range(POINTS):
+                    nc.tensor.matmul(
+                        added[:], blocks[u], ident[:], is_transpose=True,
+                        start=(n, u) == (0, 0), stop=(n, u) == (len(terms) - 1, POINTS - 1),
+                    )
             added_sb = keep.tile([P, P], F32, name="added_sb%d" % t)
             nc.scalar.copy(out=added_sb[:], in_=added[:])
             nc.tensor.matmul(
-                sums[t // 2][:, t % 2, :], added_sb[:], ident[:], is_transpose=True, start=False, stop=(t % 2 == 1)
+                sums[t // 2][:, t % 2, :], added_sb[:], ident[:], is_transpose=True, start=(t % 2 == 0), stop=(t % 2 == 1)
             )
             if t == 1:
                 nc.scalar.copy(out=b_bf[:, :, 0:2], in_=sums[0][:].rearrange("p t g -> p g t"))
@@ -193,7 +173,7 @@ def tile_attend_deformable_pl_kernel(tc, vals, ca, cb, cc, cd, aw, wo, offs, off
         out_planes = out_0.rearrange("(p t) g -> p t g", t=PACK)
         for h in range(2):
             two = slice(2 * h, 2 * h + 2)
-            y_bank = bank(6 + h, [P, 2, G], "y_bank")
+            y_bank = bank(4 + h, [P, 2, G], "y_bank")
             for u in range(2):
                 cols = slice((2 * h + u) * P, (2 * h + u + 1) * P)
                 nc.tensor.matmul_mx(

@@ -25,6 +25,7 @@ STEPS = PACK * CORNERS
 BLOCKS = J // P
 ROW0 = P - BLOCKS * (CORNERS + 1)
 WO_PIECES = 8
+DIRECT = 2
 
 
 def tile_attend_deformable_pl_kernel(tc, vals, ca, cb, cc, cd, aw, wo, offs, offs2, offs3, offs4, out_0, out_1, out_2):
@@ -80,14 +81,16 @@ def tile_attend_deformable_pl_kernel(tc, vals, ca, cb, cc, cd, aw, wo, offs, off
             nc.scalar.copy(out=spread[c][:], in_=spread_bank[:].rearrange("p q m -> p (q m)"))
 
         sums = [bank(i, [P, 2, G], "sums") for i in range(2)]
-        picks = [keep.tile([P, J], F32, name="pick%d" % i, align_bytes=64) for i in range(STEPS)]
-        direct = keep.tile([P, 2, G], F32)
+        picks = [keep.tile([P, J], F32, name="pick%d" % i, align_bytes=64) for i in range(STEPS - DIRECT)]
+        last_picks = keep.tile([P, DIRECT, J], F32)
+        picks = [pick[:] for pick in picks] + [last_picks[:, i, :] for i in range(DIRECT)]
+        direct = keep.tile([P, 2, G], F32, tag="direct", align_bytes=64)
         nc.vector.memset(direct[:, 0, :], 0.0)
 
         samples = bank(2, [P, BLOCKS, P], "samples")
         for c in range(CORNERS):
             picked = picks[c]
-            nc.vector.tensor_copy(picked[:], planes[0][:].indirect(lists[c][:]))
+            nc.vector.tensor_copy(picked, planes[0][:].indirect(lists[c][:]))
             turned = bank((3, 5, 6, 3)[c], [P, BLOCKS, P], "turned")
             scaled = keep.tile([P, BLOCKS, P], F32, name="scaled", tag="scaled%d" % c, align_bytes=64)
             for q in range(BLOCKS):
@@ -122,7 +125,7 @@ def tile_attend_deformable_pl_kernel(tc, vals, ca, cb, cc, cd, aw, wo, offs, off
                     j = slice(h * J // parts, (h + 1) * J // parts)
                     offsets = lists[c][:, j.start // 16 : j.stop // 16]
                     nc.vector.tensor_tensor(picked[:, j], planes[t][:].indirect(offsets), spread[c][:, j], MULT)
-                if step < STEPS - 1:
+                if step < STEPS - DIRECT:
                     terms.append([picked[:, u:J:POINTS] for u in range(POINTS)])
             for n, blocks in enumerate(terms):
                 for u in range(POINTS):
@@ -140,21 +143,19 @@ def tile_attend_deformable_pl_kernel(tc, vals, ca, cb, cc, cd, aw, wo, offs, off
 
         halves = [slice(h * G // 2, (h + 1) * G // 2) for h in range(2)]
         wo_scales = keep.tile([P, F], U8, align_bytes=64)
-        wo_codes = {}
 
-        def quantize_wo(h, tag):
-            wo_codes[h] = keep.tile([P, F // 2], U32, name="wo_codes", tag=tag, align_bytes=64)
+        def quantize_wo(codes, first, last):
             nc.vector.quantize_mx(
-                out=wo_codes[h][:].bitcast(FP8X4),
-                scales=wo_scales[:, h * F // 2 : (h + 1) * F // 2],
-                in_=wo_bf[:, 2 * h : 2 * h + 2, :, :].rearrange("p t m k -> p (t m k)"),
+                out=codes.bitcast(FP8X4),
+                scales=wo_scales[:, first * P : last * P],
+                in_=wo_bf[:, first:last, :, :].rearrange("p t m k -> p (t m k)"),
             )
 
         for g in halves:
             nc.vector.tensor_reduce(
-                direct[:, 1, g], picked[:].rearrange("p (g u) -> p g u", u=POINTS)[:, g, :], mybir.AxisListType.X, ADD
+                direct[:, 1, g], last_picks[:].rearrange("p l (g u) -> p g l u", u=POINTS)[:, g, :, :],
+                mybir.AxisListType.XY, ADD,
             )
-        quantize_wo(0, "wo_codes")
         for g in halves:
             nc.vector.tensor_tensor(
                 b_bf[:, g, 2:4], sums[1][:].rearrange("p t g -> p g t")[:, g, :],
@@ -162,11 +163,17 @@ def tile_attend_deformable_pl_kernel(tc, vals, ca, cb, cc, cd, aw, wo, offs, off
             )
         b_codes = keep.tile([P, G], U32, align_bytes=64)
         b_scales = keep.tile([P, G], U8, align_bytes=64)
-        for g in halves:
+        wo_first = keep.tile([P, P], U32, tag="direct", align_bytes=64)
+        for h, g in enumerate(halves):
+            if h == 1:
+                quantize_wo(wo_first[:], 0, 1)
             nc.vector.quantize_mx(
                 out=b_codes[:, g].bitcast(FP8X4), scales=b_scales[:, g], in_=b_bf[:, g, :].rearrange("p g t -> p (g t)")
             )
-        quantize_wo(1, "b_bf")
+        wo_rest = keep.tile([P, F - P], U32, tag="b_bf", align_bytes=64)
+        quantize_wo(wo_rest[:, 0:P], 1, 2)
+        quantize_wo(wo_rest[:, P:], 2, PACK)
+        wo_codes = [wo_first[:]] + [wo_rest[:, t * P : (t + 1) * P] for t in range(PACK - 1)]
 
         y = keep.tile([P, PACK, G], F32)
         y_bf = keep.tile([P, G, PACK], BF16, align_bytes=64)
@@ -178,7 +185,7 @@ def tile_attend_deformable_pl_kernel(tc, vals, ca, cb, cc, cd, aw, wo, offs, off
                 cols = slice((2 * h + u) * P, (2 * h + u + 1) * P)
                 nc.tensor.matmul_mx(
                     out=y_bank[:, u, :],
-                    lhsT=wo_codes[h][:, u * P : (u + 1) * P].bitcast(FP8X4),
+                    lhsT=wo_codes[2 * h + u].bitcast(FP8X4),
                     lhsT_scale=wo_scales[:, cols],
                     rhs=b_codes[:].bitcast(FP8X4),
                     rhs_scale=b_scales[:],

@@ -25,7 +25,7 @@ STEPS = PACK * CORNERS
 BLOCKS = J // P
 ROW0 = P - BLOCKS * (CORNERS + 1)
 WO_PIECES = 8
-DIRECT = 2
+DIRECT = 1
 
 
 def tile_attend_deformable_pl_kernel(tc, vals, ca, cb, cc, cd, aw, wo, offs, offs2, offs3, offs4, out_0, out_1, out_2):
@@ -57,6 +57,9 @@ def tile_attend_deformable_pl_kernel(tc, vals, ca, cb, cc, cd, aw, wo, offs, off
         for t in range(1, PACK):
             load_plane(t)
         nc.sync.dma_start(out=wo_raw[:], in_=wo.rearrange("(p t) f -> p t f", t=PACK))
+        by_query = [keep.tile([P, POINTS], F32, name="by_query%d" % i) for i in range(2)]
+        for tile, row in zip(by_query, (cc, aw)):
+            nc.sync.dma_start(out=tile[:], in_=row.rearrange("o (g u) -> (o g) u", u=POINTS))
 
         ident = keep.tile([P, P], F32)
         make_identity(nc, ident[:])
@@ -81,11 +84,12 @@ def tile_attend_deformable_pl_kernel(tc, vals, ca, cb, cc, cd, aw, wo, offs, off
             nc.scalar.copy(out=spread[c][:], in_=spread_bank[:].rearrange("p q m -> p (q m)"))
 
         sums = [bank(i, [P, 2, G], "sums") for i in range(2)]
-        picks = [keep.tile([P, J], F32, name="pick%d" % i, align_bytes=64) for i in range(STEPS - DIRECT)]
-        last_picks = keep.tile([P, DIRECT, J], F32)
-        picks = [pick[:] for pick in picks] + [last_picks[:, i, :] for i in range(DIRECT)]
-        direct = keep.tile([P, 2, G], F32, tag="direct", align_bytes=64)
-        nc.vector.memset(direct[:, 0, :], 0.0)
+        picks = [keep.tile([P, J], F32, name="pick", tag="pick%d" % i, align_bytes=64) for i in range(STEPS - 2)]
+        picks = [pick[:] for pick in picks]
+        halves = [slice(h * G // 2, (h + 1) * G // 2) for h in range(2)]
+        direct = [keep.tile([P, 2, G // 2], F32, name="direct", tag="direct%d" % h, align_bytes=64) for h in range(2)]
+        for h in range(2):
+            nc.vector.memset(direct[h][:, 0, :], 0.0)
 
         samples = bank(2, [P, BLOCKS, P], "samples")
         for c in range(CORNERS):
@@ -109,17 +113,25 @@ def tile_attend_deformable_pl_kernel(tc, vals, ca, cb, cc, cd, aw, wo, offs, off
         wo_bf = keep.tile([P, PACK, P, PACK], BF16, tag="scaled2", align_bytes=64)
         wo_into = wo_bf[:].rearrange("p t m k -> p m t k")
         piece = P // WO_PIECES
-        b_bf = keep.tile([P, G, PACK], BF16, tag="b_bf", align_bytes=64)
+        b_bf = [keep.tile([P, G // 2, PACK], BF16, name="b_bf", tag="b_bf%d" % h, align_bytes=64) for h in range(2)]
         for t in range(PACK):
             added = bank((3, 6)[t % 2], [P, P], "added")
             terms = [[dealt[:, u, :] for u in range(POINTS)]] if t == 0 else []
             for c in range(CORNERS if t > 0 else 0):
                 step = CORNERS * t + c
+                if step >= STEPS - 2:
+                    picks.append(keep.tile([P, J], F32, name="pick", tag="pick%d" % (step - CORNERS), align_bytes=64)[:])
                 picked = picks[step]
                 i = step - CORNERS
                 if i < WO_PIECES:
                     m = slice(i * piece, (i + 1) * piece)
                     nc.scalar.copy(out=wo_into[:, m, :, :], in_=wo_dealt[:, m, :, :])
+                if step == STEPS - 2:
+                    nc.vector.tensor_copy(
+                        picked.bitcast(U32).rearrange("p (u g) -> p g u", u=POINTS),
+                        planes[t][:].bitcast(U32).indirect(lists[c][:]),
+                    )
+                    continue
                 parts = 2 if step == STEPS - 1 else 1
                 for h in range(parts):
                     j = slice(h * J // parts, (h + 1) * J // parts)
@@ -136,12 +148,29 @@ def tile_attend_deformable_pl_kernel(tc, vals, ca, cb, cc, cd, aw, wo, offs, off
             added_sb = keep.tile([P, P], F32, name="added_sb%d" % t)
             nc.scalar.copy(out=added_sb[:], in_=added[:])
             nc.tensor.matmul(
-                sums[t // 2][:, t % 2, :], added_sb[:], ident[:], is_transpose=True, start=(t % 2 == 0), stop=(t % 2 == 1)
+                sums[t // 2][:, t % 2, :], added_sb[:], ident[:], is_transpose=True, start=(t % 2 == 0), stop=(t == 1)
             )
             if t == 1:
-                nc.scalar.copy(out=b_bf[:, :, 0:2], in_=sums[0][:].rearrange("p t g -> p g t"))
+                for h, g in enumerate(halves):
+                    nc.scalar.copy(out=b_bf[h][:, :, 0:2], in_=sums[0][:].rearrange("p t g -> p g t")[:, g, :])
 
-        halves = [slice(h * G // 2, (h + 1) * G // 2) for h in range(2)]
+        late_weight = keep.tile([P, POINTS], F32, tag="scaled3", align_bytes=64)
+        for u in range(POINTS):
+            nc.scalar.activation(
+                out=late_weight[:, u : u + 1], in_=by_query[0][:, u : u + 1], func=COPY, scale=by_query[1][:, u : u + 1]
+            )
+        picked = picks[STEPS - 2]
+        scaled = keep.tile([P, POINTS, P], F32, name="late_scaled")
+        turned = [bank(i, [P, P], "late_turned") for i in (2, 7, 4, 5)]
+        for u in range(POINTS):
+            nc.tensor.transpose(turned[u][:], picked[:, u * G : (u + 1) * G], ident[:])
+        for u in range(POINTS):
+            nc.scalar.activation(out=scaled[:, u, :], in_=turned[u][:], func=COPY, scale=late_weight[:, u : u + 1])
+        for u in range(POINTS):
+            nc.tensor.matmul(
+                sums[1][:, 1, :], scaled[:, u, :], ident[:], is_transpose=True, start=False, stop=(u == POINTS - 1)
+            )
+
         wo_scales = keep.tile([P, F], U8, align_bytes=64)
 
         def quantize_wo(codes, first, last):
@@ -151,29 +180,29 @@ def tile_attend_deformable_pl_kernel(tc, vals, ca, cb, cc, cd, aw, wo, offs, off
                 in_=wo_bf[:, first:last, :, :].rearrange("p t m k -> p (t m k)"),
             )
 
-        for g in halves:
+        for h, g in enumerate(halves):
             nc.vector.tensor_reduce(
-                direct[:, 1, g], last_picks[:].rearrange("p l (g u) -> p g l u", u=POINTS)[:, g, :, :],
-                mybir.AxisListType.XY, ADD,
+                direct[h][:, 1, :], picks[STEPS - 1].rearrange("p (g u) -> p g u", u=POINTS)[:, g, :],
+                mybir.AxisListType.X, ADD,
             )
-        for g in halves:
+        for h, g in enumerate(halves):
             nc.vector.tensor_tensor(
-                b_bf[:, g, 2:4], sums[1][:].rearrange("p t g -> p g t")[:, g, :],
-                direct[:].rearrange("p t g -> p g t")[:, g, :], ADD,
+                b_bf[h][:, :, 2:4], sums[1][:].rearrange("p t g -> p g t")[:, g, :],
+                direct[h][:].rearrange("p t g -> p g t"), ADD,
             )
         b_codes = keep.tile([P, G], U32, align_bytes=64)
         b_scales = keep.tile([P, G], U8, align_bytes=64)
-        wo_first = keep.tile([P, P], U32, tag="direct", align_bytes=64)
+        wo_first = keep.tile([P, P], U32, tag="direct0", align_bytes=64)
         for h, g in enumerate(halves):
             if h == 1:
                 quantize_wo(wo_first[:], 0, 1)
             nc.vector.quantize_mx(
-                out=b_codes[:, g].bitcast(FP8X4), scales=b_scales[:, g], in_=b_bf[:, g, :].rearrange("p g t -> p (g t)")
+                out=b_codes[:, g].bitcast(FP8X4), scales=b_scales[:, g], in_=b_bf[h][:].rearrange("p g t -> p (g t)")
             )
-        wo_rest = keep.tile([P, F - P], U32, tag="b_bf", align_bytes=64)
-        quantize_wo(wo_rest[:, 0:P], 1, 2)
-        quantize_wo(wo_rest[:, P:], 2, PACK)
+        wo_rest = keep.tile([P, F - P], U32, tag="b_bf0", align_bytes=64)
         wo_codes = [wo_first[:]] + [wo_rest[:, t * P : (t + 1) * P] for t in range(PACK - 1)]
+        for t in range(1, PACK):
+            quantize_wo(wo_codes[t], t, t + 1)
 
         y = keep.tile([P, PACK, G], F32)
         y_bf = keep.tile([P, G, PACK], BF16, align_bytes=64)

@@ -21,11 +21,9 @@ P = 128
 PACK = 4
 CORNERS = 4
 POINTS = 4
-STEPS = PACK * CORNERS
-BLOCKS = J // P
-ROW0 = P - BLOCKS * (CORNERS + 1)
-WO_PIECES = 8
-DIRECT = 1
+ROW_PITCH = 8
+WO_PIECES = 4
+RING = 3
 
 
 def tile_attend_deformable_pl_kernel(tc, vals, ca, cb, cc, cd, aw, wo, offs, offs2, offs3, offs4, out_0, out_1, out_2):
@@ -38,7 +36,7 @@ def tile_attend_deformable_pl_kernel(tc, vals, ca, cb, cc, cd, aw, wo, offs, off
 
         planes = [keep.tile([P, T], F32, name="plane%d" % t) for t in range(PACK)]
         lists = [keep.tile([P, J // 16], U16, name="list%d" % c) for c in range(CORNERS)]
-        rows = keep.tile([P, P], F32)
+        given = keep.tile([P, CORNERS + 1, ROW_PITCH], F32)
         wo_raw = keep.tile([P, PACK, F], F32)
         vals_planes = vals.rearrange("(p t) c -> p t c", t=PACK)
 
@@ -49,172 +47,148 @@ def tile_attend_deformable_pl_kernel(tc, vals, ca, cb, cc, cd, aw, wo, offs, off
             nc.sync.dma_start(out=planes[t][:], in_=vals_planes[:, t, :])
 
         load_plane(0)
-        for r, row in enumerate((aw, ca, cb, cc, cd)):
-            first = ROW0 + BLOCKS * r
-            nc.scalar.dma_start(out=rows[first : first + BLOCKS, :], in_=row.rearrange("o (q m) -> (o q) m", m=P))
-        for c in range(CORNERS):
+        for r in (0, 1, 3, 2, 4):
+            row = (aw, ca, cb, cc, cd)[r]
+            nc.sync.dma_start(out=given[:, r, 0:POINTS], in_=row.rearrange("o (g u) -> (o g) u", u=POINTS))
+        for c in (2, 0, 3, 1):
             nc.sync.dma_start(lists[c][:], lists_hbm[c])
         for t in range(1, PACK):
             load_plane(t)
         nc.sync.dma_start(out=wo_raw[:], in_=wo.rearrange("(p t) f -> p t f", t=PACK))
-        by_query = [keep.tile([P, POINTS], F32, name="by_query%d" % i) for i in range(2)]
-        for tile, row in zip(by_query, (cc, aw)):
-            nc.sync.dma_start(out=tile[:], in_=row.rearrange("o (g u) -> (o g) u", u=POINTS))
 
         ident = keep.tile([P, P], F32)
         make_identity(nc, ident[:])
 
-        nc.vector.memset(rows[0:ROW0, :], 0.0)
-        columns = bank(3, [P, P], "columns")
-        nc.tensor.transpose(columns[:], rows[:], ident[:])
-        attn = keep.tile([P, BLOCKS], F32)
-        nc.scalar.copy(out=attn[:], in_=columns[:, ROW0 : ROW0 + BLOCKS])
-        weight = keep.tile([P, BLOCKS, CORNERS], F32)
-        for q in range(BLOCKS):
-            nc.scalar.activation(
-                out=weight[:, q, :], in_=columns[:, ROW0 + BLOCKS + q : P : BLOCKS], func=COPY, scale=attn[:, q : q + 1]
-            )
+        weight = keep.tile([P, CORNERS, POINTS], F32)
+        nc.vector.tensor_tensor(weight[:, 0, :], given[:, 1, 0:POINTS], given[:, 0, 0:POINTS], MULT)
+        nc.vector.tensor_tensor(
+            weight[:, 1:, :], given[:, 2:, 0:POINTS], given[:, 0:1, 0:POINTS].to_broadcast([P, CORNERS - 1, POINTS]), MULT
+        )
 
-        spread = []
-        for c, i in enumerate((5, 6, 7, 1)):
-            spread_bank = bank(i, [P, BLOCKS, P], "spread_bank")
-            for q in range(BLOCKS):
-                nc.tensor.transpose(spread_bank[:, q, :], weight[:, q, c : c + 1].to_broadcast([P, P]), ident[:])
-            spread.append(keep.tile([P, J], F32, name="spread%d" % c))
-            nc.scalar.copy(out=spread[c][:], in_=spread_bank[:].rearrange("p q m -> p (q m)"))
-
-        sums = [bank(i, [P, 2, G], "sums") for i in range(2)]
-        picks = [keep.tile([P, J], F32, name="pick", tag="pick%d" % i, align_bytes=64) for i in range(STEPS - 2)]
-        picks = [pick[:] for pick in picks]
         halves = [slice(h * G // 2, (h + 1) * G // 2) for h in range(2)]
-        direct = [keep.tile([P, 2, G // 2], F32, name="direct", tag="direct%d" % h, align_bytes=64) for h in range(2)]
-        for h in range(2):
-            nc.vector.memset(direct[h][:, 0, :], 0.0)
+        direct = [keep.tile([P, PACK, G // 2], F32, name="direct%d" % h, align_bytes=64) for h in range(2)]
+        nc.vector.memset(direct[0][:, 0 : PACK - 1, :], 0.0)
+        nc.scalar.activation(direct[1][:, 0 : PACK - 1, :], direct[0][:, 0 : PACK - 1, :], COPY)
 
-        samples = bank(2, [P, BLOCKS, P], "samples")
-        for c in range(CORNERS):
-            picked = picks[c]
-            nc.vector.tensor_copy(picked, planes[0][:].indirect(lists[c][:]))
-            turned = bank((3, 5, 6, 3)[c], [P, BLOCKS, P], "turned")
-            scaled = keep.tile([P, BLOCKS, P], F32, name="scaled", tag="scaled%d" % c, align_bytes=64)
-            for q in range(BLOCKS):
-                nc.tensor.transpose(turned[:, q, :], picked[:, q * P : (q + 1) * P], ident[:])
-            for q in range(BLOCKS):
-                nc.scalar.activation(out=scaled[:, q, :], in_=turned[:, q, :], func=COPY, scale=weight[:, q, c : c + 1])
-            for q in range(BLOCKS):
+        spread_psum = {}
+        for c in (0, 2, 1, 3):
+            spread_bank = bank(c, [P, POINTS, G], "spread_bank")
+            for u in range(POINTS):
+                nc.tensor.transpose(spread_bank[:, u, :], weight[:, c, u : u + 1].to_broadcast([P, P]), ident[:])
+            spread_psum[c] = spread_bank[:].rearrange("p u g -> p g u")
+        spread = [keep.tile([P, J], F32, name="spread%d" % c) for c in range(2)]
+
+        def by_point(ap):
+            return ap.rearrange("p (g u) -> p g u", u=POINTS)
+
+        sums = bank(4, [P, PACK, G], "sums")
+        added = {}
+        done = {t: 0 for t in range(PACK)}
+        picked = {}
+
+        def turn(t, product):
+            terms = CORNERS - 1 if t == PACK - 1 else CORNERS
+            if t not in added:
+                added[t] = bank((0, 5, 6, 7)[t], [P, P], "added")
+            for u in range(POINTS):
                 nc.tensor.matmul(
-                    samples[:, q, :], scaled[:, q, :], ident[:], is_transpose=True,
-                    start=(c, q) == (0, 0), stop=(c, q) == (CORNERS - 1, BLOCKS - 1),
+                    added[t][:], product[:, u:J:POINTS], ident[:], is_transpose=True,
+                    start=(done[t], u) == (0, 0), stop=(done[t], u) == (terms - 1, POINTS - 1),
                 )
-        dealt = keep.tile([P, POINTS, G], F32)
-        nc.scalar.copy(out=dealt[:], in_=samples[:].rearrange("p q m -> p (q m)").rearrange("p (g u) -> p u g", u=POINTS))
+            done[t] = done[t] + 1
+
+        def close(t, copy):
+            added_sb = keep.tile([P, P], F32, name="added_sb%d" % t)
+            copy(out=added_sb[:], in_=added[t][:])
+            nc.tensor.transpose(sums[:, t, :], added_sb[:], ident[:])
+
+        def pick(t, c):
+            picked[t, c] = keep.tile([P, J], F32, name="picked", tag="ring%d" % (len(picked) % RING), align_bytes=64)
+            nc.scalar.activation(picked[t, c][:], planes[t][:].indirect(lists[c][:]), COPY)
+
+        def weigh(t, c):
+            product = keep.tile([P, J], F32, name="product%d%d" % (t, c))
+            nc.vector.tensor_tensor(by_point(product[:]), by_point(picked[t, c][:]), spread_psum[c], MULT)
+            turn(t, product)
+
+        def fused(t, c):
+            product = keep.tile([P, J], F32, name="product%d%d" % (t, c))
+            nc.vector.tensor_tensor(product[:], planes[t][:].indirect(lists[c][:]), spread[c][:], MULT)
+            turn(t, product)
+
+        nc.vector.tensor_copy(out=by_point(spread[0][:]), in_=spread_psum[0])
+        for t in range(PACK - 1):
+            pick(t, 2)
+            fused(t, 0)
+            if t == 0:
+                nc.scalar.copy(out=by_point(spread[1][:]), in_=spread_psum[1])
+            else:
+                close(t - 1, nc.scalar.copy)
+            pick(t, 3)
+            weigh(t, 2)
+            fused(t, 1)
+            weigh(t, 3)
+        pick(3, 2)
+        weigh(3, 2)
+        pick(3, 3)
+        close(2, nc.scalar.copy)
+        fused(3, 0)
+        weigh(3, 3)
 
         wo_dealt = wo_raw[:].rearrange("p k (m t) -> p m t k", t=PACK)
-        wo_bf = keep.tile([P, PACK, P, PACK], BF16, tag="scaled2", align_bytes=64)
+        wo_bf = keep.tile([P, PACK, P, PACK], BF16, tag="ring%d" % (len(picked) % RING), align_bytes=64)
         wo_into = wo_bf[:].rearrange("p t m k -> p m t k")
         piece = P // WO_PIECES
-        b_bf = [keep.tile([P, G // 2, PACK], BF16, name="b_bf", tag="b_bf%d" % h, align_bytes=64) for h in range(2)]
-        for t in range(PACK):
-            added = bank((3, 6)[t % 2], [P, P], "added")
-            terms = [[dealt[:, u, :] for u in range(POINTS)]] if t == 0 else []
-            for c in range(CORNERS if t > 0 else 0):
-                step = CORNERS * t + c
-                if step >= STEPS - 2:
-                    picks.append(keep.tile([P, J], F32, name="pick", tag="pick%d" % (step - CORNERS), align_bytes=64)[:])
-                picked = picks[step]
-                i = step - CORNERS
-                if i < WO_PIECES:
-                    m = slice(i * piece, (i + 1) * piece)
-                    nc.scalar.copy(out=wo_into[:, m, :, :], in_=wo_dealt[:, m, :, :])
-                if step == STEPS - 2:
-                    nc.vector.tensor_copy(
-                        picked.bitcast(U32).rearrange("p (u g) -> p g u", u=POINTS),
-                        planes[t][:].bitcast(U32).indirect(lists[c][:]),
-                    )
-                    continue
-                parts = 2 if step == STEPS - 1 else 1
-                for h in range(parts):
-                    j = slice(h * J // parts, (h + 1) * J // parts)
-                    offsets = lists[c][:, j.start // 16 : j.stop // 16]
-                    nc.vector.tensor_tensor(picked[:, j], planes[t][:].indirect(offsets), spread[c][:, j], MULT)
-                if step < STEPS - DIRECT:
-                    terms.append([picked[:, u:J:POINTS] for u in range(POINTS)])
-            for n, blocks in enumerate(terms):
-                for u in range(POINTS):
-                    nc.tensor.matmul(
-                        added[:], blocks[u], ident[:], is_transpose=True,
-                        start=(n, u) == (0, 0), stop=(n, u) == (len(terms) - 1, POINTS - 1),
-                    )
-            added_sb = keep.tile([P, P], F32, name="added_sb%d" % t)
-            nc.scalar.copy(out=added_sb[:], in_=added[:])
-            nc.tensor.matmul(
-                sums[t // 2][:, t % 2, :], added_sb[:], ident[:], is_transpose=True, start=(t % 2 == 0), stop=(t == 1)
-            )
-            if t == 1:
-                for h, g in enumerate(halves):
-                    nc.scalar.copy(out=b_bf[h][:, :, 0:2], in_=sums[0][:].rearrange("p t g -> p g t")[:, g, :])
+        for i in range(WO_PIECES):
+            m = slice(i * piece, (i + 1) * piece)
+            nc.scalar.copy(out=wo_into[:, m, :, :], in_=wo_dealt[:, m, :, :])
 
-        late_weight = keep.tile([P, POINTS], F32, tag="scaled3", align_bytes=64)
-        for u in range(POINTS):
-            nc.scalar.activation(
-                out=late_weight[:, u : u + 1], in_=by_query[0][:, u : u + 1], func=COPY, scale=by_query[1][:, u : u + 1]
-            )
-        picked = picks[STEPS - 2]
-        scaled = keep.tile([P, POINTS, P], F32, name="late_scaled")
-        turned = [bank(i, [P, P], "late_turned") for i in (2, 7, 4, 5)]
-        for u in range(POINTS):
-            nc.tensor.transpose(turned[u][:], picked[:, u * G : (u + 1) * G], ident[:])
-        for u in range(POINTS):
-            nc.scalar.activation(out=scaled[:, u, :], in_=turned[u][:], func=COPY, scale=late_weight[:, u : u + 1])
-        for u in range(POINTS):
-            nc.tensor.matmul(
-                sums[1][:, 1, :], scaled[:, u, :], ident[:], is_transpose=True, start=False, stop=(u == POINTS - 1)
-            )
+        last = keep.tile([P, J], F32)
+        for h in range(2):
+            j = slice(h * J // 2, (h + 1) * J // 2)
+            offsets = lists[1][:, j.start // 16 : j.stop // 16]
+            nc.vector.tensor_tensor(last[:, j], planes[PACK - 1][:].indirect(offsets), spread[1][:, j], MULT)
+        close(PACK - 1, nc.scalar.copy)
 
         wo_scales = keep.tile([P, F], U8, align_bytes=64)
+        wo_codes = keep.tile([P, F], U32, align_bytes=64)
 
-        def quantize_wo(codes, first, last):
+        def quantize_wo(t):
+            cols = slice(t * P, (t + 1) * P)
             nc.vector.quantize_mx(
-                out=codes.bitcast(FP8X4),
-                scales=wo_scales[:, first * P : last * P],
-                in_=wo_bf[:, first:last, :, :].rearrange("p t m k -> p (t m k)"),
+                out=wo_codes[:, cols].bitcast(FP8X4),
+                scales=wo_scales[:, cols],
+                in_=wo_bf[:, t, :, :].rearrange("p m k -> p (m k)"),
             )
 
+        b_bf = [keep.tile([P, G // 2, PACK], BF16, name="b_bf%d" % h, align_bytes=64) for h in range(2)]
         for h, g in enumerate(halves):
-            nc.vector.tensor_reduce(
-                direct[h][:, 1, :], picks[STEPS - 1].rearrange("p (g u) -> p g u", u=POINTS)[:, g, :],
-                mybir.AxisListType.X, ADD,
-            )
+            nc.vector.tensor_reduce(direct[h][:, PACK - 1, :], by_point(last[:])[:, g, :], mybir.AxisListType.X, ADD)
+        quantize_wo(0)
         for h, g in enumerate(halves):
             nc.vector.tensor_tensor(
-                b_bf[h][:, :, 2:4], sums[1][:].rearrange("p t g -> p g t")[:, g, :],
-                direct[h][:].rearrange("p t g -> p g t"), ADD,
+                b_bf[h][:], sums[:].rearrange("p t g -> p g t")[:, g, :], direct[h][:].rearrange("p t g -> p g t"), ADD
             )
         b_codes = keep.tile([P, G], U32, align_bytes=64)
         b_scales = keep.tile([P, G], U8, align_bytes=64)
-        wo_first = keep.tile([P, P], U32, tag="direct0", align_bytes=64)
         for h, g in enumerate(halves):
-            if h == 1:
-                quantize_wo(wo_first[:], 0, 1)
             nc.vector.quantize_mx(
                 out=b_codes[:, g].bitcast(FP8X4), scales=b_scales[:, g], in_=b_bf[h][:].rearrange("p g t -> p (g t)")
             )
-        wo_rest = keep.tile([P, F - P], U32, tag="b_bf0", align_bytes=64)
-        wo_codes = [wo_first[:]] + [wo_rest[:, t * P : (t + 1) * P] for t in range(PACK - 1)]
         for t in range(1, PACK):
-            quantize_wo(wo_codes[t], t, t + 1)
+            quantize_wo(t)
 
         y = keep.tile([P, PACK, G], F32)
         y_bf = keep.tile([P, G, PACK], BF16, align_bytes=64)
         out_planes = out_0.rearrange("(p t) g -> p t g", t=PACK)
         for h in range(2):
             two = slice(2 * h, 2 * h + 2)
-            y_bank = bank(4 + h, [P, 2, G], "y_bank")
+            y_bank = bank(5 + h, [P, 2, G], "y_bank")
             for u in range(2):
                 cols = slice((2 * h + u) * P, (2 * h + u + 1) * P)
                 nc.tensor.matmul_mx(
                     out=y_bank[:, u, :],
-                    lhsT=wo_codes[2 * h + u].bitcast(FP8X4),
+                    lhsT=wo_codes[:, cols].bitcast(FP8X4),
                     lhsT_scale=wo_scales[:, cols],
                     rhs=b_codes[:].bitcast(FP8X4),
                     rhs_scale=b_scales[:],

@@ -22,8 +22,8 @@ PACK = 4
 CORNERS = 4
 POINTS = 4
 ROW_PITCH = 8
-WO_PIECES = 4
 RING = 3
+PRODUCTS = 5
 
 
 def tile_attend_deformable_pl_kernel(tc, vals, ca, cb, cc, cd, aw, wo, offs, offs2, offs3, offs4, out_0, out_1, out_2):
@@ -36,7 +36,7 @@ def tile_attend_deformable_pl_kernel(tc, vals, ca, cb, cc, cd, aw, wo, offs, off
 
         planes = [keep.tile([P, T], F32, name="plane%d" % t) for t in range(PACK)]
         lists = [keep.tile([P, J // 16], U16, name="list%d" % c) for c in range(CORNERS)]
-        given = keep.tile([P, CORNERS + 1, ROW_PITCH], F32)
+        given = keep.tile([P, CORNERS + 1, ROW_PITCH], F32, tag="product0", align_bytes=64)
         wo_raw = keep.tile([P, PACK, F], F32)
         vals_planes = vals.rearrange("(p t) c -> p t c", t=PACK)
 
@@ -46,53 +46,73 @@ def tile_attend_deformable_pl_kernel(tc, vals, ca, cb, cc, cd, aw, wo, offs, off
         def load_plane(t):
             nc.sync.dma_start(out=planes[t][:], in_=vals_planes[:, t, :])
 
-        load_plane(0)
-        for r in (0, 1, 3, 2, 4):
+        def load_row(r):
             row = (aw, ca, cb, cc, cd)[r]
             nc.sync.dma_start(out=given[:, r, 0:POINTS], in_=row.rearrange("o (g u) -> (o g) u", u=POINTS))
-        for c in (2, 0, 3, 1):
+
+        def load_list(c):
             nc.sync.dma_start(lists[c][:], lists_hbm[c])
-        for t in range(1, PACK):
-            load_plane(t)
+
+        load_row(0)
+        load_row(1)
+        load_plane(0)
+        load_list(2)
+        load_list(0)
+        for r in (3, 4, 2):
+            load_row(r)
+        load_list(3)
+        load_plane(1)
+        load_list(1)
+        load_plane(2)
         nc.sync.dma_start(out=wo_raw[:], in_=wo.rearrange("(p t) f -> p t f", t=PACK))
+        load_plane(3)
 
         ident = keep.tile([P, P], F32)
         make_identity(nc, ident[:])
 
-        weight = keep.tile([P, CORNERS, POINTS], F32)
+        weight = keep.tile([P, CORNERS, POINTS], F32, tag="ring2", align_bytes=64)
         nc.vector.tensor_tensor(weight[:, 0, :], given[:, 1, 0:POINTS], given[:, 0, 0:POINTS], MULT)
         nc.vector.tensor_tensor(
             weight[:, 1:, :], given[:, 2:, 0:POINTS], given[:, 0:1, 0:POINTS].to_broadcast([P, CORNERS - 1, POINTS]), MULT
         )
 
         halves = [slice(h * G // 2, (h + 1) * G // 2) for h in range(2)]
-        direct = [keep.tile([P, PACK, G // 2], F32, name="direct%d" % h, align_bytes=64) for h in range(2)]
-        nc.vector.memset(direct[0][:, 0 : PACK - 1, :], 0.0)
-        nc.scalar.activation(direct[1][:, 0 : PACK - 1, :], direct[0][:, 0 : PACK - 1, :], COPY)
+        direct = [keep.tile([P, 2, G // 2], F32, name="direct", tag="direct%d" % h, align_bytes=64) for h in range(2)]
+        nc.vector.memset(direct[0][:, 0, :], 0.0)
+        nc.scalar.activation(direct[1][:, 0, :], direct[0][:, 0, :], COPY)
 
         spread_psum = {}
-        for c in (0, 2, 1, 3):
+        spread_dealt = {}
+        for c in (0, 2, 3, 1):
             spread_bank = bank(c, [P, POINTS, G], "spread_bank")
             for u in range(POINTS):
                 nc.tensor.transpose(spread_bank[:, u, :], weight[:, c, u : u + 1].to_broadcast([P, P]), ident[:])
             spread_psum[c] = spread_bank[:].rearrange("p u g -> p g u")
+            spread_dealt[c] = spread_bank[:].rearrange("p u (b i) -> p b u i", i=2)
         spread = [keep.tile([P, J], F32, name="spread%d" % c) for c in range(2)]
 
         def by_point(ap):
             return ap.rearrange("p (g u) -> p g u", u=POINTS)
 
-        sums = bank(4, [P, PACK, G], "sums")
+        sums = {}
+        b_bf = [keep.tile([P, G // 2, PACK], BF16, name="b_bf", tag="b_bf%d" % h, align_bytes=64) for h in range(2)]
         added = {}
         done = {t: 0 for t in range(PACK)}
         picked = {}
 
-        def turn(t, product):
+        products = []
+
+        def next_product():
+            products.append(keep.tile([P, J], F32, name="product", tag="product%d" % (len(products) % PRODUCTS), align_bytes=64))
+            return products[-1]
+
+        def turn(t, blocks):
             terms = CORNERS - 1 if t == PACK - 1 else CORNERS
             if t not in added:
                 added[t] = bank((0, 5, 6, 7)[t], [P, P], "added")
             for u in range(POINTS):
                 nc.tensor.matmul(
-                    added[t][:], product[:, u:J:POINTS], ident[:], is_transpose=True,
+                    added[t][:], blocks[u], ident[:], is_transpose=True,
                     start=(done[t], u) == (0, 0), stop=(done[t], u) == (terms - 1, POINTS - 1),
                 )
             done[t] = done[t] + 1
@@ -100,82 +120,109 @@ def tile_attend_deformable_pl_kernel(tc, vals, ca, cb, cc, cd, aw, wo, offs, off
         def close(t, copy):
             added_sb = keep.tile([P, P], F32, name="added_sb%d" % t)
             copy(out=added_sb[:], in_=added[t][:])
-            nc.tensor.transpose(sums[:, t, :], added_sb[:], ident[:])
+            if t % 2 == 0:
+                sums[t // 2] = bank((4, 0)[t // 2], [P, 2, G], "sums")
+            nc.tensor.transpose(sums[t // 2][:, t % 2, :], added_sb[:], ident[:])
 
         def pick(t, c):
             picked[t, c] = keep.tile([P, J], F32, name="picked", tag="ring%d" % (len(picked) % RING), align_bytes=64)
             nc.scalar.activation(picked[t, c][:], planes[t][:].indirect(lists[c][:]), COPY)
 
         def weigh(t, c):
-            product = keep.tile([P, J], F32, name="product%d%d" % (t, c))
-            nc.vector.tensor_tensor(by_point(product[:]), by_point(picked[t, c][:]), spread_psum[c], MULT)
-            turn(t, product)
+            product = next_product()
+            nc.vector.tensor_tensor(
+                product[:].rearrange("p (u b i) -> p b u i", u=POINTS, i=2),
+                picked[t, c][:].rearrange("p (b i u) -> p b u i", u=POINTS, i=2),
+                spread_dealt[c],
+                MULT,
+            )
+            turn(t, [product[:, u * G : (u + 1) * G] for u in range(POINTS)])
 
         def fused(t, c):
-            product = keep.tile([P, J], F32, name="product%d%d" % (t, c))
+            product = next_product()
             nc.vector.tensor_tensor(product[:], planes[t][:].indirect(lists[c][:]), spread[c][:], MULT)
-            turn(t, product)
+            turn(t, [product[:, u:J:POINTS] for u in range(POINTS)])
 
         nc.vector.tensor_copy(out=by_point(spread[0][:]), in_=spread_psum[0])
-        for t in range(PACK - 1):
-            pick(t, 2)
-            fused(t, 0)
-            if t == 0:
-                nc.scalar.copy(out=by_point(spread[1][:]), in_=spread_psum[1])
-            else:
-                close(t - 1, nc.scalar.copy)
-            pick(t, 3)
-            weigh(t, 2)
-            fused(t, 1)
-            weigh(t, 3)
+        pick(0, 2)
+        pick(0, 3)
+        fused(0, 0)
+        weigh(0, 2)
+        nc.scalar.copy(out=by_point(spread[1][:]), in_=spread_psum[1])
+        pick(1, 2)
+        weigh(0, 3)
+        fused(1, 0)
+        pick(1, 3)
+        weigh(1, 2)
+        pick(1, 1)
+        fused(0, 1)
+        weigh(1, 3)
+        close(0, nc.scalar.copy)
+        pick(2, 2)
+        fused(2, 0)
+        weigh(1, 1)
+        pick(2, 3)
+        weigh(2, 2)
+        close(1, nc.scalar.copy)
         pick(3, 2)
-        weigh(3, 2)
+        fused(2, 1)
+        weigh(2, 3)
         pick(3, 3)
+        weigh(3, 2)
         close(2, nc.scalar.copy)
         fused(3, 0)
         weigh(3, 3)
 
-        wo_dealt = wo_raw[:].rearrange("p k (m t) -> p m t k", t=PACK)
-        wo_bf = keep.tile([P, PACK, P, PACK], BF16, tag="ring%d" % (len(picked) % RING), align_bytes=64)
-        wo_into = wo_bf[:].rearrange("p t m k -> p m t k")
-        piece = P // WO_PIECES
-        for i in range(WO_PIECES):
-            m = slice(i * piece, (i + 1) * piece)
-            nc.scalar.copy(out=wo_into[:, m, :, :], in_=wo_dealt[:, m, :, :])
+        wo_dealt = wo_raw[:].rearrange("p k (m t) -> p m k t", t=PACK)
+        wo_bf = []
 
-        last = keep.tile([P, J], F32)
+        def round_wo(tile):
+            two = slice(2 * len(wo_bf), 2 * len(wo_bf) + 2)
+            wo_bf.append(tile)
+            nc.scalar.copy(out=tile[:].rearrange("p t m k -> p m k t"), in_=wo_dealt[:, :, :, two])
+
+        round_wo(keep.tile([P, 2, P, PACK], BF16, name="wo_bf0", tag="ring%d" % ((len(picked) - 2) % RING), align_bytes=64))
+        for h, g in enumerate(halves):
+            nc.scalar.copy(out=b_bf[h][:, :, 0:2], in_=sums[0][:].rearrange("p t g -> p g t")[:, g, :])
+        freed_by_last_turn = "product%d" % ((len(products) - 1) % PRODUCTS)
+
+        last = next_product()
         for h in range(2):
             j = slice(h * J // 2, (h + 1) * J // 2)
             offsets = lists[1][:, j.start // 16 : j.stop // 16]
             nc.vector.tensor_tensor(last[:, j], planes[PACK - 1][:].indirect(offsets), spread[1][:, j], MULT)
         close(PACK - 1, nc.scalar.copy)
+        round_wo(keep.tile([P, 2, P, PACK], BF16, name="wo_bf1", tag=freed_by_last_turn, align_bytes=64))
 
         wo_scales = keep.tile([P, F], U8, align_bytes=64)
-        wo_codes = keep.tile([P, F], U32, align_bytes=64)
 
         def quantize_wo(t):
-            cols = slice(t * P, (t + 1) * P)
             nc.vector.quantize_mx(
-                out=wo_codes[:, cols].bitcast(FP8X4),
-                scales=wo_scales[:, cols],
-                in_=wo_bf[:, t, :, :].rearrange("p m k -> p (m k)"),
+                out=wo_codes[t].bitcast(FP8X4),
+                scales=wo_scales[:, t * P : (t + 1) * P],
+                in_=wo_bf[t // 2][:, t % 2, :, :].rearrange("p m k -> p (m k)"),
             )
 
-        b_bf = [keep.tile([P, G // 2, PACK], BF16, name="b_bf%d" % h, align_bytes=64) for h in range(2)]
         for h, g in enumerate(halves):
-            nc.vector.tensor_reduce(direct[h][:, PACK - 1, :], by_point(last[:])[:, g, :], mybir.AxisListType.X, ADD)
-        quantize_wo(0)
+            nc.vector.tensor_reduce(direct[h][:, 1, :], by_point(last[:])[:, g, :], mybir.AxisListType.X, ADD)
         for h, g in enumerate(halves):
             nc.vector.tensor_tensor(
-                b_bf[h][:], sums[:].rearrange("p t g -> p g t")[:, g, :], direct[h][:].rearrange("p t g -> p g t"), ADD
+                b_bf[h][:, :, 2:4], sums[1][:].rearrange("p t g -> p g t")[:, g, :],
+                direct[h][:].rearrange("p t g -> p g t"), ADD,
             )
         b_codes = keep.tile([P, G], U32, align_bytes=64)
         b_scales = keep.tile([P, G], U8, align_bytes=64)
+        wo_first = keep.tile([P, P], U32, tag="direct0", align_bytes=64)
+        wo_codes = [wo_first[:]]
         for h, g in enumerate(halves):
+            if h == 1:
+                quantize_wo(0)
             nc.vector.quantize_mx(
                 out=b_codes[:, g].bitcast(FP8X4), scales=b_scales[:, g], in_=b_bf[h][:].rearrange("p g t -> p (g t)")
             )
+        wo_rest = keep.tile([P, F - P], U32, tag="b_bf0", align_bytes=64)
         for t in range(1, PACK):
+            wo_codes.append(wo_rest[:, (t - 1) * P : t * P])
             quantize_wo(t)
 
         y = keep.tile([P, PACK, G], F32)
@@ -183,12 +230,12 @@ def tile_attend_deformable_pl_kernel(tc, vals, ca, cb, cc, cd, aw, wo, offs, off
         out_planes = out_0.rearrange("(p t) g -> p t g", t=PACK)
         for h in range(2):
             two = slice(2 * h, 2 * h + 2)
-            y_bank = bank(5 + h, [P, 2, G], "y_bank")
+            y_bank = bank(1 + h, [P, 2, G], "y_bank")
             for u in range(2):
                 cols = slice((2 * h + u) * P, (2 * h + u + 1) * P)
                 nc.tensor.matmul_mx(
                     out=y_bank[:, u, :],
-                    lhsT=wo_codes[:, cols].bitcast(FP8X4),
+                    lhsT=wo_codes[2 * h + u].bitcast(FP8X4),
                     lhsT_scale=wo_scales[:, cols],
                     rhs=b_codes[:].bitcast(FP8X4),
                     rhs_scale=b_scales[:],

@@ -37,7 +37,7 @@ def tile_attend_deformable_pl_kernel(tc, vals, ca, cb, cc, cd, aw, wo, offs, off
         planes = [keep.tile([P, T], F32, name="plane%d" % t) for t in range(PACK)]
         lists = [keep.tile([P, J // 16], U16, name="list%d" % c) for c in range(CORNERS)]
         given = keep.tile([P, CORNERS + 1, ROW_PITCH], F32, tag="product0", align_bytes=64)
-        wo_raw = keep.tile([P, PACK, F], F32)
+        wo_raw = [keep.tile([P, PACK, F // 2], F32, name="wo_raw", tag="wo_raw%d" % h, align_bytes=64) for h in range(2)]
         vals_planes = vals.rearrange("(p t) c -> p t c", t=PACK)
 
         def bank(i, shape, name):
@@ -64,8 +64,10 @@ def tile_attend_deformable_pl_kernel(tc, vals, ca, cb, cc, cd, aw, wo, offs, off
         load_plane(1)
         load_list(1)
         load_plane(2)
-        nc.sync.dma_start(out=wo_raw[:], in_=wo.rearrange("(p t) f -> p t f", t=PACK))
         load_plane(3)
+        for h in range(2):
+            f = slice(h * F // 2, (h + 1) * F // 2)
+            nc.sync.dma_start(out=wo_raw[h][:], in_=wo.rearrange("(p t) f -> p t f", t=PACK)[:, :, f])
 
         ident = keep.tile([P, P], F32)
         make_identity(nc, ident[:])
@@ -117,12 +119,11 @@ def tile_attend_deformable_pl_kernel(tc, vals, ca, cb, cc, cd, aw, wo, offs, off
                 )
             done[t] = done[t] + 1
 
-        def close(t, copy):
-            added_sb = keep.tile([P, P], F32, name="added_sb%d" % t)
-            copy(out=added_sb[:], in_=added[t][:])
+        def close(t):
+            nc.scalar.copy(out=added_sb[:, t, :], in_=added[t][:])
             if t % 2 == 0:
                 sums[t // 2] = bank((4, 0)[t // 2], [P, 2, G], "sums")
-            nc.tensor.transpose(sums[t // 2][:, t % 2, :], added_sb[:], ident[:])
+            nc.tensor.transpose(sums[t // 2][:, t % 2, :], added_sb[:, t, :], ident[:])
 
         def pick(t, c):
             picked[t, c] = keep.tile([P, J], F32, name="picked", tag="ring%d" % (len(picked) % RING), align_bytes=64)
@@ -138,8 +139,8 @@ def tile_attend_deformable_pl_kernel(tc, vals, ca, cb, cc, cd, aw, wo, offs, off
             )
             turn(t, [product[:, u * G : (u + 1) * G] for u in range(POINTS)])
 
-        def fused(t, c):
-            product = next_product()
+        def fused(t, c, product=None):
+            product = product or next_product()
             nc.vector.tensor_tensor(product[:], planes[t][:].indirect(lists[c][:]), spread[c][:], MULT)
             turn(t, [product[:, u:J:POINTS] for u in range(POINTS)])
 
@@ -154,45 +155,48 @@ def tile_attend_deformable_pl_kernel(tc, vals, ca, cb, cc, cd, aw, wo, offs, off
         fused(1, 0)
         pick(1, 3)
         weigh(1, 2)
-        pick(1, 1)
+        extra = keep.tile([P, J], F32)
+        nc.scalar.activation(extra[:], planes[1][:].indirect(lists[1][:]), COPY)
         fused(0, 1)
         weigh(1, 3)
-        close(0, nc.scalar.copy)
         pick(2, 2)
-        fused(2, 0)
-        weigh(1, 1)
+        fused(2, 0, keep.tile([P, J], F32, name="product", tag="handed_on"))
         pick(2, 3)
-        weigh(2, 2)
-        close(1, nc.scalar.copy)
-        pick(3, 2)
         fused(2, 1)
+        extra_product = keep.tile([P, J], F32, tag="handed_on")
+        nc.gpsimd.tensor_tensor(extra_product[:], extra[:], spread[1][:], MULT)
+        weigh(2, 2)
+        pick(3, 2)
         weigh(2, 3)
+        turn(1, [extra_product[:, u:J:POINTS] for u in range(POINTS)])
         pick(3, 3)
-        weigh(3, 2)
-        close(2, nc.scalar.copy)
         fused(3, 0)
+        weigh(3, 2)
         weigh(3, 3)
 
-        wo_dealt = wo_raw[:].rearrange("p k (m t) -> p m k t", t=PACK)
-        wo_bf = []
+        wo_bf = keep.tile([P, PACK, P, PACK], BF16, align_bytes=64)
 
-        def round_wo(tile):
-            two = slice(2 * len(wo_bf), 2 * len(wo_bf) + 2)
-            wo_bf.append(tile)
-            nc.scalar.copy(out=tile[:].rearrange("p t m k -> p m k t"), in_=wo_dealt[:, :, :, two])
+        def round_wo(h):
+            m = slice(h * P // 2, (h + 1) * P // 2)
+            nc.scalar.copy(
+                out=wo_bf[:].rearrange("p t m k -> p m t k")[:, m, :, :],
+                in_=wo_raw[h][:].rearrange("p k (m t) -> p m t k", t=PACK),
+            )
 
-        round_wo(keep.tile([P, 2, P, PACK], BF16, name="wo_bf0", tag="ring%d" % ((len(picked) - 2) % RING), align_bytes=64))
+        round_wo(0)
+        added_sb = keep.tile([P, PACK, P], F32, tag="wo_raw0", align_bytes=64)
+        for t in range(PACK - 1):
+            close(t)
         for h, g in enumerate(halves):
             nc.scalar.copy(out=b_bf[h][:, :, 0:2], in_=sums[0][:].rearrange("p t g -> p g t")[:, g, :])
-        freed_by_last_turn = "product%d" % ((len(products) - 1) % PRODUCTS)
 
         last = next_product()
         for h in range(2):
             j = slice(h * J // 2, (h + 1) * J // 2)
             offsets = lists[1][:, j.start // 16 : j.stop // 16]
             nc.vector.tensor_tensor(last[:, j], planes[PACK - 1][:].indirect(offsets), spread[1][:, j], MULT)
-        close(PACK - 1, nc.scalar.copy)
-        round_wo(keep.tile([P, 2, P, PACK], BF16, name="wo_bf1", tag=freed_by_last_turn, align_bytes=64))
+        close(PACK - 1)
+        round_wo(1)
 
         wo_scales = keep.tile([P, F], U8, align_bytes=64)
 
@@ -200,7 +204,7 @@ def tile_attend_deformable_pl_kernel(tc, vals, ca, cb, cc, cd, aw, wo, offs, off
             nc.vector.quantize_mx(
                 out=wo_codes[t].bitcast(FP8X4),
                 scales=wo_scales[:, t * P : (t + 1) * P],
-                in_=wo_bf[t // 2][:, t % 2, :, :].rearrange("p m k -> p (m k)"),
+                in_=wo_bf[:, t, :, :].rearrange("p m k -> p (m k)"),
             )
 
         for h, g in enumerate(halves):

@@ -22,8 +22,7 @@ PACK = 4
 CORNERS = 4
 POINTS = 4
 ROW_PITCH = 8
-RING = 3
-PRODUCTS = 5
+PRODUCTS = 4
 
 
 def tile_attend_deformable_pl_kernel(tc, vals, ca, cb, cc, cd, aw, wo, offs, offs2, offs3, offs4, out_0, out_1, out_2):
@@ -34,7 +33,7 @@ def tile_attend_deformable_pl_kernel(tc, vals, ca, cb, cc, cd, aw, wo, offs, off
         keep = ctx.enter_context(tc.tile_pool(name="keep", bufs=1))
         psum = ctx.enter_context(tc.psum_pool(name="psum", bufs=1))
 
-        planes = [keep.tile([P, T], F32, name="plane%d" % t) for t in range(PACK)]
+        planes = [keep.tile([P, T], F32, name="plane", tag="plane%d" % t) for t in range(PACK)]
         lists = [keep.tile([P, J // 16], U16, name="list%d" % c) for c in range(CORNERS)]
         given = keep.tile([P, CORNERS + 1, ROW_PITCH], F32, tag="product0", align_bytes=64)
         wo_raw = [keep.tile([P, PACK, F // 2], F32, name="wo_raw", tag="wo_raw%d" % h, align_bytes=64) for h in range(2)]
@@ -58,10 +57,10 @@ def tile_attend_deformable_pl_kernel(tc, vals, ca, cb, cc, cd, aw, wo, offs, off
         load_plane(0)
         load_list(2)
         load_list(0)
-        for r in (3, 4, 2):
+        for r in (2, 3, 4):
             load_row(r)
-        load_list(3)
         load_plane(1)
+        load_list(3)
         load_list(1)
         load_plane(2)
         load_plane(3)
@@ -72,11 +71,10 @@ def tile_attend_deformable_pl_kernel(tc, vals, ca, cb, cc, cd, aw, wo, offs, off
         ident = keep.tile([P, P], F32)
         make_identity(nc, ident[:])
 
-        weight = keep.tile([P, CORNERS, POINTS], F32, tag="ring2", align_bytes=64)
-        nc.vector.tensor_tensor(weight[:, 0, :], given[:, 1, 0:POINTS], given[:, 0, 0:POINTS], MULT)
-        nc.vector.tensor_tensor(
-            weight[:, 1:, :], given[:, 2:, 0:POINTS], given[:, 0:1, 0:POINTS].to_broadcast([P, CORNERS - 1, POINTS]), MULT
-        )
+        weight = []
+        for c in range(CORNERS):
+            weight.append(keep.tile([P, POINTS], F32, name="weight", tag="picked%d" % c, align_bytes=64))
+            nc.vector.tensor_tensor(weight[c][:], given[:, 1 + c, 0:POINTS], given[:, 0, 0:POINTS], MULT)
 
         halves = [slice(h * G // 2, (h + 1) * G // 2) for h in range(2)]
         direct = [keep.tile([P, 2, G // 2], F32, name="direct", tag="direct%d" % h, align_bytes=64) for h in range(2)]
@@ -85,13 +83,13 @@ def tile_attend_deformable_pl_kernel(tc, vals, ca, cb, cc, cd, aw, wo, offs, off
 
         spread_psum = {}
         spread_dealt = {}
-        for c in (0, 2, 3, 1):
+        for c in range(CORNERS):
             spread_bank = bank(c, [P, POINTS, G], "spread_bank")
             for u in range(POINTS):
-                nc.tensor.transpose(spread_bank[:, u, :], weight[:, c, u : u + 1].to_broadcast([P, P]), ident[:])
+                nc.tensor.transpose(spread_bank[:, u, :], weight[c][:, u : u + 1].to_broadcast([P, P]), ident[:])
             spread_psum[c] = spread_bank[:].rearrange("p u g -> p g u")
             spread_dealt[c] = spread_bank[:].rearrange("p u (b i) -> p b u i", i=2)
-        spread = [keep.tile([P, J], F32, name="spread%d" % c) for c in range(2)]
+        spread = [keep.tile([P, J], F32, name="spread%d" % c) for c in range(3)]
 
         def by_point(ap):
             return ap.rearrange("p (g u) -> p g u", u=POINTS)
@@ -125,8 +123,8 @@ def tile_attend_deformable_pl_kernel(tc, vals, ca, cb, cc, cd, aw, wo, offs, off
                 sums[t // 2] = bank((4, 0)[t // 2], [P, 2, G], "sums")
             nc.tensor.transpose(sums[t // 2][:, t % 2, :], added_sb[:, t, :], ident[:])
 
-        def pick(t, c):
-            picked[t, c] = keep.tile([P, J], F32, name="picked", tag="ring%d" % (len(picked) % RING), align_bytes=64)
+        def pick(t, c, tag):
+            picked[t, c] = keep.tile([P, J], F32, name="picked", tag=tag, align_bytes=64)
             nc.scalar.activation(picked[t, c][:], planes[t][:].indirect(lists[c][:]), COPY)
 
         def weigh(t, c):
@@ -139,37 +137,43 @@ def tile_attend_deformable_pl_kernel(tc, vals, ca, cb, cc, cd, aw, wo, offs, off
             )
             turn(t, [product[:, u * G : (u + 1) * G] for u in range(POINTS)])
 
-        def fused(t, c, product=None):
-            product = product or next_product()
+        def pick_aside(t, c):
+            picked[t, c] = keep.tile([P, J], F32, name="aside%d" % t)
+            nc.scalar.activation(picked[t, c][:], planes[t][:].indirect(lists[c][:]), COPY)
+
+        def weigh_aside(t, c, tag):
+            product = keep.tile([P, J], F32, name="product", tag=tag)
+            nc.gpsimd.tensor_tensor(product[:], picked[t, c][:], spread[c][:], MULT)
+            turn(t, [product[:, u:J:POINTS] for u in range(POINTS)])
+
+        def fused(t, c):
+            product = next_product()
             nc.vector.tensor_tensor(product[:], planes[t][:].indirect(lists[c][:]), spread[c][:], MULT)
             turn(t, [product[:, u:J:POINTS] for u in range(POINTS)])
 
         nc.vector.tensor_copy(out=by_point(spread[0][:]), in_=spread_psum[0])
-        pick(0, 2)
-        pick(0, 3)
-        fused(0, 0)
-        weigh(0, 2)
+        pick_aside(0, 2)
         nc.scalar.copy(out=by_point(spread[1][:]), in_=spread_psum[1])
-        pick(1, 2)
-        weigh(0, 3)
+        fused(0, 0)
+        pick(0, 3, "picked1")
+        nc.scalar.copy(out=by_point(spread[2][:]), in_=spread_psum[2])
         fused(1, 0)
-        pick(1, 3)
-        weigh(1, 2)
-        extra = keep.tile([P, J], F32)
-        nc.scalar.activation(extra[:], planes[1][:].indirect(lists[1][:]), COPY)
+        pick(1, 2, "picked2")
         fused(0, 1)
-        weigh(1, 3)
-        pick(2, 2)
-        fused(2, 0, keep.tile([P, J], F32, name="product", tag="handed_on"))
-        pick(2, 3)
+        fused(2, 0)
+        pick(1, 3, "picked3")
+        weigh(0, 3)
+        weigh(1, 2)
+        weigh_aside(0, 2, "plane0")
+        pick_aside(2, 2)
+        fused(1, 1)
+        pick(2, 3, "picked1")
         fused(2, 1)
-        extra_product = keep.tile([P, J], F32, tag="handed_on")
-        nc.gpsimd.tensor_tensor(extra_product[:], extra[:], spread[1][:], MULT)
-        weigh(2, 2)
-        pick(3, 2)
+        pick(3, 2, "picked2")
+        weigh(1, 3)
         weigh(2, 3)
-        turn(1, [extra_product[:, u:J:POINTS] for u in range(POINTS)])
-        pick(3, 3)
+        weigh_aside(2, 2, "plane1")
+        pick(3, 3, "picked3")
         fused(3, 0)
         weigh(3, 2)
         weigh(3, 3)

@@ -35,7 +35,7 @@ def tile_attend_deformable_pl_kernel(tc, vals, ca, cb, cc, cd, aw, wo, offs, off
 
         planes = [keep.tile([P, T], F32, name="plane", tag="plane%d" % t) for t in range(PACK)]
         lists = [keep.tile([P, J // 16], U16, name="list%d" % c) for c in range(CORNERS)]
-        given = keep.tile([P, CORNERS + 1, ROW_PITCH], F32, tag="product0", align_bytes=64)
+        given = keep.tile([P, CORNERS + 1, ROW_PITCH], F32)
         wo_raw = [keep.tile([P, PACK, F // 2], F32, name="wo_raw", tag="wo_raw%d" % h, align_bytes=64) for h in range(2)]
         vals_planes = vals.rearrange("(p t) c -> p t c", t=PACK)
 
@@ -45,14 +45,14 @@ def tile_attend_deformable_pl_kernel(tc, vals, ca, cb, cc, cd, aw, wo, offs, off
         def load_plane(t):
             nc.sync.dma_start(out=planes[t][:], in_=vals_planes[:, t, :])
 
-        def load_row(r):
+        def load_row(r, queue=nc.sync):
             row = (aw, ca, cb, cc, cd)[r]
-            nc.sync.dma_start(out=given[:, r, 0:POINTS], in_=row.rearrange("o (g u) -> (o g) u", u=POINTS))
+            queue.dma_start(out=given[:, r, 0:POINTS], in_=row.rearrange("o (g u) -> (o g) u", u=POINTS))
 
         def load_list(c):
             nc.sync.dma_start(lists[c][:], lists_hbm[c])
 
-        load_row(0)
+        load_row(0, nc.scalar)
         load_row(1)
         load_plane(0)
         load_list(2)
@@ -74,7 +74,8 @@ def tile_attend_deformable_pl_kernel(tc, vals, ca, cb, cc, cd, aw, wo, offs, off
         weight = []
         for c in range(CORNERS):
             weight.append(keep.tile([P, POINTS], F32, name="weight", tag="picked%d" % c, align_bytes=64))
-            nc.vector.tensor_tensor(weight[c][:], given[:, 1 + c, 0:POINTS], given[:, 0, 0:POINTS], MULT)
+            engine = nc.vector if c == 0 else nc.gpsimd
+            engine.tensor_tensor(weight[c][:], given[:, 1 + c, 0:POINTS], given[:, 0, 0:POINTS], MULT)
 
         halves = [slice(h * G // 2, (h + 1) * G // 2) for h in range(2)]
         direct = [keep.tile([P, 2, G // 2], F32, name="direct", tag="direct%d" % h, align_bytes=64) for h in range(2)]
@@ -109,7 +110,7 @@ def tile_attend_deformable_pl_kernel(tc, vals, ca, cb, cc, cd, aw, wo, offs, off
         def turn(t, blocks):
             terms = CORNERS - 1 if t == PACK - 1 else CORNERS
             if t not in added:
-                added[t] = bank((0, 5, 6, 7)[t], [P, P], "added")
+                added[t] = bank((1, 5, 6, 7)[t], [P, P], "added")
             for u in range(POINTS):
                 nc.tensor.matmul(
                     added[t][:], blocks[u], ident[:], is_transpose=True,
@@ -138,7 +139,7 @@ def tile_attend_deformable_pl_kernel(tc, vals, ca, cb, cc, cd, aw, wo, offs, off
             turn(t, [product[:, u * G : (u + 1) * G] for u in range(POINTS)])
 
         def pick_aside(t, c):
-            picked[t, c] = keep.tile([P, J], F32, name="aside%d" % t)
+            picked[t, c] = keep.tile([P, J], F32, name="aside", tag="aside%d" % t, align_bytes=64)
             nc.scalar.activation(picked[t, c][:], planes[t][:].indirect(lists[c][:]), COPY)
 
         def weigh_aside(t, c, tag):
@@ -178,17 +179,11 @@ def tile_attend_deformable_pl_kernel(tc, vals, ca, cb, cc, cd, aw, wo, offs, off
         weigh(3, 2)
         weigh(3, 3)
 
-        wo_bf = keep.tile([P, PACK, P, PACK], BF16, align_bytes=64)
-
-        def round_wo(h):
-            m = slice(h * P // 2, (h + 1) * P // 2)
-            nc.scalar.copy(
-                out=wo_bf[:].rearrange("p t m k -> p m t k")[:, m, :, :],
-                in_=wo_raw[h][:].rearrange("p k (m t) -> p m t k", t=PACK),
-            )
-
-        round_wo(0)
-        added_sb = keep.tile([P, PACK, P], F32, tag="wo_raw0", align_bytes=64)
+        wo_bf = keep.tile([P, PACK, P, PACK], BF16, tag="picked1", align_bytes=64)
+        wo_into = [wo_bf[:].rearrange("p t m k -> p m t k")[:, h * P // 2 : (h + 1) * P // 2, :, :] for h in range(2)]
+        wo_from = [wo_raw[h][:].rearrange("p k (m t) -> p m t k", t=PACK) for h in range(2)]
+        nc.gpsimd.tensor_scalar(wo_into[0], wo_from[0], 1.0, 0.0, MULT, ADD)
+        added_sb = keep.tile([P, PACK, P], F32, tag="aside2", align_bytes=64)
         for t in range(PACK - 1):
             close(t)
         for h, g in enumerate(halves):
@@ -200,7 +195,7 @@ def tile_attend_deformable_pl_kernel(tc, vals, ca, cb, cc, cd, aw, wo, offs, off
             offsets = lists[1][:, j.start // 16 : j.stop // 16]
             nc.vector.tensor_tensor(last[:, j], planes[PACK - 1][:].indirect(offsets), spread[1][:, j], MULT)
         close(PACK - 1)
-        round_wo(1)
+        nc.scalar.copy(out=wo_into[1], in_=wo_from[1])
 
         wo_scales = keep.tile([P, F], U8, align_bytes=64)
 

@@ -23,6 +23,7 @@ CORNERS = 4
 POINTS = 4
 ROW_PITCH = 8
 PRODUCTS = 4
+WO_ASIDE = 52
 
 
 def tile_attend_deformable_pl_kernel(tc, vals, ca, cb, cc, cd, aw, wo, offs, offs2, offs3, offs4, out_0, out_1, out_2):
@@ -36,7 +37,8 @@ def tile_attend_deformable_pl_kernel(tc, vals, ca, cb, cc, cd, aw, wo, offs, off
         planes = [keep.tile([P, T], F32, name="plane", tag="plane%d" % t) for t in range(PACK)]
         lists = [keep.tile([P, J // 16], U16, name="list%d" % c) for c in range(CORNERS)]
         given = keep.tile([P, CORNERS + 1, ROW_PITCH], F32)
-        wo_raw = [keep.tile([P, PACK, F // 2], F32, name="wo_raw", tag="wo_raw%d" % h, align_bytes=64) for h in range(2)]
+        wo_parts = (slice(0, WO_ASIDE), slice(WO_ASIDE, P))
+        wo_raw = [keep.tile([P, PACK, PACK * (m.stop - m.start)], F32, name="wo_raw%d" % m.start) for m in wo_parts]
         vals_planes = vals.rearrange("(p t) c -> p t c", t=PACK)
 
         def bank(i, shape, name):
@@ -59,14 +61,14 @@ def tile_attend_deformable_pl_kernel(tc, vals, ca, cb, cc, cd, aw, wo, offs, off
         load_list(0)
         for r in (2, 3, 4):
             load_row(r)
-        load_plane(1)
         load_list(3)
+        load_plane(1)
         load_list(1)
         load_plane(2)
         load_plane(3)
-        for h in range(2):
-            f = slice(h * F // 2, (h + 1) * F // 2)
-            nc.sync.dma_start(out=wo_raw[h][:], in_=wo.rearrange("(p t) f -> p t f", t=PACK)[:, :, f])
+        for tile, m in zip(wo_raw, wo_parts):
+            f = slice(PACK * m.start, PACK * m.stop)
+            nc.sync.dma_start(out=tile[:], in_=wo.rearrange("(p t) f -> p t f", t=PACK)[:, :, f])
 
         ident = keep.tile([P, P], F32)
         make_identity(nc, ident[:])
@@ -147,15 +149,23 @@ def tile_attend_deformable_pl_kernel(tc, vals, ca, cb, cc, cd, aw, wo, offs, off
             nc.gpsimd.tensor_tensor(product[:], picked[t, c][:], spread[c][:], MULT)
             turn(t, [product[:, u:J:POINTS] for u in range(POINTS)])
 
-        def fused(t, c):
+        def gather_fused(t, c, parts):
             product = next_product()
-            nc.vector.tensor_tensor(product[:], planes[t][:].indirect(lists[c][:]), spread[c][:], MULT)
+            for h in range(parts):
+                j = slice(h * J // parts, (h + 1) * J // parts)
+                offsets = lists[c][:, j.start // 16 : j.stop // 16]
+                nc.vector.tensor_tensor(product[:, j], planes[t][:].indirect(offsets), spread[c][:, j], MULT)
+            return product
+
+        def fused(t, c, parts=1):
+            product = gather_fused(t, c, parts)
             turn(t, [product[:, u:J:POINTS] for u in range(POINTS)])
 
-        nc.vector.tensor_copy(out=by_point(spread[0][:]), in_=spread_psum[0])
+        for g in halves:
+            nc.vector.tensor_copy(out=by_point(spread[0][:])[:, g, :], in_=spread_psum[0][:, g, :])
         pick_aside(0, 2)
         nc.scalar.copy(out=by_point(spread[1][:]), in_=spread_psum[1])
-        fused(0, 0)
+        fused(0, 0, parts=2)
         pick(0, 3, "picked1")
         nc.scalar.copy(out=by_point(spread[2][:]), in_=spread_psum[2])
         fused(1, 0)
@@ -180,7 +190,7 @@ def tile_attend_deformable_pl_kernel(tc, vals, ca, cb, cc, cd, aw, wo, offs, off
         weigh(3, 3)
 
         wo_bf = keep.tile([P, PACK, P, PACK], BF16, tag="picked1", align_bytes=64)
-        wo_into = [wo_bf[:].rearrange("p t m k -> p m t k")[:, h * P // 2 : (h + 1) * P // 2, :, :] for h in range(2)]
+        wo_into = [wo_bf[:].rearrange("p t m k -> p m t k")[:, m, :, :] for m in wo_parts]
         wo_from = [wo_raw[h][:].rearrange("p k (m t) -> p m t k", t=PACK) for h in range(2)]
         nc.gpsimd.tensor_scalar(wo_into[0], wo_from[0], 1.0, 0.0, MULT, ADD)
         added_sb = keep.tile([P, PACK, P], F32, tag="aside2", align_bytes=64)
@@ -189,11 +199,7 @@ def tile_attend_deformable_pl_kernel(tc, vals, ca, cb, cc, cd, aw, wo, offs, off
         for h, g in enumerate(halves):
             nc.scalar.copy(out=b_bf[h][:, :, 0:2], in_=sums[0][:].rearrange("p t g -> p g t")[:, g, :])
 
-        last = next_product()
-        for h in range(2):
-            j = slice(h * J // 2, (h + 1) * J // 2)
-            offsets = lists[1][:, j.start // 16 : j.stop // 16]
-            nc.vector.tensor_tensor(last[:, j], planes[PACK - 1][:].indirect(offsets), spread[1][:, j], MULT)
+        last = gather_fused(PACK - 1, 1, 2)
         close(PACK - 1)
         nc.scalar.copy(out=wo_into[1], in_=wo_from[1])
 

@@ -23,7 +23,7 @@ CORNERS = 4
 POINTS = 4
 ROW_PITCH = 8
 PRODUCTS = 4
-WO_ASIDE = 52
+WO_ASIDE = 64
 
 
 def tile_attend_deformable_pl_kernel(tc, vals, ca, cb, cc, cd, aw, wo, offs, offs2, offs3, offs4, out_0, out_1, out_2):
@@ -61,8 +61,8 @@ def tile_attend_deformable_pl_kernel(tc, vals, ca, cb, cc, cd, aw, wo, offs, off
         load_list(0)
         for r in (2, 3, 4):
             load_row(r)
-        load_list(3)
         load_plane(1)
+        load_list(3)
         load_list(1)
         load_plane(2)
         load_plane(3)
@@ -76,8 +76,7 @@ def tile_attend_deformable_pl_kernel(tc, vals, ca, cb, cc, cd, aw, wo, offs, off
         weight = []
         for c in range(CORNERS):
             weight.append(keep.tile([P, POINTS], F32, name="weight", tag="picked%d" % c, align_bytes=64))
-            engine = nc.vector if c == 0 else nc.gpsimd
-            engine.tensor_tensor(weight[c][:], given[:, 1 + c, 0:POINTS], given[:, 0, 0:POINTS], MULT)
+            nc.vector.tensor_tensor(weight[c][:], given[:, 1 + c, 0:POINTS], given[:, 0, 0:POINTS], MULT)
 
         halves = [slice(h * G // 2, (h + 1) * G // 2) for h in range(2)]
         direct = [keep.tile([P, 2, G // 2], F32, name="direct", tag="direct%d" % h, align_bytes=64) for h in range(2)]

from contextlib import ExitStack

import concourse.mybir as mybir
from concourse.masks import make_identity

E, T, J, G, F = 512, 1024, 512, 128, 512
FLOPS = 2 * E * F * G

F32 = mybir.dt.float32
BF16 = mybir.dt.bfloat16
I32 = mybir.dt.int32
U32 = mybir.dt.uint32
U16 = mybir.dt.uint16
U8 = mybir.dt.uint8
FP8X4 = mybir.dt.float8_e4m3fn_x4
MULT = mybir.AluOpType.mult
ADD = mybir.AluOpType.add
COPY = mybir.ActivationFunctionType.Copy

P = 128
PACK = 4
CORNERS = 4
POINTS = 4
ROW_PITCH = 8
PRODUCTS = 4
WO_ASIDE = 64


def tile_attend_deformable_pl_kernel(tc, vals, ca, cb, cc, cd, aw, wo, offs, offs2, offs3, offs4, out_0, out_1, out_2):
    nc = tc.nc
    lists_hbm = (offs, offs2, offs3, offs4)

    with ExitStack() as ctx:
        keep = ctx.enter_context(tc.tile_pool(name="keep", bufs=1))
        psum = ctx.enter_context(tc.psum_pool(name="psum", bufs=1))

        planes = [keep.tile([P, T], F32, name="plane", tag="plane%d" % t) for t in range(PACK)]
        lists = [keep.tile([P, J // 16], U16, name="list%d" % c) for c in range(CORNERS)]
        given = keep.tile([P, CORNERS + 1, ROW_PITCH], F32)
        wo_parts = (slice(0, WO_ASIDE), slice(WO_ASIDE, P))
        wo_raw = [keep.tile([P, PACK, PACK * (m.stop - m.start)], F32, name="wo_raw%d" % m.start) for m in wo_parts]
        vals_planes = vals.rearrange("(p t) c -> p t c", t=PACK)

        def bank(i, shape, name):
            return psum.tile(shape, F32, name=name, tag="bank%d" % i)

        def load_plane(t):
            nc.sync.dma_start(out=planes[t][:], in_=vals_planes[:, t, :])

        def load_row(r, queue=nc.sync):
            row = (aw, ca, cb, cc, cd)[r]
            queue.dma_start(out=given[:, r, 0:POINTS], in_=row.rearrange("o (g u) -> (o g) u", u=POINTS))

        def load_list(c):
            nc.sync.dma_start(lists[c][:], lists_hbm[c])

        load_row(0, nc.scalar)
        load_row(1)
        load_plane(0)
        load_list(2)
        load_list(0)
        for r in (2, 3, 4):
            load_row(r)
        load_plane(1)
        load_list(3)
        load_list(1)
        load_plane(2)
        load_plane(3)
        for tile, m in zip(wo_raw, wo_parts):
            f = slice(PACK * m.start, PACK * m.stop)
            nc.sync.dma_start(out=tile[:], in_=wo.rearrange("(p t) f -> p t f", t=PACK)[:, :, f])

        ident = keep.tile([P, P], F32)
        make_identity(nc, ident[:])

        weight = []
        for c in range(CORNERS):
            weight.append(keep.tile([P, POINTS], F32, name="weight", tag="picked%d" % c, align_bytes=64))
            nc.vector.tensor_tensor(weight[c][:], given[:, 1 + c, 0:POINTS], given[:, 0, 0:POINTS], MULT)

        halves = [slice(h * G // 2, (h + 1) * G // 2) for h in range(2)]
        direct = [keep.tile([P, 2, G // 2], F32, name="direct", tag="direct%d" % h, align_bytes=64) for h in range(2)]
        nc.vector.memset(direct[0][:, 0, :], 0.0)
        nc.scalar.activation(direct[1][:, 0, :], direct[0][:, 0, :], COPY)

        spread_psum = {}
        spread_dealt = {}
        for c in range(CORNERS):
            spread_bank = bank(c, [P, POINTS, G], "spread_bank")
            for u in range(POINTS):
                nc.tensor.transpose(spread_bank[:, u, :], weight[c][:, u : u + 1].to_broadcast([P, P]), ident[:])
            spread_psum[c] = spread_bank[:].rearrange("p u g -> p g u")
            spread_dealt[c] = spread_bank[:].rearrange("p u (b i) -> p b u i", i=2)
        spread = [keep.tile([P, J], F32, name="spread%d" % c) for c in range(3)]

        def by_point(ap):
            return ap.rearrange("p (g u) -> p g u", u=POINTS)

        sums = {}
        b_bf = [keep.tile([P, G // 2, PACK], BF16, name="b_bf", tag="b_bf%d" % h, align_bytes=64) for h in range(2)]
        added = {}
        done = {t: 0 for t in range(PACK)}
        picked = {}

        products = []

        def next_product():
            products.append(keep.tile([P, J], F32, name="product", tag="product%d" % (len(products) % PRODUCTS), align_bytes=64))
            return products[-1]

        def turn(t, blocks):
            terms = CORNERS - 1 if t == PACK - 1 else CORNERS
            if t not in added:
                added[t] = bank((1, 5, 6, 7)[t], [P, P], "added")
            for u in range(POINTS):
                nc.tensor.matmul(
                    added[t][:], blocks[u], ident[:], is_transpose=True,
                    start=(done[t], u) == (0, 0), stop=(done[t], u) == (terms - 1, POINTS - 1),
                )
            done[t] = done[t] + 1

        def close(t):
            nc.scalar.copy(out=added_sb[:, t, :], in_=added[t][:])
            if t % 2 == 0:
                sums[t // 2] = bank((4, 0)[t // 2], [P, 2, G], "sums")
            nc.tensor.transpose(sums[t // 2][:, t % 2, :], added_sb[:, t, :], ident[:])

        def pick(t, c, tag):
            picked[t, c] = keep.tile([P, J], F32, name="picked", tag=tag, align_bytes=64)
            nc.scalar.activation(picked[t, c][:], planes[t][:].indirect(lists[c][:]), COPY)

        def weigh(t, c):
            product = next_product()
            nc.vector.tensor_tensor(
                product[:].rearrange("p (u b i) -> p b u i", u=POINTS, i=2),
                picked[t, c][:].rearrange("p (b i u) -> p b u i", u=POINTS, i=2),
                spread_dealt[c],
                MULT,
            )
            turn(t, [product[:, u * G : (u + 1) * G] for u in range(POINTS)])

        def pick_aside(t, c):
            picked[t, c] = keep.tile([P, J], F32, name="aside", tag="aside%d" % t, align_bytes=64)
            nc.scalar.activation(picked[t, c][:], planes[t][:].indirect(lists[c][:]), COPY)

        def weigh_aside(t, c, tag):
            product = keep.tile([P, J], F32, name="product", tag=tag)
            nc.gpsimd.tensor_tensor(product[:], picked[t, c][:], spread[c][:], MULT)
            turn(t, [product[:, u:J:POINTS] for u in range(POINTS)])

        def gather_fused(t, c, parts):
            product = next_product()
            for h in range(parts):
                j = slice(h * J // parts, (h + 1) * J // parts)
                offsets = lists[c][:, j.start // 16 : j.stop // 16]
                nc.vector.tensor_tensor(product[:, j], planes[t][:].indirect(offsets), spread[c][:, j], MULT)
            return product

        def fused(t, c, parts=1):
            product = gather_fused(t, c, parts)
            turn(t, [product[:, u:J:POINTS] for u in range(POINTS)])

        for g in halves:
            nc.vector.tensor_copy(out=by_point(spread[0][:])[:, g, :], in_=spread_psum[0][:, g, :])
        pick_aside(0, 2)
        nc.scalar.copy(out=by_point(spread[1][:]), in_=spread_psum[1])
        fused(0, 0, parts=2)
        pick(0, 3, "picked1")
        nc.scalar.copy(out=by_point(spread[2][:]), in_=spread_psum[2])
        fused(1, 0)
        pick(1, 2, "picked2")
        fused(0, 1)
        fused(2, 0)
        pick(1, 3, "picked3")
        weigh(0, 3)
        weigh(1, 2)
        weigh_aside(0, 2, "plane0")
        pick_aside(2, 2)
        fused(1, 1)
        pick(2, 3, "picked1")
        fused(2, 1)
        pick(3, 2, "picked2")
        weigh(1, 3)
        weigh(2, 3)
        weigh_aside(2, 2, "plane1")
        pick(3, 3, "picked3")
        fused(3, 0)
        weigh(3, 2)
        weigh(3, 3)

        wo_bf = keep.tile([P, PACK, P, PACK], BF16, tag="picked1", align_bytes=64)
        wo_into = [wo_bf[:].rearrange("p t m k -> p m t k")[:, m, :, :] for m in wo_parts]
        wo_from = [wo_raw[h][:].rearrange("p k (m t) -> p m t k", t=PACK) for h in range(2)]
        nc.gpsimd.tensor_scalar(wo_into[0], wo_from[0], 1.0, 0.0, MULT, ADD)
        added_sb = keep.tile([P, PACK, P], F32, tag="aside2", align_bytes=64)
        for t in range(PACK - 1):
            close(t)
        for h, g in enumerate(halves):
            nc.scalar.copy(out=b_bf[h][:, :, 0:2], in_=sums[0][:].rearrange("p t g -> p g t")[:, g, :])

        last = gather_fused(PACK - 1, 1, 2)
        close(PACK - 1)
        nc.scalar.copy(out=wo_into[1], in_=wo_from[1])

        wo_scales = keep.tile([P, F], U8, align_bytes=64)

        def quantize_wo(t):
            nc.vector.quantize_mx(
                out=wo_codes[t].bitcast(FP8X4),
                scales=wo_scales[:, t * P : (t + 1) * P],
                in_=wo_bf[:, t, :, :].rearrange("p m k -> p (m k)"),
            )

        for h, g in enumerate(halves):
            nc.vector.tensor_reduce(direct[h][:, 1, :], by_point(last[:])[:, g, :], mybir.AxisListType.X, ADD)
        for h, g in enumerate(halves):
            nc.vector.tensor_tensor(
                b_bf[h][:, :, 2:4], sums[1][:].rearrange("p t g -> p g t")[:, g, :],
                direct[h][:].rearrange("p t g -> p g t"), ADD,
            )
        b_codes = keep.tile([P, G], U32, align_bytes=64)
        b_scales = keep.tile([P, G], U8, align_bytes=64)
        wo_first = keep.tile([P, P], U32, tag="direct0", align_bytes=64)
        wo_codes = [wo_first[:]]
        for h, g in enumerate(halves):
            if h == 1:
                quantize_wo(0)
            nc.vector.quantize_mx(
                out=b_codes[:, g].bitcast(FP8X4), scales=b_scales[:, g], in_=b_bf[h][:].rearrange("p g t -> p (g t)")
            )
        wo_rest = keep.tile([P, F - P], U32, tag="b_bf0", align_bytes=64)
        for t in range(1, PACK):
            wo_codes.append(wo_rest[:, (t - 1) * P : t * P])
            quantize_wo(t)

        y = keep.tile([P, PACK, G], F32)
        y_bf = keep.tile([P, G, PACK], BF16, align_bytes=64)
        out_planes = out_0.rearrange("(p t) g -> p t g", t=PACK)
        for h in range(2):
            two = slice(2 * h, 2 * h + 2)
            y_bank = bank(1 + h, [P, 2, G], "y_bank")
            for u in range(2):
                cols = slice((2 * h + u) * P, (2 * h + u + 1) * P)
                nc.tensor.matmul_mx(
                    out=y_bank[:, u, :],
                    lhsT=wo_codes[2 * h + u].bitcast(FP8X4),
                    lhsT_scale=wo_scales[:, cols],
                    rhs=b_codes[:].bitcast(FP8X4),
                    rhs_scale=b_scales[:],
                    start=True,
                    stop=True,
                )
            copy = nc.vector.tensor_copy if h == 0 else nc.scalar.copy
            copy(out=y_bf[:, :, two], in_=y_bank[:].rearrange("p t g -> p g t"))
            copy(out=y[:, two, :], in_=y_bank[:])
            queue = nc.sync if h == 0 else nc.scalar
            queue.dma_start(out=out_planes[:, two, :], in_=y[:, two, :])

        y_codes = keep.tile([P, G], U32, align_bytes=64)
        y_scales = keep.tile([P, G], U8, align_bytes=64)
        nc.vector.quantize_mx(out=y_codes[:].bitcast(FP8X4), scales=y_scales[:], in_=y_bf[:].rearrange("p g t -> p (g t)"))
        nc.sync.dma_start(out=out_1.rearrange("z p c r -> p (z c r)").bitcast(I32), in_=y_codes[:].bitcast(I32))
        for q in range(4):
            queue = nc.sync if q % 2 == 0 else nc.scalar
            queue.dma_start(
                out=out_2[0, 4 * q : 4 * q + 4, :].bitcast(I32), in_=y_scales[32 * q : 32 * q + 4, :].bitcast(I32)
            )
